import numpy as np, ml_dtypes
CORES = [48,51,52,55]
N = 4
import mx_ref
BF = ml_dtypes.bfloat16
def entries(a):
    return np.ascontiguousarray(a.T).reshape(-1)
def table(e):
    return np.ascontiguousarray(np.reshape(e, (-1, 16)).T).astype(np.int32)
def cols(t, e):
    v = np.concatenate([t.reshape(128, -1, 4), np.zeros((128, 1, 4), BF)], axis=1)
    return np.ascontiguousarray(v[:, e]).reshape(128, -1)
def cut(t, i, w=512):
    return t[:, w * i:w * i + w]
def pick(q, e):
    c = np.concatenate([q[0].reshape(128, -1, 4), np.zeros((128, 1, 4), np.uint8)], axis=1); s = np.concatenate([q[1], np.ones((16, 1), np.uint8)], axis=1)
    return (np.ascontiguousarray(c[:, e].reshape(128, -1)), np.ascontiguousarray(s[:, e]))
def join(*qs):
    return (np.concatenate([q[0] for q in qs], axis=1), np.concatenate([q[1] for q in qs], axis=1))
def put(q, e, v):
    c, s = q[0].reshape(128, -1, 4).copy(), q[1].copy(); c[:, e] = v[0].reshape(128, -1, 4); s[:, e] = v[1]
    return (c.reshape(128, -1), s)
def pk(c, s):
    return (np.ascontiguousarray(c), mx_ref.live(s))
def emit(q):
    return q[0], q[1]
def decode(q):
    o = []
    for b in range(4):
        e = np.zeros((128, 128, 4), np.float32); e[np.arange(128), np.arange(128), b] = 1
        o.append(mx_ref.matmul(mx_ref.quantize(e.reshape(128, 512).astype(BF)), q))
    return np.stack(o, axis=2).reshape(128, -1)
def f(rng, *shape):
    return mx_ref.flush((rng.standard_normal(shape, dtype=np.float32) * np.exp2(rng.integers(-2, 3, shape[:-1] + (1,)))).astype(BF))
def wide(rng, *shape, cols=0):
    v = rng.standard_normal(shape, dtype=np.float32) * np.exp2(rng.integers(-12, 13, shape)).astype(np.float32)
    if cols: v *= np.repeat(np.exp2(rng.integers(-cols, cols + 1, shape[:-2] + (1, shape[-1] // 4))) * (rng.random(shape[:-2] + (1, shape[-1] // 4)) > 0.0625), 4, axis=-1).astype(np.float32)
    return mx_ref.flush(v.astype(BF))
P, A, C, E, KP = 384, 32, 16, 8, 4
LC, M = 160, 3
def clean(v):
    v = np.array(v, np.float32)
    v[np.abs(v) < np.float32(2.0 ** -16)] = 0
    return v.astype(BF)
def lists(rng, full=False, own=False):
    out = []
    for r in range(N):
        pool = np.stack([P * q + rng.permutation(P)[:LC] for q in range(N)])
        must = np.zeros(0, int)
        if full: must = rng.permutation(pool[(r + 1 + rng.permutation(N - 1)[:M]) % N].reshape(-1))
        if own: must = P * r + rng.permutation(P)[:A * (C - 4)]
        rows = []
        for i in range(A):
            a = must[i::A]
            b = rng.permutation(np.setdiff1d(pool, a))[:C - a.size]
            rows.append(rng.permutation(np.concatenate([a, b])))
        out.append(table(np.concatenate(rows)))
    return {"cd": np.stack(out)}
def clusters(rng, n, low, high, noise):
    m = f(rng, 128, 4 * n).astype(np.float32).reshape(128, n, 4)
    h = rng.integers(0, n, (N, P))
    tb = np.stack([m[:, h[q]].reshape(128, -1) for q in range(N)]) + noise * f(rng, N, 128, 4 * P).astype(np.float32)
    a = low + (high - low) * rng.random((N, A, n))
    x = np.einsum("png,rin->rpig", m, a).reshape(N, 128, 4 * A) + noise * f(rng, N, 128, 4 * A).astype(np.float32)
    return {"tb": clean(tb), "x": clean(x), "w": f(rng, N, 128, 512)}
def setup_inputs(rng):
    return {**clusters(rng, 8, 0.2, 1.0, 0.5), **lists(rng)}
def setup_inputs_alike(rng):
    return {**clusters(rng, 3, 0.3, 0.7, 0.25), **lists(rng, full=True)}
def setup_inputs_one(rng):
    o, m, n = 0, min(A, LC // KP), P // KP
    kind = rng.permutation(P) % KP
    part = np.arange(128) // (128 // KP)
    tb = f(rng, N, 128, 4 * P).astype(np.float32).reshape(N, 128, P, 4) * np.float32(0.0625)
    tb[o] = (4 + 4 * rng.random((128, P, 4))) * (part[:, None] == kind[None, :])[:, :, None]
    order = np.stack([rng.permutation(np.flatnonzero(kind == k)) for k in range(KP)])
    out = []
    for r in range(N):
        size, at = (A, 0) if r == o else (m, A + m * (r - int(r > o)))
        big = P * o + order[:, (at + np.arange(A) % size) % n]
        pool = rng.permutation(np.concatenate([P * q + rng.permutation(P)[:LC] for q in range(N) if q != o]))
        rest = pool[:A * (C - KP)].reshape(A, C - KP)
        out.append(table(np.concatenate([rng.permutation(v) for v in np.concatenate([big.T, rest], axis=1)])))
    return {"tb": clean(tb.reshape(N, 128, 4 * P)), "x": clean(1 + rng.random((N, 128, 4 * A))), "w": f(rng, N, 128, 512), "cd": np.stack(out)}
def setup_inputs_ties(rng):
    m = clean(f(rng, 128, 12)).astype(np.float32).reshape(128, 3, 4)
    h = rng.integers(0, 3, (N, P))
    i = np.arange(A)
    k = np.where(i // 3 % 2 == 0, 1.0, 2.0)[None, :, None]
    tb = clean(np.stack([m[:, h[q]].reshape(128, -1) for q in range(N)])).reshape(N, 128, P, 4)
    x = clean(np.stack([(m[:, (i + r) % 3] * k).reshape(128, -1) for r in range(N)])).reshape(N, 128, A, 4)
    cd = lists(rng, own=True)["cd"]
    top = np.arange(128) < 64
    x[:, :, A - 2] = np.where(top, 4.0, 1.0).astype(BF)[None, :, None]
    x[:, :, A - 1] = np.where(top, -1.0, -4.0).astype(BF)[None, :, None]
    for r in range(N):
        g = rng.permutation(P)[:C + 1]
        g[:3] = np.sort(g[:3])
        tb[r][:, g[0]] = BF(-0.0)
        tb[r][:, g[1]] = BF(0.0)
        tb[r][:, g[2]] = np.array([1.0, -1.0, 1.0, -1.0]).astype(BF)[None, :]
        tb[r][:, g[3:]] = clean((1 + rng.random((128, C - 2, 4))) * np.where(top, -1.0, 1.0)[:, None, None])
        e = np.array(entries(cd[r])).reshape(A, C)
        e[A - 2] = P * r + rng.permutation(np.delete(g, 1))
        e[A - 1] = P * r + rng.permutation(np.delete(g, 0))
        cd[r] = table(e)
    return {"tb": tb.reshape(N, 128, 4 * P), "x": x.reshape(N, 128, 4 * A), "w": f(rng, N, 128, 512), "cd": cd}
def setup_inputs_shared(rng):
    place = np.stack([rng.permutation(P) for q in range(N)])
    tb = f(rng, N, 128, 4 * P).astype(np.float32).reshape(N, 128, P, 4) * np.float32(0.0625)
    part = np.arange(128) // (128 // KP)
    big = np.zeros((N, KP), int)
    for g in range(N):
        for k in range(KP):
            o = (g + k) % N
            tb[o, :, place[o, k]] = (4 + 4 * rng.random((128, 4))) * (part == k)[:, None]
            big[g, k] = P * o + place[o, k]
    out = []
    for r in range(N):
        pool = np.concatenate([P * q + rng.permutation(place[q, KP:])[:LC - KP] for q in range(N)])
        at = rng.integers(0, r + 1, A)
        at[0], at[A - 1] = 0, r
        out.append(table(np.concatenate([rng.permutation(np.concatenate([big[g], rng.permutation(pool)[:C - KP]])) for g in at])))
    return {"tb": clean(tb.reshape(N, 128, 4 * P)), "x": clean(1 + rng.random((N, 128, 4 * A))), "w": f(rng, N, 128, 512), "cd": np.stack(out)}
def setup_inputs_spread(rng):
    return {"tb": clean(wide(rng, N, 128, 4 * P, cols=6)), "x": clean(wide(rng, N, 128, 4 * A, cols=6)), "w": f(rng, N, 128, 512), **lists(rng)}
def check_inputs(d):
    b = []
    for k, low in (("tb", -16), ("x", -16), ("w", -30)):
        v = np.abs(d[k].astype(np.float32))
        if not (np.isfinite(v).all() and ((v == 0) | (v >= 2.0 ** low) & (v <= 2.0 ** 30)).all()): b.append("a value of " + k)
    for r in range(N):
        e = entries(d["cd"][r])
        if e.min() < 0 or e.max() >= N * P:
            b.append("cd: a number out of range")
            continue
        if any(len(set(v.tolist())) < C for v in e.reshape(A, C)): b.append("cd: a candidate twice at one point")
        n = np.bincount(np.unique(e) // P, minlength=N)
        n[r] = 0
        if n.max() > LC: b.append("cd: too many columns of one other rank")
    return b
def chosen(every, x, cd):
    kept = np.full((N, A, KP), -1)
    for r in range(N):
        e = entries(cd[r])
        t = cols(every, e)
        v = mx_ref.quantize(t)
        points = mx_ref.quantize(cols(x[r], np.concatenate([np.arange(A), np.full(128 - A, -1)])))
        s = mx_ref.matmul(points, v) + np.float32(0)
        g = np.concatenate([mx_ref.matmul(mx_ref.quantize(np.ascontiguousarray(cut(t, j))), v) for j in range(C * A // 128)]) + np.float32(0)
        for i in range(A):
            at = np.arange(C * i, C * i + C)
            best = at[np.lexsort((e[at], -s[i, at]))[:E]]
            mine = []
            for c in best:
                if len(mine) < KP and all(s[i, c] > g[c, k] for k in mine): mine.append(c)
            kept[r, i, :len(mine)] = e[mine]
    return kept
def reference(tb, x, w, cd):
    every = np.concatenate([tb[q] for q in range(N)], axis=1)
    kept = chosen(every, x, cd)
    y = np.zeros((N, 128, KP * A), np.float32)
    oc, osc = np.zeros((N, 128, 4 * P), np.uint8), np.zeros((N, 16, P), np.uint8)
    for r in range(N):
        y[r] = mx_ref.matmul(mx_ref.quantize(w[r]), mx_ref.quantize(cols(every, kept[r].reshape(-1))))
    dx = [decode(mx_ref.quantize(x[r])).reshape(128, A, 4) for r in range(N)]
    half = np.float32(0.5)
    for q in range(N):
        v = mx_ref.quantize(tb[q])
        m = decode(v).reshape(128, P, 4)
        named = np.zeros(P, bool)
        for r in range(N):
            for i in range(A):
                for c in kept[r, i]:
                    j = c - P * q
                    if 0 <= j < P and not named[j]:
                        m[:, j] = m[:, j] * half + dx[r][:, i] * half
                        named[j] = True
        at = np.flatnonzero(named)
        new = mx_ref.quantize(np.ascontiguousarray(m.reshape(128, -1).astype(BF)))
        oc[q], osc[q] = emit(put(v, at, pick(new, at)))
    return {"y": y, "kp": np.ascontiguousarray(kept.transpose(0, 2, 1)).astype(np.float32), "oc": oc, "osc": osc}

@@ -1,0 +1,529 @@
+from concourse.bass import DstId, RemoteDMATransfer
+from concourse.mybir import dt, AluOpType, AxisListType, ActivationFunctionType
+
+N, P, A, C, LC = 4, 384, 32, 16, 160
+UB = 32
+UR = UB + P
+UW = UR + 3 * LC
+MO = 3 * P
+MW = MO + 4 * P
+DB = P
+DUMP = N * P + 4
+IW = DUMP + 20
+CUT = ((0, 160), (160, 384))
+
+F32, BF, I32, U16, U8, F8 = "float32", "bfloat16", "int32", "uint16", "uint8", "float8_e4m3fn_x4"
+SCRATCH = {}
+for _d, _names in (
+    (BF, "tbt:1536 xt:512 wt:512 et:2048 nt:1536"),
+    (F8, "vq:384 xq:128 wq:128 eq:512 xa:160 uc:896 pk:480 ex:512 kq:128 qp:384 mg:768 oq:384"),
+    (U8, "vqs:384 xqs:128 wqs:128 eqs:512 xas:160 ucs:896 pks:480 exs:512 kqs:128 qps:384 mgs:768 oqs:384"),
+    (I32, "kci:64"), (U16, "bl:4 bo:8 br:4 pl:2 rl:24 hv:4"), (BF, "ones:16 eye:128 ptv:64"),
+    (F32, "kcf:512 idt:1560 ids:1560 cv:192 zz:128"),
+    (I32, "cdh:16 cdi:32"), (U16, "off:32 wl:12 lst:10 lnd:30 ls:30"), (BF, "mk0:2688 mk1:2688 tm:768 m1:24"),
+    (F32, "req:192 x0:32 xt0:32 wn:1152 wnt:160 lr:32 ld:64 ldt:64"),
+    (F32, "cdp:32 zp:12 zrep:384 zf:416 gx:128 zr:512 zt:512 z2:128 sf:32 sc:16 nc:16 n1:24 nr:64 tie:64"), (U16, "og:32 sw:32 nl:4 kl:2"),
+    (F32, "cs:128 cg:512 ob:128 obt:128 row:64 gg:64 dw:64 w2:64 bb:64 rks:68 l2a:8 l2b:8 t1:128 t1t:128 t2:640 t2t:256 cu:64 tmp:64 alg:64"), (U16, "l1:4 l2:8"),
+    (F32, "pr:160 kpt:32 yr:32 yd:64 ydt:64 yt:128"), (U16, "kd:2 ksl:8 kla:6"),
+    (BF, "wk:1568 wo:1568 tk:384 tko:384"), (F32, "wm:64 sl0:24 sl1:24"), (U16, "ln:24 sl:24"),
+):
+    for _n in _names.split():
+        SCRATCH[_n.split(":")[0]] = ("sbuf", [128, int(_n.split(":")[1])], _d)
+PART = {}
+for _d, _names in (
+    ("kcf", "pf:8 cq:8 ca:12 t32:32 tri:32 dc0:12 dc:12 dc1:12 plc:12 c4:4 bo0:8 br0:4 br1:4 hv0:4 c2:8 cst0:4 cst:4 jc0:24 jc:24 mk4:4 rst0:64 rst:64 pm0:16 pm:16 pt0:64"),
+    ("kci", "ip:2 ib:4 it:8 ir:24"),
+    ("req", "mm:12 tot:1 base:1 sn:12 g1:12 g2:12 g3:12"),
+    ("pr", "nn:8 sl8:8 mk8:8 ms8:8 ms9:8 cn:8 ck:8 z8:8 y8:8 nlv:1 nls:1 slv:1 kt:1 kw:1 kv:1 yv:1 kp2:16 kp3:8 kpo:8 own:16 same:16 dup:1"),
+    ("wm", "wa:12 wb:12 wc:12 wown:12"),
+):
+    _c = 0
+    for _n in _names.split():
+        PART[_n.split(":")[0]] = (_d, _c, int(_n.split(":")[1]))
+        _c += PART[_n.split(":")[0]][2]
+    assert _c <= SCRATCH[_d][1][1]
+BANKS = ["pb%d" % _b for _b in range(8)]
+for _n in BANKS:
+    SCRATCH[_n] = ("psum", [128, 512], F32)
+SEMAPHORES = ["ev", "ec", "et_", "ep", "dch", "dcd", "dx", "dtb", "dw", "dxa", "dmg", "dz", "dk", "dy", "do0", "do1", "dp0", "dp1",
+              "arx", "arl", "arc", "ark", "loc"]
+
+
+def rank_program(g, core, T, topo):
+    r = T.rank_of(core)
+    if r is None:
+        return
+    O, AF, X = AluOpType, ActivationFunctionType, AxisListType.X
+    eng = {"v": g.vector, "s": g.scalar, "t": g.tensor, "p": g, "y": g.sync}
+    semof = {"v": "ev", "s": "ec", "t": "et_", "p": "ep"}
+    count = {}
+    known = {k: {} for k in eng}
+    log = {}
+
+    def R(name, c0=0, c1=None, p0=0, p1=128, st=1):
+        name, base, n = PART.get(name, (name, 0, SCRATCH[name][1][1] if name in SCRATCH else 0))
+        c0, c1 = base + c0, base + (n if c1 is None else c1)
+        ap = T[name][p0:p1, c0:c1] if st == 1 else T[name][p0:p1, c0:c1:st]
+        return {"n": name, "c0": c0, "c1": c1, "p0": p0, "p1": p1, "st": st, "ap": ap}
+
+    def meet(a, b):
+        if a["p1"] <= b["p0"] or b["p1"] <= a["p0"] or a["c1"] <= b["c0"] or b["c1"] <= a["c0"]:
+            return False
+        return not (a["st"] == b["st"] and a["st"] > 1 and (a["c0"] - b["c0"]) % a["st"])
+
+    def need(q, outs, ins, skip=None):
+        todo = {}
+        for kind, regs in (("w", outs), ("r", ins)):
+            for x in regs:
+                bank = x["n"] in BANKS
+                for y, k, tok in log.get(x["n"], []):
+                    if (skip is not None and tok[3] == skip) or known[q].get(tok[0], 0) >= tok[1]:
+                        continue
+                    if bank:
+                        hit = tok[0] != semof.get(q) or (q != "t" and meet(x, y) and "w" in (kind, k))
+                    else:
+                        hit = "w" in (kind, k) and meet(x, y)
+                    if hit and (tok[0] not in todo or todo[tok[0]][1] < tok[1]):
+                        todo[tok[0]] = tok
+        for s in sorted(todo):
+            tok = todo[s]
+            if known[q].get(s, 0) >= tok[1]:
+                continue
+            eng[q].wait_ge(T.sem[s], tok[1])
+            for a, b in list(tok[2].items()) + [(s, tok[1])]:
+                known[q][a] = max(known[q].get(a, 0), b)
+
+    def note(q, outs, ins, sem, val, tag=None):
+        tok = (sem, val, dict(known[q]) if q else {}, tag)
+        for k, regs in (("w", outs), ("r", ins)):
+            for x in regs:
+                log.setdefault(x["n"], []).append((x, k, tok))
+
+    def op(q, call, outs, ins):
+        need(q, outs, ins)
+        s = semof[q]
+        count[s] = count.get(s, 0) + 1
+        call().then_inc(T.sem[s], 1)
+        note(q, outs, ins, s, count[s])
+
+    def u8(x):
+        return x["ap"].bitcast(dt.uint8) if SCRATCH[x["n"]][2] == F8 else x["ap"]
+
+    def dma(q, o, i, sem, total):
+        outs, ins = [x for x in (o,) if isinstance(x, dict)], [x for x in (i,) if isinstance(x, dict)]
+        need(q, outs, ins, skip=sem)
+        eng[q].dma_start(u8(o) if outs else o, u8(i) if ins else i).then_inc(T.sem[sem], 16)
+        count[sem] = count.get(sem, 0) + 16
+        note(q, outs, ins, sem, 16 * total, tag=sem)
+
+    def memset(a, c):
+        op("v", lambda: g.vector.memset(a["ap"], c), [a], [])
+
+    def copy(o, i, q="v"):
+        if q == "v":
+            op("v", lambda: g.vector.tensor_copy(o["ap"], i["ap"]), [o], [i])
+        else:
+            op("s", lambda: g.scalar.activation(o["ap"], i["ap"], AF.Copy), [o], [i])
+
+    def tt(o, a, b, f):
+        op("v", lambda: g.vector.tensor_tensor(o["ap"], a["ap"], b["ap"], f), [o], [a, b])
+
+    def ttg(o, win, off, b, f):
+        op("v", lambda: g.vector.tensor_tensor(o["ap"], win["ap"].indirect(off["ap"]), b["ap"], f), [o], [win, off, b])
+
+    def ts(o, a, s1, s2, f1, f2=None):
+        ins = [a] + [s for s in (s1, s2) if isinstance(s, dict)]
+        v1 = s1["ap"] if isinstance(s1, dict) else s1
+        v2 = s2["ap"] if isinstance(s2, dict) else s2
+        if f2 is None:
+            op("v", lambda: g.vector.tensor_scalar(o["ap"], a["ap"], v1, None, f1), [o], ins)
+        else:
+            op("v", lambda: g.vector.tensor_scalar(o["ap"], a["ap"], v1, v2, f1, f2), [o], ins)
+
+    def red(o, a, f, size=False):
+        kw = {"apply_absolute_value": True} if size else {}
+        op("v", lambda: g.vector.tensor_reduce(o["ap"], a["ap"], X, f, **kw), [o], [a])
+
+    def scan(o, a, b, f1, f2):
+        op("v", lambda: g.vector.tensor_tensor_scan(o["ap"], a["ap"], b["ap"], 0.0, f1, f2), [o], [a, b])
+
+    def lin(o, a, scale=1.0, bias=0.0, f=AF.Identity):
+        ins = [a] + [s for s in (scale, bias) if isinstance(s, dict)]
+        kw = {"scale": scale["ap"] if isinstance(scale, dict) else scale, "bias": bias["ap"] if isinstance(bias, dict) else bias}
+        op("s", lambda: g.scalar.activation(o["ap"], a["ap"], f, **kw), [o], ins)
+
+    def turn(o, a):
+        op("v", lambda: g.vector.transpose(o["ap"], a["ap"]), [o], [a])
+
+    def gather(o, win, off, q="v"):
+        if q == "v":
+            op("v", lambda: g.vector.tensor_copy(o["ap"], win["ap"].indirect(off["ap"])), [o], [win, off])
+        else:
+            op("s", lambda: g.scalar.activation(o["ap"], win["ap"].indirect(off["ap"]), AF.Copy), [o], [win, off])
+
+    def scatter(win, off, i):
+        op("v", lambda: g.vector.tensor_copy(win["ap"].indirect(off["ap"]), i["ap"]), [win], [off, i])
+
+    def pick(cn, o0, o1, wn, w1, off):
+        o, w = R(cn, o0, o1), R(wn, 0, w1)
+        op("v", lambda: g.vector.tensor_copy(o["ap"].bitcast(dt.uint32), w["ap"].bitcast(dt.uint32).indirect(off["ap"])), [o], [w, off])
+        gather(R(cn + "s", o0, o1), R(wn + "s", 0, w1), off, "s")
+
+    def quant(cn, c0, c1, tile):
+        o, s = R(cn, c0, c1), R(cn + "s", c0, c1)
+        op("v", lambda: g.vector.quantize_mx(o["ap"], s["ap"], tile["ap"]), [o, s], [tile])
+
+    def mm(bank, n, a, a0, b, b0, b1, start=True, stop=True):
+        o, l, ls, m, ms = R(bank, 0, n), R(a, a0, a0 + 128), R(a + "s", a0, a0 + 128), R(b, b0, b1), R(b + "s", b0, b1)
+        op("t", lambda: g.tensor.matmul_mx(o["ap"], l["ap"], ls["ap"], m["ap"], ms["ap"], start, stop), [o], [l, ls, m, ms])
+
+    def iota(name, pattern, base, cm, c0=0, c1=None):
+        o = R(name, c0, c1)
+        kw = {"allow_small_or_imprecise_dtypes": True} if SCRATCH[o["n"]][2] in (F32, BF) else {}
+        op("p", lambda: g.iota(o["ap"], pattern, base, cm, **kw), [o], [])
+
+    others = [q for q in range(N) if q != r]
+    here = {q: (r if r < q else r - 1) for q in others}
+
+    def send(pieces, sem, turned=0):
+        need("p", [], [s for _q, s, _d in pieces])
+        parts = 1 if len(pieces) == 1 else 4
+        tr = []
+        for k, (q, s, d) in enumerate(pieces):
+            e = topo.engines(core, T.cores[q])
+            m = len(e) // parts
+            k4 = (k + turned) % parts
+            rid, pid, _s = topo.addr(T.cores[q])
+            tr.append(RemoteDMATransfer(dst_ids=[DstId(rid=rid, pnc=pid)], dma_engine_mask=sum(1 << n for n in e[k4 * m:k4 * m + m]),
+                                        remote_sem=T.sem[sem], src=u8(s), dst=u8(d)))
+            count["loc"] = count.get("loc", 0) + m
+            count[sem] = count.get(sem, 0) + m
+        g.remote_dma_fused(tr, local_sem=T.sem.loc)
+
+    for k in range(8):
+        dma("ys"[k % 2], R("cdh", 0, 16, 16 * k, 16 * k + 16), T.cd[:, 16 * (k % 2):16 * (k % 2) + 16], "dch", 8)
+    dma("y", R("xt", 0, 128), T.x[:, :], "dx", 1)
+    dma("y", R("tbt"), T.tb[:, :], "dtb", 1)
+    for k in range(8):
+        dma("y", R("cdi", 0, 32, 16 * k, 16 * k + 16), T.cd[:, :], "dcd", 8)
+    dma("y", R("wt"), T.w[:, :], "dw", 1)
+
+    IQ = IW // 4
+    iota("ip", [[1, 1]], 0, 1, 0, 1)
+    iota("t32", [[1, 32]], 0, 0)
+    iota("dc0", [[1, 12]], DB, 0)
+    iota("cv", [[32, 12], [1, 16]], 0, 0)
+    iota("idt", [[1, IQ]], 0, 0, 0, IQ)
+    iota("hv0", [[16, 2], [0, 2]], 0, 0)
+    iota("plc", [[32, 12]], UB - 32 * r, 1)
+    iota("ir", [[1, 12], [0, 2]], 0, 0)
+    iota("c4", [[1, 4]], 0, 0)
+    memset(R("mk0", MO, MO + P), 0.0)
+    p = R("ip", 0, 1)
+    for k, (sh, msk) in enumerate(((0, 15), (4, 1), (0, 7), (4, 7), (0, 3), (5, 3), (0, 31), (1, 3))):
+        ts(R("it", k, k + 1), p, sh, msk, O.logical_shift_right, O.bitwise_and)
+    memset(R("mk1", MO, MO + P), 0.0)
+    copy(R("pf", 0, 8), R("it", 0, 8))
+    lcol, hcol, _ecol, gcol, p3, acol, pcol, bcol = [R("pf", k, k + 1) for k in range(8)]
+    memset(R("ones"), 1.0)
+    ts(R("cq", 0, 1), acol, float(-P), float(MO), O.mult, O.add)
+    memset(R("xt", 128, 512), 0.0)
+    ts(R("tri"), R("t32"), pcol, None, O.is_gt)
+    lin(R("ca", 0, 1), hcol, 16.0)
+    lin(R("ca", 6, 7), pcol, 12.0)
+    lin(R("dc"), R("dc0"), 1.0, R("ca", 6, 7))
+    lin(R("cv"), R("cv"), 1.0, R("ca", 0, 1))
+    lin(R("dc1"), R("dc"), 1.0, 1.0)
+    memset(R("wn", 0, LC), 0.0)
+    ts(R("off", 0, 32, st=2), R("cdh"), R("cq", 0, 1), None, O.add)
+
+    for i in range(A // 2):
+        scatter(R("mk%d" % (i % 2)), R("off", 2 * i, 2 * i + 1), R("ones"))
+    for k in range(2):
+        turn(R("tm", P * k, P * k + P), R("mk%d" % k, MO, MO + P))
+
+    quant("xq", 0, 128, R("xt"))
+    for s, k in (("", 0), ("s", 3)):
+        send([(q, R("xq" + s, 0, 32), R("xa" + s, 32 * r, 32 * r + 32)) for q in others], "arx", k)
+    for s in ("", "s"):
+        dma("y", R("uc" + s, 0, 32), R("xq" + s, 32, 64), "dz", 2)
+        dma("y", R("xa" + s, 32 * r, 32 * r + 32), R("xq" + s, 0, 32), "dxa", 4)
+        dma("y", R("xa" + s, 128, 160), R("xq" + s, 32, 64), "dxa", 4)
+
+    lin(R("cq", 1, 2), acol, float(-P), 16.0)
+    lin(R("ca", 1, 2), gcol, 4.0)
+    lin(R("ca", 4, 5), lcol, 1.0, float(DUMP))
+    lin(R("ca", 2, 3), hcol, -1.0, 1.0)
+    lin(R("ca", 3, 4), hcol, 32.0)
+    lin(R("ca", 5, 6), hcol, -32.0, 32.0)
+    lin(R("ca", 8, 9), p3, -1.0, -1.0)
+    for k in range(8):
+        lin(R("et", 256 * k, 256 * k + 256), R("idt", 0, 256), 0.0)
+    eye, nil = R("eye"), R("et", 0, 128)
+    op("p", lambda: g.affine_select(eye["ap"], nil["ap"], [[1, 128]], O.not_equal, 0.5, 0, -1), [eye], [nil])
+    for k in range(1, 4):
+        lin(R("idt", IQ * k, IQ * k + IQ), R("idt", 0, IQ), 1.0, float(IQ * k))
+    for j in range(4):
+        copy(R("cdp", 8 * j, 8 * j + 8), R("cdi", j, 32, st=4), "s")
+    for b in range(4):
+        copy(R("et", 513 * b, 512 * b + 512, st=4), eye, "s")
+    tt(R("m1"), R("tm", 0, 2 * P, st=32), R("tm", 16, 2 * P, st=32), O.max)
+    ts(R("hv"), R("hv0"), lcol, None, O.add)
+    tt(R("mm"), R("m1", 0, 12), R("m1", 12, 24), O.max)
+    memset(R("zf", 0, 16), 0.0)
+    red(R("tot"), R("mm"), O.add)
+    scan(R("sn"), R("mm"), R("mm"), O.add, O.max)
+    ts(R("x0"), R("tri"), R("tot"), None, O.mult)
+    tt(R("g1"), R("sn"), R("dc1"), O.subtract)
+    turn(R("xt0"), R("x0"))
+    tt(R("g2"), R("g1"), R("mm"), O.mult)
+    red(R("base"), R("xt0"), O.add)
+    tt(R("g3"), R("g2"), R("dc"), O.add)
+    ts(R("cq", 3, 4), acol, float(r), float(-LC), O.is_gt, O.mult)
+    ts(R("wl"), R("g3"), R("base"), None, O.add)
+    ts(R("cq", 2, 3), acol, float(LC), R("cq", 3, 4), O.mult, O.add)
+    scatter(R("wn"), R("wl"), R("cv"))
+    ts(R("zp"), R("sn"), R("base"), R("cq", 2, 3), O.add, O.add)
+    turn(R("wnt"), R("wn", 0, LC))
+    memset(R("zz"), 0.0)
+    tt(R("zz", 0, 5), R("wnt", 0, LC, st=32), R("wnt", 16, LC, st=32), O.add)
+    ts(R("zp"), R("zp"), float(UR - 1), None, O.add)
+    turn(R("lr"), R("zz", 0, 32))
+    copy(R("zp", 0, 12, 32 * r, 32 * r + 32), R("plc", 0, 12, 32 * r, 32 * r + 32))
+    gather(R("ld"), R("lr"), R("hv"))
+    copy(R("rl"), R("ir"))
+    turn(R("ldt"), R("ld"))
+    for k in range(2):
+        copy(R("lst", k, 10, st=2), R("ldt", 32 * k, 32 * k + 5), "vs"[k])
+    send([(q, R("lst"), R("lnd", 10 * here[q], 10 * here[q] + 10)) for q in others], "arl")
+
+    gather(R("zrep"), R("zp"), R("rl"), "s")
+    iota("br0", [[32, 4]], 0, 0)
+    iota("rst0", [[0, 4], [1, 16]], 0, 0)
+    iota("pm0", [[4, 4], [0, 4]], 3, 0)
+    iota("ib", [[128, 4]], 0, 1)
+    iota("bo0", [[33, 4], [0, 2]], 0, 0)
+    iota("cst0", [[32, 4]], 0, 0)
+    iota("pt0", [[A, N], [1, 4], [0, 4]], 0, 0)
+    iota("jc0", [[16, 24]], 0, 0)
+    quant("vq", 0, P, R("tbt"))
+    memset(R("zf", 400, 416), 0.0)
+    quant("uc", UB, UR, R("tbt"))
+    ts(R("gx", 0, 32), R("cdp"), R("cq", 1, 2), 15.0, O.add, O.max)
+    turn(R("zf", 16, 400), R("zrep"))
+    tt(R("gx", 32, 64, st=2), R("gx", 1, 32, st=2), R("gx", 0, 32, st=2), O.subtract)
+    tt(R("gx", 33, 64, st=2), R("gx", 0, 32, st=2), R("gx", 1, 32, st=2), O.subtract)
+    ts(R("pl", 0, 1), bcol, 8.0, gcol, O.mult, O.add)
+    ts(R("gx", 64, 96), R("gx", 32, 64), hcol, None, O.mult)
+    gather(R("nc"), R("cdp"), R("pl", 0, 1))
+    tt(R("gx", 96, 128), R("gx", 64, 96), R("gx", 0, 32), O.add)
+    ts(R("og"), R("gx", 96, 128), 400.0, None, O.min)
+
+    note(None, [R("lnd", 0, 30)], [], "arl", count["arl"])
+    for a in range(4):
+        copy(R("ls", 0, 30, 32 * a, 32 * a + 32), R("lnd", 0, 30, 32 * r, 32 * r + 32), "vs"[a % 2])
+    for k, q in enumerate(others):
+        pick("pk", LC * k, LC * k + LC, "vq", P, R("ls", 10 * k, 10 * k + 10))
+        send([(q, R("pk", LC * k, LC * k + LC), R("uc", UR + LC * here[q], UR + LC * here[q] + LC))], "arc")
+    send([(q, R("pks", LC * k, LC * k + LC), R("ucs", UR + LC * here[q], UR + LC * here[q] + LC)) for k, q in enumerate(others)], "arc", 3)
+
+    iota("t1", [[0, 128]], 0, 0)
+    iota("t2", [[0, 256]], 0, 0, 0, 256)
+    for n in ("wk", "wo"):
+        iota(n, [[0, P]], N * A, 0, P * r, P * r + P)
+    lin(R("br1"), R("br0"), 1.0, R("ca", 0, 1))
+    for j in range(4):
+        lin(R("gg", 16 * j, 16 * j + 16), R("t32", 0, 16), 0.0, R("nc", 2 * j, 2 * j + 1))
+    gather(R("zr"), R("zf"), R("og"), "s")
+    lin(R("cst"), R("cst0"), 1.0, R("ca", 0, 1))
+    lin(R("n1", 8, 16), R("nc", 0, 8), 1.0 / 8192)
+    lin(R("jc"), R("jc0"), 1.0, lcol)
+    lin(R("ptv"), R("pt0"), 1.0, R("ca", 1, 2))
+    lin(R("ca", 7, 8), hcol, 28.0, 4.0)
+    lin(R("ca", 9, 10), hcol, -28.0, 32.0)
+    lin(R("ca", 10, 11), hcol, 512.0)
+    lin(R("ca", 11, 12), hcol, -512.0, 528.0)
+    lin(R("cq", 4, 5), lcol, hcol, R("ca", 10, 11))
+    lin(R("cq", 5, 6), lcol, R("ca", 2, 3), R("ca", 11, 12))
+    lin(R("c2", 0, 8, st=2), R("c4"), R("ca", 7, 8), R("cq", 4, 5))
+    lin(R("c2", 1, 8, st=2), R("c4"), R("ca", 9, 10), R("cq", 5, 6))
+
+    copy(R("nl"), R("nc", 0, 8, st=2))
+    ts(R("br"), R("br1"), lcol, None, O.add)
+    ts(R("rst"), R("rst0"), 0.5, None, O.is_gt)
+    ts(R("pm"), R("pm0"), lcol, 4096.0, O.is_ge, O.mult)
+    memset(R("kd"), 0.0)
+    quant("wq", 0, 128, R("wt"))
+    quant("eq", 0, 512, R("et"))
+    ttg(R("nr"), R("idt"), R("nl"), R("gg"), O.is_lt)
+    turn(R("zt"), R("zr"))
+    ev, od = R("z2", 0, 32, 0, 32, 2), R("z2", 1, 32, 0, 32, 2)
+    ts(R("tie"), R("nr"), -2.0 ** -100, None, O.mult)
+    tt(R("z2", 96, 128, 0, 64), R("zt", 0, 512, 0, 64, 16), R("zt", 0, 512, 64, 128, 16), O.add)
+    tt(R("z2", 0, 32, 0, 32), R("z2", 96, 128, 0, 32), R("z2", 96, 128, 32, 64), O.add)
+    tt(R("z2", 32, 48, 0, 32), od, ev, O.subtract)
+    ts(R("mk4"), R("c4"), p3, None, O.is_equal)
+    ts(R("z2", 48, 64, 0, 32), R("z2", 32, 48, 0, 32), R("pf", 1, 2, 0, 32), None, O.mult)
+    memset(R("alg", 0, 1), 1.0)
+    tt(R("z2", 64, 96, 0, 32, 2), ev, R("z2", 48, 64, 0, 32), O.add)
+    tt(R("z2", 65, 96, 0, 32, 2), od, R("z2", 48, 64, 0, 32), O.subtract)
+    copy(R("bl"), R("ib"))
+    ts(R("bo"), R("bo0"), R("ca", 1, 2), None, O.add)
+    for a in range(4):
+        copy(R("sf", 0, 32, 32 * a, 32 * a + 32), R("z2", 64, 96, 0, 32), "vs"[a % 2])
+    copy(R("sw"), R("sf"))
+    gather(R("sc"), R("sf"), R("pl", 0, 1))
+    ts(R("n1", 16, 24), R("sc", 0, 8), 1.0 / 8192, None, O.mult)
+
+    note(None, [R(n, UR, UW) for n in ("uc", "ucs")], [], "arc", count["arc"])
+    for j in range(4):
+        pick("ex", 128 * j, 128 * j + 128, "uc", UW, R("sw", 8 * j, 8 * j + 8))
+    for j, w in ((0, 1), (0, 0), (1, 1), (1, 0), (2, 1), (3, 1), (2, 0), (3, 0)):
+        mm(BANKS[4 * w + j], 128, "ex", 128 * j, "xq" if w else "ex", 0 if w else 128 * j, 128 if w else 128 * j + 128)
+        if w:
+            copy(R("cs", 32 * j, 32 * j + 32), R(BANKS[4 + j], 0, 32), "ssvv"[j])
+        else:
+            copy(R("cg", 128 * j, 128 * j + 128), R(BANKS[j], 0, 128), "s")
+    lin(R("ids"), R("idt"), 1.0 / 8192)
+    gather(R("ob"), R("cs"), R("bo"))
+    own = R("ob", 0, 128, st=2)
+    need("y", [], [R("ob")])
+    for s in ("", "s"):
+        dma("y", R("mg" + s, 0, P), R("vq" + s), "dmg", 2)
+    turn(R("obt"), R("ob"))
+    gather(R("gg"), R("cg"), R("bl"))
+    gather(R("row"), R("obt"), R("br"))
+    tt(R("bb"), R("gg"), own, O.is_lt)
+    tt(R("dw"), R("row"), own, O.subtract)
+    tt(R("w2"), R("dw"), R("tie"), O.is_gt)
+    scan(R("rks", 0, 64), R("rst"), R("w2"), O.mult, O.add)
+    rank = R("rks", 15, 64, st=16)
+    tt(R("rks", 64, 68), rank, R("cst"), O.add)
+    ts(R("l2a", 0, 8, st=2), rank, R("ca", 5, 6), None, O.mult)
+    ts(R("l2a", 1, 8, st=2), rank, R("ca", 3, 4), None, O.mult)
+    copy(R("l1"), R("rks", 64, 68))
+    tt(R("l2b"), R("l2a"), R("c2"), O.add)
+    scatter(R("t1"), R("l1"), R("bb"))
+    copy(R("l2"), R("l2b"))
+    copy(R("t1", 15, 128, st=16), R("n1", 8, 16))
+    copy(R("t1", 14, 128, st=16), R("n1", 16, 24), "s")
+    turn(R("t1t"), R("t1"))
+    scatter(R("t2"), R("l2"), R("t1t"))
+    for k in range(1, 4):
+        copy(R("t2", k, 256, st=4), R("t2", 0, 256, st=4), "vvsv"[k])
+    turn(R("t2t"), R("t2", 0, 256))
+
+    def both(o, v, k):
+        tt(o, R("t2t", 32 * v + k, 256, st=32), R("t2t", 32 * v + 16 + k, 256, st=32), O.add)
+    both(R("alg", 9, 16), 1, 0)
+    both(R("cu", 8, 14), 2, 1)
+    ts(R("tmp", 10, 16), R("cu", 8, 14), R("alg", 9, 10), None, O.is_ge)
+    both(R("cu", 16, 21), 3, 2)
+    both(R("nn"), 0, 15)
+    for u in range(2, 8):
+        if u < 7:
+            ts(R("tmp", 9 * u + 1, 8 * u + 8), R("cu", 8 * u, 8 * u + 7 - u), R("alg", 9 * u - 8, 9 * u - 7), R("tmp", 9 * u - 8, 9 * u - 7), O.is_ge, O.is_ge)
+        tt(R("alg", 9 * u, 8 * u + 8), R("alg", 9 * u - 8, 8 * u), R("tmp", 9 * u - 8, 8 * u), O.min)
+        if u < 6:
+            both(R("cu", 8 * u + 8, 8 * u + 14 - u), u + 2, u + 1)
+        if u == 2:
+            ts(R("mk8"), R("nn"), R("ca", 8, 9), None, O.add)
+        if u == 6:
+            both(R("sl8"), 0, 14)
+    al = R("alg", 0, 64, st=9)
+    scan(R("cn"), al, al, O.add, O.max)
+    tt(R("ck"), R("mk8"), al, O.mult)
+    ts(R("ms8"), R("sl8"), R("ca", 8, 9), None, O.add)
+    tt(R("z8"), R("cn"), R("ck"), O.add)
+    red(R("nlv"), R("z8"), O.min, True)
+    ts(R("kl", 0, 1), R("nlv"), 8192.0, R("ca", 4, 5), O.mult, O.min)
+    ts(R("own"), R("pm"), R("nlv"), None, O.add)
+    ts(R("nls"), R("nlv"), 8192.0, R("ca", 4, 5), O.mult, O.min)
+    ttg(R("same"), R("ids"), R("kl", 0, 1), R("own"), O.is_equal)
+    tt(R("ms9"), R("ms8"), al, O.mult)
+    red(R("dup"), R("same"), O.max)
+    tt(R("y8"), R("cn"), R("ms9"), O.add)
+    ts(R("kd", 0, 1), R("dup"), R("ca", 4, 5), R("nls"), O.mult, O.max)
+    send([(q, R("kd"), R("kla", 2 * here[q], 2 * here[q] + 2)) for q in others], "ark")
+
+    parts = [(ch, b) for ch in range(2) for b in range(4)]
+    for ch, b in parts:
+        mm(BANKS[4 * ch + b], CUT[ch][1] - CUT[ch][0], "eq", 128 * b, "vq", CUT[ch][0], CUT[ch][1], True, False)
+    scatter(R("wo"), R("kd", 0, 1), R("ptv", 16 * r, 16 * r + 16))
+    red(R("slv"), R("y8"), O.min, True)
+    ts(R("yv"), R("slv"), 0.5, 8192.0, O.is_lt, O.mult)
+    turn(R("tko"), R("wo", P * r, P * r + P))
+    tt(R("zz", 96, 97), R("slv"), R("yv"), O.mult)
+    turn(R("yr"), R("zz", 96, 128))
+    tt(R("wown"), R("tko", 0, P, st=32), R("tko", 16, P, st=32), O.min)
+    gather(R("yd"), R("yr"), R("hv"))
+    turn(R("ydt"), R("yd"))
+    for a in range(4):
+        for b in range(4):
+            copy(R("ksl", 2 * a, 2 * a + 2, 32 * b, 32 * b + 32), R("ydt", 0, 64, 32 * a, 32 * a + 32, 32), "s")
+
+    note(None, [R("kla")], [], "ark", count["ark"])
+    for k, q in reversed(list(enumerate(others))):
+        scatter(R("wk"), R("kla", 2 * k, 2 * k + 1), R("ptv", 16 * q, 16 * q + 16))
+        if k == 2:
+            ts(R("kt"), R("nlv"), 0.5, None, O.is_lt)
+        if k == 1:
+            ts(R("kw"), R("nlv"), 8192.0, 1.0, O.mult, O.add)
+    tt(R("kv"), R("kw"), R("kt"), O.mult)
+    turn(R("tk"), R("wk", P * r, P * r + P))
+    ts(R("zz", 64, 68), R("mk4"), R("kv"), None, O.mult)
+    tt(R("wa"), R("tk", 0, P, st=32), R("tk", 16, P, st=32), O.min)
+    pick("kq", 0, 64, "uc", UW, R("ksl", 0, 4))
+    tt(R("wb"), R("wa"), R("wown"), O.min)
+    turn(R("kpt"), R("zz", 64, 96))
+    tt(R("wc", 0, 12, 0, 64), R("wb", 0, 12, 0, 64), R("wb", 0, 12, 64, 128), O.min)
+    for a in range(4):
+        tt(R("zz", 32, 44, 32 * a, 32 * a + 32), R("wc", 0, 12, 0, 32), R("wc", 0, 12, 32, 64), O.min)
+    turn(R("lr"), R("zz", 32, 64))
+    pick("kq", 64, 128, "uc", UW, R("ksl", 4, 8))
+    gather(R("ld"), R("lr"), R("hv"))
+    tt(R("kp2"), R("kpt", 0, 32, st=2), R("kpt", 1, 32, st=2), O.add)
+    turn(R("ldt"), R("ld"))
+    tt(R("kp3"), R("kp2", 0, 16, st=2), R("kp2", 1, 16, st=2), O.add)
+    copy(R("ln", 0, 24, st=2), R("ldt", 0, 12))
+    copy(R("ln", 1, 24, st=2), R("ldt", 32, 44), "s")
+    ts(R("kpo"), R("kp3"), -1.0, None, O.add)
+    for a in range(4):
+        dma("y", T.kp[:, 8 * a:8 * a + 8], R("kpo", 0, 8, 32 * a, 32 * a + 4), "dk", 4)
+
+    note(None, [R("xa" + s, 32 * q, 32 * q + 32) for q in others for s in ("", "s")], [], "arx", count["arx"])
+    for a, b in CUT:
+        pick("qp", a, b, "xa", 160, R("ln", a // 16, b // 16))
+    for ch, b in parts:
+        mm(BANKS[4 * ch + b], CUT[ch][1] - CUT[ch][0], "eq", 128 * b, "qp", CUT[ch][0], CUT[ch][1], False, True)
+    ts(R("sl0"), R("ln"), N * A - 0.5, float(P), O.is_lt, O.mult)
+    tt(R("sl1"), R("sl0"), R("jc"), O.add)
+
+    def half(ch, bs):
+        for b in bs:
+            copy(R("nt", 4 * CUT[ch][0] + b, 4 * CUT[ch][1], st=4), R(BANKS[4 * ch + b], 0, CUT[ch][1] - CUT[ch][0]), "sv"[b % 2])
+
+    def new(ch):
+        quant("mg", P + CUT[ch][0], P + CUT[ch][1], R("nt", 4 * CUT[ch][0], 4 * CUT[ch][1]))
+
+    def store(ch, late):
+        a, b = CUT[ch]
+        pick("oq", a, b, "mg", 2 * P, R("sl", a // 16, b // 16))
+        dma("y", T.oc[:, 4 * a:4 * b], R("oq", a, b), "do%d" % ch, 1)
+        for k in range(4):
+            dma("sy"[k % 2] if late else "y", T.osc[4 * k:4 * k + 4, a:b], R("oqs", a, b, 32 * k, 32 * k + 4), "dp%d" % ch, 4)
+    half(0, (0, 1))
+    copy(R("sl"), R("sl1"))
+    half(0, (2, 3))
+    mm(BANKS[0], 128, "wq", 0, "kq", 0, 128)
+    new(0)
+    half(1, (0, 2))
+    store(0, False)
+    half(1, (1, 3))
+    copy(R("yt"), R(BANKS[0], 0, 128), "s")
+    dma("y", T.y[:, :], R("yt"), "dy", 1)
+    new(1)
+    store(1, True)
+
+    for s in sorted(count):
+        g.wait_ge(T.sem[s], count[s])

@@ -6,36 +6,36 @@ UB = 32
 UR = UB + P
 UW = UR + 3 * LC
 MO = 3 * P
-MW = MO + 4 * P
 DB = P
 DUMP = N * P + 4
 IW = DUMP + 20
+NOP = 224
 CUT = ((0, 160), (160, 384))
 
 F32, BF, I32, U16, U8, F8 = "float32", "bfloat16", "int32", "uint16", "uint8", "float8_e4m3fn_x4"
 SCRATCH = {}
 for _d, _names in (
-    (BF, "tbt:1536 xt:512 wt:512 et:2048 nt:1536"),
-    (F8, "vq:384 xq:128 wq:128 eq:512 xa:160 uc:896 pk:480 ex:512 kq:128 qp:384 mg:768 oq:384"),
-    (U8, "vqs:384 xqs:128 wqs:128 eqs:512 xas:160 ucs:896 pks:480 exs:512 kqs:128 qps:384 mgs:768 oqs:384"),
-    (I32, "kci:64"), (U16, "bl:4 bo:8 br:4 pl:2 rl:24 hv:4"), (BF, "ones:16 eye:128 ptv:64"),
-    (F32, "kcf:512 idt:1560 ids:1560 cv:192 zz:128"),
-    (I32, "cdh:16 cdi:32"), (U16, "off:32 wl:12 lst:10 lnd:30 ls:30"), (BF, "mk0:2688 mk1:2688 tm:768 m1:24"),
-    (F32, "req:192 x0:32 xt0:32 wn:1152 wnt:160 lr:32 ld:64 ldt:64"),
-    (F32, "cdp:32 zp:12 zrep:384 zf:416 gx:128 zr:512 zt:512 z2:128 sf:32 sc:16 nc:16 n1:24 nr:64 tie:64"), (U16, "og:32 sw:32 nl:4 kl:2"),
-    (F32, "cs:128 cg:512 ob:128 obt:128 row:64 gg:64 dw:64 w2:64 bb:64 rks:68 l2a:8 l2b:8 t1:128 t1t:128 t2:640 t2t:256 cu:64 tmp:64 alg:64"), (U16, "l1:4 l2:8"),
+    (BF, "tbt:1664 xt:640 wt:512 et:2048 nt:1536"),
+    (F8, "vq:384 xq:128 wq:128 eq:512 xa:352 uc:896 pk:480 ex:512 kq:128 qp:384 mg:768 oq:384"),
+    (U8, "vqs:384 xqs:128 wqs:128 eqs:512 xas:352 ucs:896 pks:480 exs:512 kqs:128 qps:384 mgs:768 oqs:384"),
+    (I32, "kci:64"), (U16, "bl:4 bo:8 br:4 pl:4 rl:24 hv:4 wr:6"), (BF, "ones:16 ptv:64"),
+    (F32, "kcf:512 idt:1560 ab:516 cv:192 zz:128"),
+    (I32, "cdh:16 cdi:32"), (U16, "off:32 wl:12 lst:16 lnd:30"), (BF, "mk0:2688 mk1:2688 tm:768 m1:24"),
+    (F32, "req:192 x0:32 xt0:32 wn:1184 wnt:352"),
+    (F32, "cdp:32 zp:12 zrep:384 zf:416 gx:32 zr:512 zt:512 z2:32 sf:32 sc:16 nc:16 n1:24 nr:64 tie:64"), (U16, "og:32 sw:32 nl:4 kl:2"),
+    (F32, "cs:128 cg:512 ob:128 obt:128 gg:64 dw:64 w2:64 bb:64 rks:64 l2a:8 l2b:8 t1:128 t1t:128 t2:640 t2t:256 cu:64 tmp:64 alg:64"), (U16, "l1:4 l2:8"),
     (F32, "pr:160 kpt:32 yr:32 yd:64 ydt:64 yt:128"), (U16, "kd:2 ksl:8 kla:6"),
-    (BF, "wk:1568 wo:1568 tk:384 tko:384"), (F32, "wm:64 sl0:24 sl1:24"), (U16, "ln:24 sl:24"),
+    (BF, "wk:1600 wo:1600 tk:800 tko:800"), (F32, "wm:128 sl0:24 sl1:24"), (U16, "ln:32 sl:24"),
 ):
     for _n in _names.split():
         SCRATCH[_n.split(":")[0]] = ("sbuf", [128, int(_n.split(":")[1])], _d)
 PART = {}
 for _d, _names in (
-    ("kcf", "pf:8 cq:8 ca:12 t32:32 tri:32 dc0:12 dc:12 dc1:12 plc:12 c4:4 bo0:8 br0:4 br1:4 hv0:4 c2:8 cst0:4 cst:4 jc0:24 jc:24 mk4:4 rst0:64 rst:64 pm0:16 pm:16 pt0:64"),
-    ("kci", "ip:2 ib:4 it:8 ir:24"),
+    ("kcf", "pf:10 xr:10 cq:8 ca:12 t32:32 tri:32 dc0:12 dc:12 dc1:12 plc:12 c4:4 bo0:8 br0:4 br1:4 hv0:4 c2:8 jc0:24 jc:24 mk4:4 rst0:64 rst:64 pm0:16 pm:16 pt0:64 ce:1"),
+    ("kci", "ip:2 ib:4 it:10 ir:24"),
     ("req", "mm:12 tot:1 base:1 sn:12 g1:12 g2:12 g3:12"),
     ("pr", "nn:8 sl8:8 mk8:8 ms8:8 ms9:8 cn:8 ck:8 z8:8 y8:8 nlv:1 nls:1 slv:1 kt:1 kw:1 kv:1 yv:1 kp2:16 kp3:8 kpo:8 own:16 same:16 dup:1"),
-    ("wm", "wa:12 wb:12 wc:12 wown:12"),
+    ("wm", "wa:25 wb:25 wc:25 wown:25"),
 ):
     _c = 0
     for _n in _names.split():
@@ -45,7 +45,7 @@ for _d, _names in (
 BANKS = ["pb%d" % _b for _b in range(8)]
 for _n in BANKS:
     SCRATCH[_n] = ("psum", [128, 512], F32)
-SEMAPHORES = ["ev", "ec", "et_", "ep", "dch", "dcd", "dx", "dtb", "dw", "dxa", "dmg", "dz", "dk", "dy", "do0", "do1", "dp0", "dp1",
+SEMAPHORES = ["ev", "ec", "et_", "ep", "dch", "dcd", "dx", "dtb", "dw", "dmg", "dk", "dy", "do0", "do1", "dp0", "dp1",
               "arx", "arl", "arc", "ark", "loc"]
 
 
@@ -131,14 +131,15 @@ def rank_program(g, core, T, topo):
     def ttg(o, win, off, b, f):
         op("v", lambda: g.vector.tensor_tensor(o["ap"], win["ap"].indirect(off["ap"]), b["ap"], f), [o], [win, off, b])
 
-    def ts(o, a, s1, s2, f1, f2=None):
-        ins = [a] + [s for s in (s1, s2) if isinstance(s, dict)]
+    def ts(o, a, s1, s2, f1, f2=None, off=None):
+        ins = [a] + [s for s in (s1, s2, off) if isinstance(s, dict)]
+        v0 = a["ap"] if off is None else a["ap"].indirect(off["ap"])
         v1 = s1["ap"] if isinstance(s1, dict) else s1
         v2 = s2["ap"] if isinstance(s2, dict) else s2
         if f2 is None:
-            op("v", lambda: g.vector.tensor_scalar(o["ap"], a["ap"], v1, None, f1), [o], ins)
+            op("v", lambda: g.vector.tensor_scalar(o["ap"], v0, v1, None, f1), [o], ins)
         else:
-            op("v", lambda: g.vector.tensor_scalar(o["ap"], a["ap"], v1, v2, f1, f2), [o], ins)
+            op("v", lambda: g.vector.tensor_scalar(o["ap"], v0, v1, v2, f1, f2), [o], ins)
 
     def red(o, a, f, size=False):
         kw = {"apply_absolute_value": True} if size else {}
@@ -200,10 +201,22 @@ def rank_program(g, core, T, topo):
             count[sem] = count.get(sem, 0) + m
         g.remote_dma_fused(tr, local_sem=T.sem.loc)
 
+    def spread(s, dst, sem):
+        need("p", [], [s])
+        e = [n for n in topo.engines(core, T.cores[others[0]]) if all(n in topo.engines(core, T.cores[q]) for q in others)]
+        ids = [DstId(rid=topo.addr(T.cores[q])[0], pnc=topo.addr(T.cores[q])[1]) for q in others]
+        count["loc"] = count.get("loc", 0) + len(e)
+        count[sem] = count.get(sem, 0) + len(e) * len(others)
+        g.remote_dma_fused([RemoteDMATransfer(dst_ids=ids, dma_engine_mask=sum(1 << n for n in e), remote_sem=T.sem[sem],
+                                              srcs=[u8(s)], dsts=[u8(dst(q)) for q in others])], local_sem=T.sem.loc)
+
+    def points(s):
+        spread(R("xq" + s, 0, 32), lambda q: R("xa" + s, 32 * r + 96 * (r > q), 32 * r + 96 * (r > q) + 32), "arx")
+
     for k in range(8):
         dma("ys"[k % 2], R("cdh", 0, 16, 16 * k, 16 * k + 16), T.cd[:, 16 * (k % 2):16 * (k % 2) + 16], "dch", 8)
     dma("y", R("xt", 0, 128), T.x[:, :], "dx", 1)
-    dma("y", R("tbt"), T.tb[:, :], "dtb", 1)
+    dma("y", R("tbt", 128), T.tb[:, :], "dtb", 1)
     for k in range(8):
         dma("y", R("cdi", 0, 32, 16 * k, 16 * k + 16), T.cd[:, :], "dcd", 8)
     dma("y", R("wt"), T.w[:, :], "dw", 1)
@@ -214,61 +227,60 @@ def rank_program(g, core, T, topo):
     iota("dc0", [[1, 12]], DB, 0)
     iota("cv", [[32, 12], [1, 16]], 0, 0)
     iota("idt", [[1, IQ]], 0, 0, 0, IQ)
-    iota("hv0", [[16, 2], [0, 2]], 0, 0)
-    iota("plc", [[32, 12]], UB - 32 * r, 1)
-    iota("ir", [[1, 12], [0, 2]], 0, 0)
-    iota("c4", [[1, 4]], 0, 0)
     memset(R("mk0", MO, MO + P), 0.0)
     p = R("ip", 0, 1)
-    for k, (sh, msk) in enumerate(((0, 15), (4, 1), (0, 7), (4, 7), (0, 3), (5, 3), (0, 31), (1, 3))):
+    for k, (sh, msk) in enumerate(((0, 15), (4, 1), (0, 1), (4, 7), (0, 3), (5, 3), (0, 31), (1, 3), (1, 7))):
         ts(R("it", k, k + 1), p, sh, msk, O.logical_shift_right, O.bitwise_and)
     memset(R("mk1", MO, MO + P), 0.0)
-    copy(R("pf", 0, 8), R("it", 0, 8))
-    lcol, hcol, _ecol, gcol, p3, acol, pcol, bcol = [R("pf", k, k + 1) for k in range(8)]
+    copy(R("pf", 0, 9), R("it", 0, 9))
+    lcol, hcol, ecol, gcol, p3, acol, pcol, bcol, wcol = [R("pf", k, k + 1) for k in range(9)]
     memset(R("ones"), 1.0)
     ts(R("cq", 0, 1), acol, float(-P), float(MO), O.mult, O.add)
     memset(R("xt", 128, 512), 0.0)
-    ts(R("tri"), R("t32"), pcol, None, O.is_gt)
     lin(R("ca", 0, 1), hcol, 16.0)
     lin(R("ca", 6, 7), pcol, 12.0)
     lin(R("dc"), R("dc0"), 1.0, R("ca", 6, 7))
     lin(R("cv"), R("cv"), 1.0, R("ca", 0, 1))
     lin(R("dc1"), R("dc"), 1.0, 1.0)
-    memset(R("wn", 0, LC), 0.0)
+    lin(R("wn", 16, 208), R("cv"), 0.0)
+    lin(R("zz"), R("cv", 0, 128), 0.0)
     ts(R("off", 0, 32, st=2), R("cdh"), R("cq", 0, 1), None, O.add)
+    ts(R("tri"), R("t32"), pcol, None, O.is_gt)
+    ts(R("cq", 3, 4), acol, float(r), float(-LC), O.is_gt, O.mult)
 
     for i in range(A // 2):
         scatter(R("mk%d" % (i % 2)), R("off", 2 * i, 2 * i + 1), R("ones"))
+        if i == 5:
+            quant("xq", 0, 128, R("xt", 0, 512))
+            points("")
+    iota("plc", [[32, 12]], UB - 32 * r, 1)
+    iota("ir", [[1, 12], [0, 2]], 0, 0)
+    iota("c4", [[1, 4]], 0, 0)
+    iota("ce", [[1, 1]], -3, -4)
+    iota("hv0", [[16, 2], [0, 2]], 0, 0)
     for k in range(2):
         turn(R("tm", P * k, P * k + P), R("mk%d" % k, MO, MO + P))
 
-    quant("xq", 0, 128, R("xt"))
-    for s, k in (("", 0), ("s", 3)):
-        send([(q, R("xq" + s, 0, 32), R("xa" + s, 32 * r, 32 * r + 32)) for q in others], "arx", k)
-    for s in ("", "s"):
-        dma("y", R("uc" + s, 0, 32), R("xq" + s, 32, 64), "dz", 2)
-        dma("y", R("xa" + s, 32 * r, 32 * r + 32), R("xq" + s, 0, 32), "dxa", 4)
-        dma("y", R("xa" + s, 128, 160), R("xq" + s, 32, 64), "dxa", 4)
-
+    lin(R("xr", 0, 1), hcol, -1.0, ecol, AF.Abs)
+    lin(R("xr", 1, 2), hcol, -1.0, 6.0)
+    lin(R("xr", 2, 3), hcol, -1.0, 13.0)
+    lin(R("xr", 9, 10), ecol, -1.0, lcol)
+    lin(R("xr", 3, 4), R("xr", 0, 1), R("xr", 1, 2), wcol)
+    lin(R("xr", 5, 6), R("xr", 0, 1), R("xr", 2, 3), wcol)
+    lin(R("xr", 7, 8), R("xr", 0, 1), 1.0, R("xr", 9, 10))
+    lin(R("cq", 6, 7), R("cq", 3, 4), 1.0, float(UR - 1))
+    lin(R("xr", 4, 5), R("xr", 3, 4))
+    lin(R("xr", 6, 7), R("xr", 5, 6), 1.0, 8.0)
+    lin(R("xr", 8, 9), R("xr", 7, 8), 1.0, 16.0)
+    lin(R("cq", 2, 3), acol, float(LC), R("cq", 6, 7))
     lin(R("cq", 1, 2), acol, float(-P), 16.0)
     lin(R("ca", 1, 2), gcol, 4.0)
-    lin(R("ca", 4, 5), lcol, 1.0, float(DUMP))
-    lin(R("ca", 2, 3), hcol, -1.0, 1.0)
-    lin(R("ca", 3, 4), hcol, 32.0)
-    lin(R("ca", 5, 6), hcol, -32.0, 32.0)
-    lin(R("ca", 8, 9), p3, -1.0, -1.0)
-    for k in range(8):
-        lin(R("et", 256 * k, 256 * k + 256), R("idt", 0, 256), 0.0)
-    eye, nil = R("eye"), R("et", 0, 128)
-    op("p", lambda: g.affine_select(eye["ap"], nil["ap"], [[1, 128]], O.not_equal, 0.5, 0, -1), [eye], [nil])
-    for k in range(1, 4):
-        lin(R("idt", IQ * k, IQ * k + IQ), R("idt", 0, IQ), 1.0, float(IQ * k))
     for j in range(4):
         copy(R("cdp", 8 * j, 8 * j + 8), R("cdi", j, 32, st=4), "s")
-    for b in range(4):
-        copy(R("et", 513 * b, 512 * b + 512, st=4), eye, "s")
+    for k in range(1, 4):
+        lin(R("idt", IQ * k, IQ * k + IQ), R("idt", 0, IQ), 1.0, float(IQ * k))
     tt(R("m1"), R("tm", 0, 2 * P, st=32), R("tm", 16, 2 * P, st=32), O.max)
-    ts(R("hv"), R("hv0"), lcol, None, O.add)
+    memset(R("zf", 400, 416), 0.0)
     tt(R("mm"), R("m1", 0, 12), R("m1", 12, 24), O.max)
     memset(R("zf", 0, 16), 0.0)
     red(R("tot"), R("mm"), O.add)
@@ -279,101 +291,82 @@ def rank_program(g, core, T, topo):
     tt(R("g2"), R("g1"), R("mm"), O.mult)
     red(R("base"), R("xt0"), O.add)
     tt(R("g3"), R("g2"), R("dc"), O.add)
-    ts(R("cq", 3, 4), acol, float(r), float(-LC), O.is_gt, O.mult)
     ts(R("wl"), R("g3"), R("base"), None, O.add)
-    ts(R("cq", 2, 3), acol, float(LC), R("cq", 3, 4), O.mult, O.add)
-    scatter(R("wn"), R("wl"), R("cv"))
+    copy(R("wr"), R("xr", 3, 9))
+    scatter(R("wn", 32), R("wl"), R("cv"))
     ts(R("zp"), R("sn"), R("base"), R("cq", 2, 3), O.add, O.add)
-    turn(R("wnt"), R("wn", 0, LC))
-    memset(R("zz"), 0.0)
-    tt(R("zz", 0, 5), R("wnt", 0, LC, st=32), R("wnt", 16, LC, st=32), O.add)
-    ts(R("zp"), R("zp"), float(UR - 1), None, O.add)
-    turn(R("lr"), R("zz", 0, 32))
+    turn(R("wnt", 0, LC), R("wn", 32, 192))
+    turn(R("wnt", LC), R("wn", 16, 208))
     copy(R("zp", 0, 12, 32 * r, 32 * r + 32), R("plc", 0, 12, 32 * r, 32 * r + 32))
-    gather(R("ld"), R("lr"), R("hv"))
+    tt(R("zz", 0, 11), R("wnt", 0, 352, st=32), R("wnt", 16, 352, st=32), O.add)
     copy(R("rl"), R("ir"))
-    turn(R("ldt"), R("ld"))
-    for k in range(2):
-        copy(R("lst", k, 10, st=2), R("ldt", 32 * k, 32 * k + 5), "vs"[k])
-    send([(q, R("lst"), R("lnd", 10 * here[q], 10 * here[q] + 10)) for q in others], "arl")
+    gather(R("lst"), R("zz", 0, 16), R("wr", 0, 1))
+    spread(R("lst", 0, 10), lambda q: R("lnd", 10 * here[q], 10 * here[q] + 10), "arl")
 
     gather(R("zrep"), R("zp"), R("rl"), "s")
     iota("br0", [[32, 4]], 0, 0)
-    iota("rst0", [[0, 4], [1, 16]], 0, 0)
+    iota("rst0", [[32, 4], [0, 16]], 0, 0)
     iota("pm0", [[4, 4], [0, 4]], 3, 0)
     iota("ib", [[128, 4]], 0, 1)
     iota("bo0", [[33, 4], [0, 2]], 0, 0)
-    iota("cst0", [[32, 4]], 0, 0)
-    iota("pt0", [[A, N], [1, 4], [0, 4]], 0, 0)
     iota("jc0", [[16, 24]], 0, 0)
-    quant("vq", 0, P, R("tbt"))
-    memset(R("zf", 400, 416), 0.0)
-    quant("uc", UB, UR, R("tbt"))
-    ts(R("gx", 0, 32), R("cdp"), R("cq", 1, 2), 15.0, O.add, O.max)
-    turn(R("zf", 16, 400), R("zrep"))
-    tt(R("gx", 32, 64, st=2), R("gx", 1, 32, st=2), R("gx", 0, 32, st=2), O.subtract)
-    tt(R("gx", 33, 64, st=2), R("gx", 0, 32, st=2), R("gx", 1, 32, st=2), O.subtract)
+    ts(R("gx"), R("cdp"), R("cq", 1, 2), 15.0, O.add, O.max, R("wr", 4, 6))
     ts(R("pl", 0, 1), bcol, 8.0, gcol, O.mult, O.add)
-    ts(R("gx", 64, 96), R("gx", 32, 64), hcol, None, O.mult)
+    quant("vq", 0, P, R("tbt", 128))
+    ts(R("og"), R("gx"), 400.0, None, O.min)
+    turn(R("zf", 16, 400), R("zrep"))
+    memset(R("tbt", 0, 128), 0.0)
     gather(R("nc"), R("cdp"), R("pl", 0, 1))
-    tt(R("gx", 96, 128), R("gx", 64, 96), R("gx", 0, 32), O.add)
-    ts(R("og"), R("gx", 96, 128), 400.0, None, O.min)
+    gather(R("zr", 0, 256), R("zf"), R("og", 0, 16), "s")
 
     note(None, [R("lnd", 0, 30)], [], "arl", count["arl"])
-    for a in range(4):
-        copy(R("ls", 0, 30, 32 * a, 32 * a + 32), R("lnd", 0, 30, 32 * r, 32 * r + 32), "vs"[a % 2])
+    for a in others:
+        copy(R("lnd", 0, 30, 32 * a, 32 * a + 32), R("lnd", 0, 30, 32 * r, 32 * r + 32))
     for k, q in enumerate(others):
-        pick("pk", LC * k, LC * k + LC, "vq", P, R("ls", 10 * k, 10 * k + 10))
+        pick("pk", LC * k, LC * k + LC, "vq", P, R("lnd", 10 * k, 10 * k + 10))
         send([(q, R("pk", LC * k, LC * k + LC), R("uc", UR + LC * here[q], UR + LC * here[q] + LC))], "arc")
     send([(q, R("pks", LC * k, LC * k + LC), R("ucs", UR + LC * here[q], UR + LC * here[q] + LC)) for k, q in enumerate(others)], "arc", 3)
 
     iota("t1", [[0, 128]], 0, 0)
     iota("t2", [[0, 256]], 0, 0, 0, 256)
+    iota("pt0", [[A, r + 1], [1, 4], [0, 4]], 0, 0, 0, 16 * r + 16)
+    if r < N - 1:
+        iota("pt0", [[A, N - 1 - r], [1, 4], [0, 4]], A * r + 128, 0, 16 * r + 16, 64)
+    points("s")
     for n in ("wk", "wo"):
-        iota(n, [[0, P]], N * A, 0, P * r, P * r + P)
-    lin(R("br1"), R("br0"), 1.0, R("ca", 0, 1))
+        iota(n, [[0, 416]], NOP, 0, P * r + 16, P * r + 432)
+    gather(R("zr", 256, 512), R("zf"), R("og", 16, 32), "s")
     for j in range(4):
         lin(R("gg", 16 * j, 16 * j + 16), R("t32", 0, 16), 0.0, R("nc", 2 * j, 2 * j + 1))
-    gather(R("zr"), R("zf"), R("og"), "s")
-    lin(R("cst"), R("cst0"), 1.0, R("ca", 0, 1))
+    lin(R("br1"), R("br0"), 1.0, R("ca", 0, 1))
+    lin(R("rst"), R("rst0"), 1.0, R("ca", 0, 1))
     lin(R("n1", 8, 16), R("nc", 0, 8), 1.0 / 8192)
-    lin(R("jc"), R("jc0"), 1.0, lcol)
-    lin(R("ptv"), R("pt0"), 1.0, R("ca", 1, 2))
-    lin(R("ca", 7, 8), hcol, 28.0, 4.0)
-    lin(R("ca", 9, 10), hcol, -28.0, 32.0)
+    lin(R("ca", 2, 3), hcol, -1.0, 1.0)
+    lin(R("ca", 3, 4), hcol, 32.0)
+    lin(R("ca", 5, 6), hcol, -32.0, 32.0)
+    lin(R("ca", 7, 8), hcol, 1052.0, -1020.0)
+    lin(R("ca", 9, 10), hcol, -1052.0, 32.0)
     lin(R("ca", 10, 11), hcol, 512.0)
-    lin(R("ca", 11, 12), hcol, -512.0, 528.0)
-    lin(R("cq", 4, 5), lcol, hcol, R("ca", 10, 11))
-    lin(R("cq", 5, 6), lcol, R("ca", 2, 3), R("ca", 11, 12))
-    lin(R("c2", 0, 8, st=2), R("c4"), R("ca", 7, 8), R("cq", 4, 5))
-    lin(R("c2", 1, 8, st=2), R("c4"), R("ca", 9, 10), R("cq", 5, 6))
+    lin(R("ca", 11, 12), hcol, -1024.0, 528.0)
 
+    turn(R("zt", 0, 256), R("zr", 0, 256))
     copy(R("nl"), R("nc", 0, 8, st=2))
-    ts(R("br"), R("br1"), lcol, None, O.add)
-    ts(R("rst"), R("rst0"), 0.5, None, O.is_gt)
-    ts(R("pm"), R("pm0"), lcol, 4096.0, O.is_ge, O.mult)
-    memset(R("kd"), 0.0)
+    memset(R("xt", 512, 640), 0.0)
     quant("wq", 0, 128, R("wt"))
-    quant("eq", 0, 512, R("et"))
+    ts(R("pl", 2, 3), R("pl", 0, 1), hcol, None, O.subtract)
+    turn(R("zt", 256, 512), R("zr", 256, 512))
+    quant("xa", 32 * r, 32 * r + 128, R("xt", 0, 512))
+    tt(R("z2", 0, 32, 0, 64), R("zt", 0, 512, 0, 64, 16), R("zt", 0, 512, 64, 128, 16), O.add)
+    for a in range(4):
+        tt(R("sf", 0, 32, 32 * a, 32 * a + 32), R("z2", 0, 32, 0, 32), R("z2", 0, 32, 32, 64), O.add)
+    gather(R("sw"), R("sf"), R("wr", 4, 6))
+    quant("uc", 0, UR, R("tbt"))
+    gather(R("sc"), R("sf"), R("pl", 2, 3))
     ttg(R("nr"), R("idt"), R("nl"), R("gg"), O.is_lt)
-    turn(R("zt"), R("zr"))
-    ev, od = R("z2", 0, 32, 0, 32, 2), R("z2", 1, 32, 0, 32, 2)
-    ts(R("tie"), R("nr"), -2.0 ** -100, None, O.mult)
-    tt(R("z2", 96, 128, 0, 64), R("zt", 0, 512, 0, 64, 16), R("zt", 0, 512, 64, 128, 16), O.add)
-    tt(R("z2", 0, 32, 0, 32), R("z2", 96, 128, 0, 32), R("z2", 96, 128, 32, 64), O.add)
-    tt(R("z2", 32, 48, 0, 32), od, ev, O.subtract)
-    ts(R("mk4"), R("c4"), p3, None, O.is_equal)
-    ts(R("z2", 48, 64, 0, 32), R("z2", 32, 48, 0, 32), R("pf", 1, 2, 0, 32), None, O.mult)
-    memset(R("alg", 0, 1), 1.0)
-    tt(R("z2", 64, 96, 0, 32, 2), ev, R("z2", 48, 64, 0, 32), O.add)
-    tt(R("z2", 65, 96, 0, 32, 2), od, R("z2", 48, 64, 0, 32), O.subtract)
     copy(R("bl"), R("ib"))
     ts(R("bo"), R("bo0"), R("ca", 1, 2), None, O.add)
-    for a in range(4):
-        copy(R("sf", 0, 32, 32 * a, 32 * a + 32), R("z2", 64, 96, 0, 32), "vs"[a % 2])
-    copy(R("sw"), R("sf"))
-    gather(R("sc"), R("sf"), R("pl", 0, 1))
-    ts(R("n1", 16, 24), R("sc", 0, 8), 1.0 / 8192, None, O.mult)
+    ts(R("br"), R("br1"), lcol, None, O.add)
+    ts(R("tie"), R("nr"), -2.0 ** -100, None, O.mult)
 
     note(None, [R(n, UR, UW) for n in ("uc", "ucs")], [], "arc", count["arc"])
     for j in range(4):
@@ -381,37 +374,50 @@ def rank_program(g, core, T, topo):
     for j, w in ((0, 1), (0, 0), (1, 1), (1, 0), (2, 1), (3, 1), (2, 0), (3, 0)):
         mm(BANKS[4 * w + j], 128, "ex", 128 * j, "xq" if w else "ex", 0 if w else 128 * j, 128 if w else 128 * j + 128)
         if w:
-            copy(R("cs", 32 * j, 32 * j + 32), R(BANKS[4 + j], 0, 32), "ssvv"[j])
+            copy(R("cs", 32 * j, 32 * j + 32), R(BANKS[4 + j], 0, 32))
         else:
             copy(R("cg", 128 * j, 128 * j + 128), R(BANKS[j], 0, 128), "s")
-    lin(R("ids"), R("idt"), 1.0 / 8192)
+    lin(R("cq", 4, 5), lcol, hcol, R("ca", 10, 11))
+    lin(R("cq", 5, 6), lcol, R("ca", 2, 3), R("ca", 11, 12))
+    lin(R("c2", 0, 8, st=2), R("c4"), R("ca", 7, 8), R("cq", 4, 5))
+    lin(R("c2", 1, 8, st=2), R("c4"), R("ca", 9, 10), R("cq", 5, 6))
+    lin(R("ca", 4, 5), lcol, 1.0, float(DUMP))
+    lin(R("ca", 8, 9), p3, -1.0, -1.0)
     gather(R("ob"), R("cs"), R("bo"))
     own = R("ob", 0, 128, st=2)
     need("y", [], [R("ob")])
     for s in ("", "s"):
         dma("y", R("mg" + s, 0, P), R("vq" + s), "dmg", 2)
+    ts(R("n1", 16, 24), R("sc", 0, 8), 1.0 / 8192, None, O.mult)
     turn(R("obt"), R("ob"))
-    gather(R("gg"), R("cg"), R("bl"))
-    gather(R("row"), R("obt"), R("br"))
-    tt(R("bb"), R("gg"), own, O.is_lt)
-    tt(R("dw"), R("row"), own, O.subtract)
+    ttg(R("bb"), R("cg"), R("bl"), own, O.is_lt)
+    ttg(R("dw"), R("obt"), R("br"), own, O.subtract)
+    memset(R("kd"), 0.0)
     tt(R("w2"), R("dw"), R("tie"), O.is_gt)
-    scan(R("rks", 0, 64), R("rst"), R("w2"), O.mult, O.add)
+    memset(R("alg", 0, 1), 1.0)
+    scan(R("rks"), R("rst"), R("w2"), O.max, O.add)
+    ts(R("mk4"), R("c4"), p3, None, O.is_equal)
     rank = R("rks", 15, 64, st=16)
-    tt(R("rks", 64, 68), rank, R("cst"), O.add)
+    copy(R("l1"), rank)
     ts(R("l2a", 0, 8, st=2), rank, R("ca", 5, 6), None, O.mult)
     ts(R("l2a", 1, 8, st=2), rank, R("ca", 3, 4), None, O.mult)
-    copy(R("l1"), R("rks", 64, 68))
-    tt(R("l2b"), R("l2a"), R("c2"), O.add)
     scatter(R("t1"), R("l1"), R("bb"))
-    copy(R("l2"), R("l2b"))
+    tt(R("l2b"), R("l2a"), R("c2"), O.add)
     copy(R("t1", 15, 128, st=16), R("n1", 8, 16))
-    copy(R("t1", 14, 128, st=16), R("n1", 16, 24), "s")
+    copy(R("t1", 14, 128, st=16), R("n1", 16, 24))
+    copy(R("l2"), R("l2b"))
     turn(R("t1t"), R("t1"))
+    ts(R("pm"), R("pm0"), lcol, 4096.0, O.is_ge, O.mult)
     scatter(R("t2"), R("l2"), R("t1t"))
+    ts(R("hv"), R("hv0"), lcol, None, O.add)
     for k in range(1, 4):
-        copy(R("t2", k, 256, st=4), R("t2", 0, 256, st=4), "vvsv"[k])
+        copy(R("t2", k, 256, st=4), R("t2", 0, 256, st=4))
     turn(R("t2t"), R("t2", 0, 256))
+    lin(R("ab"), R("idt", 0, 516), 1.0, R("ce"), AF.Abs)
+    for b in range(4):
+        lin(R("et", 512 * b, 512 * b + 512), R("ab", 3 - b, 515 - b), -0.5, 0.5, AF.Relu)
+    lin(R("ptv"), R("pt0"), 1.0, R("ca", 1, 2))
+    lin(R("jc"), R("jc0"), 1.0, lcol)
 
     def both(o, v, k):
         tt(o, R("t2t", 32 * v + k, 256, st=32), R("t2t", 32 * v + 16 + k, 256, st=32), O.add)
@@ -437,67 +443,67 @@ def rank_program(g, core, T, topo):
     tt(R("z8"), R("cn"), R("ck"), O.add)
     red(R("nlv"), R("z8"), O.min, True)
     ts(R("kl", 0, 1), R("nlv"), 8192.0, R("ca", 4, 5), O.mult, O.min)
-    ts(R("own"), R("pm"), R("nlv"), None, O.add)
+    ts(R("own"), R("pm"), R("nlv"), 8192.0, O.add, O.mult)
     ts(R("nls"), R("nlv"), 8192.0, R("ca", 4, 5), O.mult, O.min)
-    ttg(R("same"), R("ids"), R("kl", 0, 1), R("own"), O.is_equal)
+    ttg(R("same"), R("idt"), R("kl", 0, 1), R("own"), O.is_equal)
     tt(R("ms9"), R("ms8"), al, O.mult)
     red(R("dup"), R("same"), O.max)
     tt(R("y8"), R("cn"), R("ms9"), O.add)
     ts(R("kd", 0, 1), R("dup"), R("ca", 4, 5), R("nls"), O.mult, O.max)
-    send([(q, R("kd"), R("kla", 2 * here[q], 2 * here[q] + 2)) for q in others], "ark")
+    spread(R("kd"), lambda q: R("kla", 2 * here[q], 2 * here[q] + 2), "ark")
 
     parts = [(ch, b) for ch in range(2) for b in range(4)]
+
+    def twice(t, w):
+        turn(R(t, 0, P), R(w, P * r + 32, P * r + 416))
+        turn(R(t, P), R(w, P * r + 16, P * r + 432))
+    red(R("slv"), R("y8"), O.min, True)
+    scatter(R("wo", 32), R("kd", 0, 1), R("ptv", 16 * r, 16 * r + 16))
+    ts(R("yv"), R("slv"), 0.5, 8192.0, O.is_lt, O.mult)
+    turn(R("tko", 0, P), R("wo", P * r + 32, P * r + 416))
+    tt(R("zz", 96, 97), R("slv"), R("yv"), O.mult)
+    turn(R("tko", P), R("wo", P * r + 16, P * r + 432))
+    turn(R("yr"), R("zz", 96, 128))
+    tt(R("wown"), R("tko", 0, 800, st=32), R("tko", 16, 800, st=32), O.min)
+    gather(R("yd"), R("yr"), R("hv"))
+    quant("eq", 0, 512, R("et"))
+    turn(R("ydt"), R("yd"))
     for ch, b in parts:
         mm(BANKS[4 * ch + b], CUT[ch][1] - CUT[ch][0], "eq", 128 * b, "vq", CUT[ch][0], CUT[ch][1], True, False)
-    scatter(R("wo"), R("kd", 0, 1), R("ptv", 16 * r, 16 * r + 16))
-    red(R("slv"), R("y8"), O.min, True)
-    ts(R("yv"), R("slv"), 0.5, 8192.0, O.is_lt, O.mult)
-    turn(R("tko"), R("wo", P * r, P * r + P))
-    tt(R("zz", 96, 97), R("slv"), R("yv"), O.mult)
-    turn(R("yr"), R("zz", 96, 128))
-    tt(R("wown"), R("tko", 0, P, st=32), R("tko", 16, P, st=32), O.min)
-    gather(R("yd"), R("yr"), R("hv"))
-    turn(R("ydt"), R("yd"))
     for a in range(4):
-        for b in range(4):
-            copy(R("ksl", 2 * a, 2 * a + 2, 32 * b, 32 * b + 32), R("ydt", 0, 64, 32 * a, 32 * a + 32, 32), "s")
+        copy(R("ksl", 2 * a, 2 * a + 2, 0, 32), R("ydt", 0, 64, 32 * a, 32 * a + 32, 32), "s")
+    for b in range(1, 4):
+        copy(R("ksl", 0, 8, 32 * b, 32 * b + 32), R("ksl", 0, 8, 0, 32), "s")
 
     note(None, [R("kla")], [], "ark", count["ark"])
     for k, q in reversed(list(enumerate(others))):
-        scatter(R("wk"), R("kla", 2 * k, 2 * k + 1), R("ptv", 16 * q, 16 * q + 16))
+        scatter(R("wk", 32), R("kla", 2 * k, 2 * k + 1), R("ptv", 16 * q, 16 * q + 16))
         if k == 2:
             ts(R("kt"), R("nlv"), 0.5, None, O.is_lt)
-        if k == 1:
             ts(R("kw"), R("nlv"), 8192.0, 1.0, O.mult, O.add)
+        if k == 1:
+            quant("xa", NOP, NOP + 128, R("xt", 128, 640))
     tt(R("kv"), R("kw"), R("kt"), O.mult)
-    turn(R("tk"), R("wk", P * r, P * r + P))
+    twice("tk", "wk")
     ts(R("zz", 64, 68), R("mk4"), R("kv"), None, O.mult)
-    tt(R("wa"), R("tk", 0, P, st=32), R("tk", 16, P, st=32), O.min)
+    tt(R("wa"), R("tk", 0, 800, st=32), R("tk", 16, 800, st=32), O.min)
     pick("kq", 0, 64, "uc", UW, R("ksl", 0, 4))
     tt(R("wb"), R("wa"), R("wown"), O.min)
     turn(R("kpt"), R("zz", 64, 96))
-    tt(R("wc", 0, 12, 0, 64), R("wb", 0, 12, 0, 64), R("wb", 0, 12, 64, 128), O.min)
+    tt(R("wc", 0, 25, 0, 64), R("wb", 0, 25, 0, 64), R("wb", 0, 25, 64, 128), O.min)
     for a in range(4):
-        tt(R("zz", 32, 44, 32 * a, 32 * a + 32), R("wc", 0, 12, 0, 32), R("wc", 0, 12, 32, 64), O.min)
-    turn(R("lr"), R("zz", 32, 64))
-    pick("kq", 64, 128, "uc", UW, R("ksl", 4, 8))
-    gather(R("ld"), R("lr"), R("hv"))
+        tt(R("zz", 32, 57, 32 * a, 32 * a + 32), R("wc", 0, 25, 0, 32), R("wc", 0, 25, 32, 64), O.min)
+    gather(R("ln"), R("zz", 32, 64), R("wr", 2, 4))
     tt(R("kp2"), R("kpt", 0, 32, st=2), R("kpt", 1, 32, st=2), O.add)
-    turn(R("ldt"), R("ld"))
-    tt(R("kp3"), R("kp2", 0, 16, st=2), R("kp2", 1, 16, st=2), O.add)
-    copy(R("ln", 0, 24, st=2), R("ldt", 0, 12))
-    copy(R("ln", 1, 24, st=2), R("ldt", 32, 44), "s")
-    ts(R("kpo"), R("kp3"), -1.0, None, O.add)
-    for a in range(4):
-        dma("y", T.kp[:, 8 * a:8 * a + 8], R("kpo", 0, 8, 32 * a, 32 * a + 4), "dk", 4)
+    ts(R("sl0"), R("ln", 0, 24), NOP - 0.5, float(P), O.is_lt, O.mult)
 
-    note(None, [R("xa" + s, 32 * q, 32 * q + 32) for q in others for s in ("", "s")], [], "arx", count["arx"])
+    note(None, [R("xa" + s, 32 * q + 96 * (q > r), 32 * q + 96 * (q > r) + 32) for q in others for s in ("", "s")], [], "arx", count["arx"])
     for a, b in CUT:
-        pick("qp", a, b, "xa", 160, R("ln", a // 16, b // 16))
+        pick("qp", a, b, "xa", NOP + 128, R("ln", a // 16, b // 16))
     for ch, b in parts:
         mm(BANKS[4 * ch + b], CUT[ch][1] - CUT[ch][0], "eq", 128 * b, "qp", CUT[ch][0], CUT[ch][1], False, True)
-    ts(R("sl0"), R("ln"), N * A - 0.5, float(P), O.is_lt, O.mult)
     tt(R("sl1"), R("sl0"), R("jc"), O.add)
+    tt(R("kp3"), R("kp2", 0, 16, st=2), R("kp2", 1, 16, st=2), O.add)
 
     def half(ch, bs):
         for b in bs:
@@ -512,12 +518,15 @@ def rank_program(g, core, T, topo):
         dma("y", T.oc[:, 4 * a:4 * b], R("oq", a, b), "do%d" % ch, 1)
         for k in range(4):
             dma("sy"[k % 2] if late else "y", T.osc[4 * k:4 * k + 4, a:b], R("oqs", a, b, 32 * k, 32 * k + 4), "dp%d" % ch, 4)
-    half(0, (0, 1))
+    half(0, (0, 1, 2, 3))
     copy(R("sl"), R("sl1"))
-    half(0, (2, 3))
-    mm(BANKS[0], 128, "wq", 0, "kq", 0, 128)
+    ts(R("kpo"), R("kp3"), -1.0, None, O.add)
+    for a in range(4):
+        dma("y", T.kp[:, 8 * a:8 * a + 8], R("kpo", 0, 8, 32 * a, 32 * a + 4), "dk", 4)
     new(0)
     half(1, (0, 2))
+    pick("kq", 64, 128, "uc", UW, R("ksl", 4, 8))
+    mm(BANKS[0], 128, "wq", 0, "kq", 0, 128)
     store(0, False)
     half(1, (1, 3))
     copy(R("yt"), R(BANKS[0], 0, 128), "s")

@@ -5,37 +5,38 @@ N, P, A, C, LC = 4, 384, 32, 16, 160
 UB = 32
 UR = UB + P
 UW = UR + 3 * LC
-MO = 3 * P
 DB = P
+MID = P // 2
 DUMP = N * P + 4
 IW = DUMP + 20
 NOP = 224
 CUT = ((0, 160), (160, 384))
+ORDER = "h00v s0 h02v s1 h01s s2 h03s n0 h10s h11s o0v h12s ym o0s ys h13v n1 o1v o1s"
 
 F32, BF, I32, U16, U8, F8 = "float32", "bfloat16", "int32", "uint16", "uint8", "float8_e4m3fn_x4"
 SCRATCH = {}
 for _d, _names in (
-    (BF, "tbt:1664 xt:640 wt:512 et:2048 nt:1536"),
+    (BF, "tbt:1664 xt:640 wt:512 et:528 nt:1536"),
     (F8, "vq:384 xq:128 wq:128 eq:512 xa:352 uc:896 pk:480 ex:512 kq:128 qp:384 mg:768 oq:384"),
     (U8, "vqs:384 xqs:128 wqs:128 eqs:512 xas:352 ucs:896 pks:480 exs:512 kqs:128 qps:384 mgs:768 oqs:384"),
-    (I32, "kci:64"), (U16, "bl:4 bo:8 br:4 pl:4 rl:24 hv:4 wr:6"), (BF, "ones:16 ptv:64"),
+    (I32, "kci:64"), (U16, "bl:4 bo:8 br:4 pl:4 rl:24 hv:4 wr:6 gl:6"), (BF, "ones:16 ptv:64"),
     (F32, "kcf:512 idt:1560 ab:516 cv:192 zz:128"),
-    (I32, "cdh:16 cdi:32"), (U16, "off:32 wl:12 lst:16 lnd:30"), (BF, "mk0:2688 mk1:2688 tm:768 m1:24"),
-    (F32, "req:192 x0:32 xt0:32 wn:1184 wnt:352"),
+    (I32, "cdh:4 cdi:32"), (U16, "off:8 wl:12 lst:16 lnd:30"), (BF, "mk:1536 tm:1152 m1:36 m2:36 wn:1184 wnt:352"),
+    (F32, "req:192 x0:32 xt0:32"),
     (F32, "cdp:32 zp:12 zrep:384 zf:416 gx:32 zr:512 zt:512 z2:32 sf:32 sc:16 nc:16 n1:24 nr:64 tie:64"), (U16, "og:32 sw:32 nl:4 kl:2"),
-    (F32, "cs:128 cg:512 ob:128 obt:128 gg:64 dw:64 w2:64 bb:64 rks:64 l2a:8 l2b:8 t1:128 t1t:128 t2:640 t2t:256 cu:64 tmp:64 alg:64"), (U16, "l1:4 l2:8"),
+    (F32, "cs:128 cg:512 ob:128 obt:128 gg:64 dw:64 w2:64 bb:64 rks:64 l2a:8 t1:144 t1t:128 t2:1024 t2t:256 tmp:64 alg:128"), (U16, "l1:4 l2:8"),
     (F32, "pr:160 kpt:32 yr:32 yd:64 ydt:64 yt:128"), (U16, "kd:2 ksl:8 kla:6"),
-    (BF, "wk:1600 wo:1600 tk:800 tko:800"), (F32, "wm:128 sl0:24 sl1:24"), (U16, "ln:32 sl:24"),
+    (BF, "wk:1600 tk:800"), (F32, "wm:128 sl0:24 sl1:24"), (U16, "ln:32 sl:24"),
 ):
     for _n in _names.split():
         SCRATCH[_n.split(":")[0]] = ("sbuf", [128, int(_n.split(":")[1])], _d)
 PART = {}
 for _d, _names in (
-    ("kcf", "pf:10 xr:10 cq:8 ca:12 t32:32 tri:32 dc0:12 dc:12 dc1:12 plc:12 c4:4 bo0:8 br0:4 br1:4 hv0:4 c2:8 jc0:24 jc:24 mk4:4 rst0:64 rst:64 pm0:16 pm:16 pt0:64 ce:1"),
+    ("kcf", "pf:10 xr:14 cq:8 ca:16 t32:32 tri:32 dc0:12 dc:12 dc1:12 plc:12 c4:4 bo0:8 br0:4 br1:4 hv0:4 c2:8 jc0:24 jc:24 mk4:4 rst0:64 rst:64 pm0:16 pm:16 pt0:64 ce:1 gl0:5"),
     ("kci", "ip:2 ib:4 it:10 ir:24"),
-    ("req", "mm:12 tot:1 base:1 sn:12 g1:12 g2:12 g3:12"),
-    ("pr", "nn:8 sl8:8 mk8:8 ms8:8 ms9:8 cn:8 ck:8 z8:8 y8:8 nlv:1 nls:1 slv:1 kt:1 kw:1 kv:1 yv:1 kp2:16 kp3:8 kpo:8 own:16 same:16 dup:1"),
-    ("wm", "wa:25 wb:25 wc:25 wown:25"),
+    ("req", "mm:12 base:1 sn:12 g1:12 g2:12 g3:12"),
+    ("pr", "mk8:8 ms8:8 ms9:8 cn:8 ck:8 z8:8 y8:8 nlv:1 nls:1 slv:1 kt:1 kw:1 kv:1 yv:1 kp2:16 kp3:8 kpo:8 own:16 same:16 dup:1 mk7:1 q7:1"),
+    ("wm", "wa:25 wc:25"),
 ):
     _c = 0
     for _n in _names.split():
@@ -165,10 +166,12 @@ def rank_program(g, core, T, topo):
     def scatter(win, off, i):
         op("v", lambda: g.vector.tensor_copy(win["ap"].indirect(off["ap"]), i["ap"]), [win], [off, i])
 
-    def pick(cn, o0, o1, wn, w1, off):
+    def pick(cn, o0, o1, wn, w1, off, who="vs"):
         o, w = R(cn, o0, o1), R(wn, 0, w1)
-        op("v", lambda: g.vector.tensor_copy(o["ap"].bitcast(dt.uint32), w["ap"].bitcast(dt.uint32).indirect(off["ap"])), [o], [w, off])
-        gather(R(cn + "s", o0, o1), R(wn + "s", 0, w1), off, "s")
+        if "v" in who:
+            op("v", lambda: g.vector.tensor_copy(o["ap"].bitcast(dt.uint32), w["ap"].bitcast(dt.uint32).indirect(off["ap"])), [o], [w, off])
+        if "s" in who:
+            gather(R(cn + "s", o0, o1), R(wn + "s", 0, w1), off, "s")
 
     def quant(cn, c0, c1, tile):
         o, s = R(cn, c0, c1), R(cn + "s", c0, c1)
@@ -184,18 +187,17 @@ def rank_program(g, core, T, topo):
         op("p", lambda: g.iota(o["ap"], pattern, base, cm, **kw), [o], [])
 
     others = [q for q in range(N) if q != r]
+    ring = [(r + 1 + i) % N for i in range(N - 1)]
     here = {q: (r if r < q else r - 1) for q in others}
 
-    def send(pieces, sem, turned=0):
+    def send(pieces, sem):
         need("p", [], [s for _q, s, _d in pieces])
-        parts = 1 if len(pieces) == 1 else 4
         tr = []
         for k, (q, s, d) in enumerate(pieces):
             e = topo.engines(core, T.cores[q])
-            m = len(e) // parts
-            k4 = (k + turned) % parts
+            m = len(e) // len(pieces)
             rid, pid, _s = topo.addr(T.cores[q])
-            tr.append(RemoteDMATransfer(dst_ids=[DstId(rid=rid, pnc=pid)], dma_engine_mask=sum(1 << n for n in e[k4 * m:k4 * m + m]),
+            tr.append(RemoteDMATransfer(dst_ids=[DstId(rid=rid, pnc=pid)], dma_engine_mask=sum(1 << n for n in e[k * m:k * m + m]),
                                         remote_sem=T.sem[sem], src=u8(s), dst=u8(d)))
             count["loc"] = count.get("loc", 0) + m
             count[sem] = count.get(sem, 0) + m
@@ -204,17 +206,17 @@ def rank_program(g, core, T, topo):
     def spread(s, dst, sem):
         need("p", [], [s])
         e = [n for n in topo.engines(core, T.cores[others[0]]) if all(n in topo.engines(core, T.cores[q]) for q in others)]
-        ids = [DstId(rid=topo.addr(T.cores[q])[0], pnc=topo.addr(T.cores[q])[1]) for q in others]
+        ids = [DstId(rid=topo.addr(T.cores[q])[0], pnc=topo.addr(T.cores[q])[1]) for q in ring]
         count["loc"] = count.get("loc", 0) + len(e)
         count[sem] = count.get(sem, 0) + len(e) * len(others)
         g.remote_dma_fused([RemoteDMATransfer(dst_ids=ids, dma_engine_mask=sum(1 << n for n in e), remote_sem=T.sem[sem],
-                                              srcs=[u8(s)], dsts=[u8(dst(q)) for q in others])], local_sem=T.sem.loc)
+                                              srcs=[u8(s)], dsts=[u8(dst(q)) for q in ring])], local_sem=T.sem.loc)
 
     def points(s):
         spread(R("xq" + s, 0, 32), lambda q: R("xa" + s, 32 * r + 96 * (r > q), 32 * r + 96 * (r > q) + 32), "arx")
 
     for k in range(8):
-        dma("ys"[k % 2], R("cdh", 0, 16, 16 * k, 16 * k + 16), T.cd[:, 16 * (k % 2):16 * (k % 2) + 16], "dch", 8)
+        dma("ys"[k % 2], R("cdh", 0, 4, 16 * k, 16 * k + 16), T.cd[:, 4 * k:4 * k + 4], "dch", 8)
     dma("y", R("xt", 0, 128), T.x[:, :], "dx", 1)
     dma("y", R("tbt", 128), T.tb[:, :], "dtb", 1)
     for k in range(8):
@@ -225,129 +227,147 @@ def rank_program(g, core, T, topo):
     iota("ip", [[1, 1]], 0, 1, 0, 1)
     iota("t32", [[1, 32]], 0, 0)
     iota("dc0", [[1, 12]], DB, 0)
-    iota("cv", [[32, 12], [1, 16]], 0, 0)
-    iota("idt", [[1, IQ]], 0, 0, 0, IQ)
-    memset(R("mk0", MO, MO + P), 0.0)
-    p = R("ip", 0, 1)
-    for k, (sh, msk) in enumerate(((0, 15), (4, 1), (0, 1), (4, 7), (0, 3), (5, 3), (0, 31), (1, 3), (1, 7))):
-        ts(R("it", k, k + 1), p, sh, msk, O.logical_shift_right, O.bitwise_and)
-    memset(R("mk1", MO, MO + P), 0.0)
-    copy(R("pf", 0, 9), R("it", 0, 9))
-    lcol, hcol, ecol, gcol, p3, acol, pcol, bcol, wcol = [R("pf", k, k + 1) for k in range(9)]
-    memset(R("ones"), 1.0)
-    ts(R("cq", 0, 1), acol, float(-P), float(MO), O.mult, O.add)
-    memset(R("xt", 128, 512), 0.0)
-    lin(R("ca", 0, 1), hcol, 16.0)
-    lin(R("ca", 6, 7), pcol, 12.0)
-    lin(R("dc"), R("dc0"), 1.0, R("ca", 6, 7))
-    lin(R("cv"), R("cv"), 1.0, R("ca", 0, 1))
-    lin(R("dc1"), R("dc"), 1.0, 1.0)
-    lin(R("wn", 16, 208), R("cv"), 0.0)
-    lin(R("zz"), R("cv", 0, 128), 0.0)
-    ts(R("off", 0, 32, st=2), R("cdh"), R("cq", 0, 1), None, O.add)
-    ts(R("tri"), R("t32"), pcol, None, O.is_gt)
-    ts(R("cq", 3, 4), acol, float(r), float(-LC), O.is_gt, O.mult)
-
-    for i in range(A // 2):
-        scatter(R("mk%d" % (i % 2)), R("off", 2 * i, 2 * i + 1), R("ones"))
-        if i == 5:
-            quant("xq", 0, 128, R("xt", 0, 512))
-            points("")
+    iota("cv", [[32, 12], [1, 16]], -MID, 0)
     iota("plc", [[32, 12]], UB - 32 * r, 1)
     iota("ir", [[1, 12], [0, 2]], 0, 0)
     iota("c4", [[1, 4]], 0, 0)
-    iota("ce", [[1, 1]], -3, -4)
-    iota("hv0", [[16, 2], [0, 2]], 0, 0)
-    for k in range(2):
-        turn(R("tm", P * k, P * k + P), R("mk%d" % k, MO, MO + P))
+    runs = [(a, b, c) for a, b, c in ((0, P * r, 0), (P * r + P, N * P, P * r)) if b > a]
+    for a, b, c in runs:
+        memset(R("mk", a, b), 0.0)
+    memset(R("ones"), 1.0)
+    p = R("ip", 0, 1)
+    for k, (sh, msk) in enumerate(((0, 15), (4, 1), (0, 1), (4, 7), (0, 3), (0, 7), (0, 31))):
+        ts(R("it", k, k + 1), p, sh, msk, O.logical_shift_right, O.bitwise_and)
+    lcol, hcol, ecol, gcol, p3, p7, pcol = [R("pf", k, k + 1) for k in range(7)]
+    memset(R("xt", 128, 512), 0.0)
+    copy(R("off", 0, 8, st=2), R("cdh"))
+    copy(R("pf", 0, 7), R("it", 0, 7))
+    memset(R("mm", 0, 12, 32 * r, 32 * r + 32), 0.0)
+    lin(R("ca", 0, 1), hcol, 16.0)
+    lin(R("ca", 6, 7), pcol, 12.0)
+    lin(R("wn", 16, 208), R("cv"), 0.0)
+    lin(R("dc"), R("dc0"), 1.0, R("ca", 6, 7))
+    lin(R("cv"), R("cv"), 1.0, R("ca", 0, 1))
+    lin(R("dc1"), R("dc"), -1.0, -1.0)
+    lin(R("zz"), R("cv", 0, 128), 0.0)
 
+    for i in range(4):
+        scatter(R("mk"), R("off", 2 * i, 2 * i + 1), R("ones"))
+        if i == 1:
+            quant("xq", 0, 128, R("xt", 0, 512))
+            points("")
+            iota("idt", [[1, IQ]], 0, 0, 0, IQ)
+        if i == 2:
+            ts(R("tri"), R("t32"), pcol, None, O.is_gt)
+            memset(R("zf", 400, 416), 0.0)
+    memset(R("zf", 0, 16), 0.0)
+    for a, b, c in runs:
+        turn(R("tm", c, c + b - a), R("mk", a, b))
+
+    wcol = R("xr", 10, 11)
+    lin(R("cq", 3, 4), hcol, -1.0, gcol)
+    lin(R("xr", 9, 10), ecol, -1.0, lcol)
     lin(R("xr", 0, 1), hcol, -1.0, ecol, AF.Abs)
     lin(R("xr", 1, 2), hcol, -1.0, 6.0)
     lin(R("xr", 2, 3), hcol, -1.0, 13.0)
-    lin(R("xr", 9, 10), ecol, -1.0, lcol)
+    lin(R("cq", 4, 5), R("cq", 3, 4), 1.0, -2.0 * r - 1.0, AF.Sign)
+    lin(wcol, R("xr", 9, 10), 0.5)
+    lin(R("xr", 7, 8), R("xr", 0, 1), 1.0, R("xr", 9, 10))
+    lin(R("xr", 11, 12), ecol, -1.0, p7)
+    lin(R("cq", 5, 6), R("cq", 4, 5), -LC / 2, UR - 1.0 - LC / 2)
     lin(R("xr", 3, 4), R("xr", 0, 1), R("xr", 1, 2), wcol)
     lin(R("xr", 5, 6), R("xr", 0, 1), R("xr", 2, 3), wcol)
-    lin(R("xr", 7, 8), R("xr", 0, 1), 1.0, R("xr", 9, 10))
-    lin(R("cq", 6, 7), R("cq", 3, 4), 1.0, float(UR - 1))
+    lin(R("xr", 8, 9), R("xr", 7, 8), 1.0, 16.0)
+    lin(R("ca", 1, 2), gcol, 4.0)
+    lin(R("cq", 2, 3), R("cq", 3, 4), LC / 2, R("cq", 5, 6))
+    lin(R("cq", 1, 2), R("cq", 3, 4), -P / 2, 16.0)
     lin(R("xr", 4, 5), R("xr", 3, 4))
     lin(R("xr", 6, 7), R("xr", 5, 6), 1.0, 8.0)
-    lin(R("xr", 8, 9), R("xr", 7, 8), 1.0, 16.0)
-    lin(R("cq", 2, 3), acol, float(LC), R("cq", 6, 7))
-    lin(R("cq", 1, 2), acol, float(-P), 16.0)
-    lin(R("ca", 1, 2), gcol, 4.0)
     for j in range(4):
         copy(R("cdp", 8 * j, 8 * j + 8), R("cdi", j, 32, st=4), "s")
     for k in range(1, 4):
         lin(R("idt", IQ * k, IQ * k + IQ), R("idt", 0, IQ), 1.0, float(IQ * k))
-    tt(R("m1"), R("tm", 0, 2 * P, st=32), R("tm", 16, 2 * P, st=32), O.max)
-    memset(R("zf", 400, 416), 0.0)
-    tt(R("mm"), R("m1", 0, 12), R("m1", 12, 24), O.max)
-    memset(R("zf", 0, 16), 0.0)
-    red(R("tot"), R("mm"), O.add)
+    tt(R("m1"), R("tm", 0, 3 * P, st=32), R("tm", 16, 3 * P, st=32), O.max)
+    memset(R("tbt", 0, 128), 0.0)
+    tt(R("m2", 0, 36, 0, 64), R("m1", 0, 36, 0, 64), R("m1", 0, 36, 64, 128), O.max)
+    for k, q in enumerate(others):
+        tt(R("mm", 0, 12, 32 * q, 32 * q + 32), R("m2", 12 * k, 12 * k + 12, 0, 32), R("m2", 12 * k, 12 * k + 12, 32, 64), O.max)
     scan(R("sn"), R("mm"), R("mm"), O.add, O.max)
-    ts(R("x0"), R("tri"), R("tot"), None, O.mult)
-    tt(R("g1"), R("sn"), R("dc1"), O.subtract)
+    tt(R("g1"), R("mm"), R("dc1"), O.mult)
+    ts(R("x0"), R("tri"), R("sn", 11, 12), None, O.mult)
+    tt(R("g2"), R("g1"), R("dc"), O.add)
     turn(R("xt0"), R("x0"))
-    tt(R("g2"), R("g1"), R("mm"), O.mult)
+    tt(R("g3"), R("g2"), R("sn"), O.add)
     red(R("base"), R("xt0"), O.add)
-    tt(R("g3"), R("g2"), R("dc"), O.add)
-    ts(R("wl"), R("g3"), R("base"), None, O.add)
     copy(R("wr"), R("xr", 3, 9))
-    scatter(R("wn", 32), R("wl"), R("cv"))
+    copy(R("rl"), R("ir"))
+    ts(R("wl"), R("g3"), R("base"), None, O.add)
     ts(R("zp"), R("sn"), R("base"), R("cq", 2, 3), O.add, O.add)
+    scatter(R("wn", 32), R("wl"), R("cv"))
+    copy(R("zp", 0, 12, 32 * r, 32 * r + 32), R("plc", 0, 12, 32 * r, 32 * r + 32))
     turn(R("wnt", 0, LC), R("wn", 32, 192))
     turn(R("wnt", LC), R("wn", 16, 208))
-    copy(R("zp", 0, 12, 32 * r, 32 * r + 32), R("plc", 0, 12, 32 * r, 32 * r + 32))
+    ts(R("gx"), R("cdp"), R("cq", 1, 2), 15.0, O.add, O.max, R("wr", 4, 6))
     tt(R("zz", 0, 11), R("wnt", 0, 352, st=32), R("wnt", 16, 352, st=32), O.add)
-    copy(R("rl"), R("ir"))
-    gather(R("lst"), R("zz", 0, 16), R("wr", 0, 1))
+    ts(R("pl", 0, 1), R("xr", 11, 12), 4.0, gcol, O.mult, O.add)
+    ts(R("og"), R("gx"), 400.0, None, O.min)
+    ts(R("lst"), R("zz", 0, 16), float(MID), None, O.add, None, R("wr", 0, 1))
     spread(R("lst", 0, 10), lambda q: R("lnd", 10 * here[q], 10 * here[q] + 10), "arl")
 
     gather(R("zrep"), R("zp"), R("rl"), "s")
     iota("br0", [[32, 4]], 0, 0)
-    iota("rst0", [[32, 4], [0, 16]], 0, 0)
+    iota("rst0", [[32, 4], [0, 16]], 2, 0)
     iota("pm0", [[4, 4], [0, 4]], 3, 0)
     iota("ib", [[128, 4]], 0, 1)
     iota("bo0", [[33, 4], [0, 2]], 0, 0)
-    iota("jc0", [[16, 24]], 0, 0)
-    ts(R("gx"), R("cdp"), R("cq", 1, 2), 15.0, O.add, O.max, R("wr", 4, 6))
-    ts(R("pl", 0, 1), bcol, 8.0, gcol, O.mult, O.add)
+    iota("ce", [[1, 1]], -3, -4)
     quant("vq", 0, P, R("tbt", 128))
-    ts(R("og"), R("gx"), 400.0, None, O.min)
     turn(R("zf", 16, 400), R("zrep"))
-    memset(R("tbt", 0, 128), 0.0)
     gather(R("nc"), R("cdp"), R("pl", 0, 1))
+    quant("uc", 0, UR, R("tbt"))
     gather(R("zr", 0, 256), R("zf"), R("og", 0, 16), "s")
 
     note(None, [R("lnd", 0, 30)], [], "arl", count["arl"])
     for a in others:
         copy(R("lnd", 0, 30, 32 * a, 32 * a + 32), R("lnd", 0, 30, 32 * r, 32 * r + 32))
-    for k, q in enumerate(others):
-        pick("pk", LC * k, LC * k + LC, "vq", P, R("lnd", 10 * k, 10 * k + 10))
-        send([(q, R("pk", LC * k, LC * k + LC), R("uc", UR + LC * here[q], UR + LC * here[q] + LC))], "arc")
-    send([(q, R("pks", LC * k, LC * k + LC), R("ucs", UR + LC * here[q], UR + LC * here[q] + LC)) for k, q in enumerate(others)], "arc", 3)
 
-    iota("t1", [[0, 128]], 0, 0)
+    def piece(s, k):
+        q = others[k]
+        return (q, R("pk" + s, LC * k, LC * k + LC), R("uc" + s, UR + LC * here[q], UR + LC * here[q] + LC))
+    ks = [others.index(q) for q in ring]
+    for i, k in enumerate(ks):
+        pick("pk", LC * k, LC * k + LC, "vq", P, R("lnd", 10 * k, 10 * k + 10))
+        send([piece("", k)], "arc")
+        if i:
+            send([piece("s", ks[0]), piece("s", ks[1])] if i == 1 else [piece("s", k)], "arc")
+
+    iota("t1", [[0, 144]], 0, 0)
+    iota("gl0", [[2, 3]], 3, 0, 0, 3)
+    iota("gl0", [[1, 2]], 0, 0, 3, 5)
+    points("s")
     iota("t2", [[0, 256]], 0, 0, 0, 256)
+    iota("hv0", [[16, 2], [0, 2]], 0, 0)
+    iota("jc0", [[16, 24]], 0, 0)
     iota("pt0", [[A, r + 1], [1, 4], [0, 4]], 0, 0, 0, 16 * r + 16)
     if r < N - 1:
         iota("pt0", [[A, N - 1 - r], [1, 4], [0, 4]], A * r + 128, 0, 16 * r + 16, 64)
-    points("s")
-    for n in ("wk", "wo"):
-        iota(n, [[0, 416]], NOP, 0, P * r + 16, P * r + 432)
+    iota("wk", [[0, 416]], NOP, 0, P * r + 16, P * r + 432)
     gather(R("zr", 256, 512), R("zf"), R("og", 16, 32), "s")
     for j in range(4):
         lin(R("gg", 16 * j, 16 * j + 16), R("t32", 0, 16), 0.0, R("nc", 2 * j, 2 * j + 1))
     lin(R("br1"), R("br0"), 1.0, R("ca", 0, 1))
     lin(R("rst"), R("rst0"), 1.0, R("ca", 0, 1))
     lin(R("n1", 8, 16), R("nc", 0, 8), 1.0 / 8192)
-    lin(R("ca", 2, 3), hcol, -1.0, 1.0)
-    lin(R("ca", 3, 4), hcol, 32.0)
-    lin(R("ca", 5, 6), hcol, -32.0, 32.0)
-    lin(R("ca", 7, 8), hcol, 1052.0, -1020.0)
-    lin(R("ca", 9, 10), hcol, -1052.0, 32.0)
-    lin(R("ca", 10, 11), hcol, 512.0)
-    lin(R("ca", 11, 12), hcol, -1024.0, 528.0)
+    lin(R("ca", 2, 3), hcol, 16.0, -64.0)
+    lin(R("ca", 3, 4), hcol, -1008.0, 448.0)
+    lin(R("c2", 0, 4), R("c4"), 31.875)
+    lin(R("ca", 12, 13), p7, 31.875, R("ca", 0, 1))
+    lin(R("ca", 4, 5), lcol, 1.0, float(DUMP))
+    lin(R("ca", 8, 9), p3, -1.0, -1.0)
+    lin(R("ca", 14, 15), p3, -1.0)
+    lin(R("ca", 13, 14), lcol, 0.125, R("ca", 12, 13))
+    lin(R("ab"), R("idt", 0, 516), 1.0, R("ce"), AF.Abs)
+    lin(R("et", 0, 516), R("ab"), -0.5, 0.5, AF.Relu)
 
     turn(R("zt", 0, 256), R("zr", 0, 256))
     copy(R("nl"), R("nc", 0, 8, st=2))
@@ -360,10 +380,12 @@ def rank_program(g, core, T, topo):
     for a in range(4):
         tt(R("sf", 0, 32, 32 * a, 32 * a + 32), R("z2", 0, 32, 0, 32), R("z2", 0, 32, 32, 64), O.add)
     gather(R("sw"), R("sf"), R("wr", 4, 6))
-    quant("uc", 0, UR, R("tbt"))
+    quant("xa", NOP, NOP + 128, R("xt", 128, 640))
     gather(R("sc"), R("sf"), R("pl", 2, 3))
     ttg(R("nr"), R("idt"), R("nl"), R("gg"), O.is_lt)
     copy(R("bl"), R("ib"))
+    ts(R("t1", 1, 128, st=16), R("sc", 0, 8), 1.0 / 8192, None, O.mult)
+    copy(R("t1", 0, 128, st=16), R("n1", 8, 16))
     ts(R("bo"), R("bo0"), R("ca", 1, 2), None, O.add)
     ts(R("br"), R("br1"), lcol, None, O.add)
     ts(R("tie"), R("nr"), -2.0 ** -100, None, O.mult)
@@ -375,164 +397,162 @@ def rank_program(g, core, T, topo):
         mm(BANKS[4 * w + j], 128, "ex", 128 * j, "xq" if w else "ex", 0 if w else 128 * j, 128 if w else 128 * j + 128)
         if w:
             copy(R("cs", 32 * j, 32 * j + 32), R(BANKS[4 + j], 0, 32))
+            if j == 2:
+                gather(R("ob", 0, 64), R("cs", 0, 64), R("bo", 0, 4))
         else:
             copy(R("cg", 128 * j, 128 * j + 128), R(BANKS[j], 0, 128), "s")
-    lin(R("cq", 4, 5), lcol, hcol, R("ca", 10, 11))
-    lin(R("cq", 5, 6), lcol, R("ca", 2, 3), R("ca", 11, 12))
-    lin(R("c2", 0, 8, st=2), R("c4"), R("ca", 7, 8), R("cq", 4, 5))
-    lin(R("c2", 1, 8, st=2), R("c4"), R("ca", 9, 10), R("cq", 5, 6))
-    lin(R("ca", 4, 5), lcol, 1.0, float(DUMP))
-    lin(R("ca", 8, 9), p3, -1.0, -1.0)
-    gather(R("ob"), R("cs"), R("bo"))
+    turn(R("obt", 0, 64), R("ob", 0, 64))
+    gather(R("ob", 64, 128), R("cs"), R("bo", 4, 8))
     own = R("ob", 0, 128, st=2)
     need("y", [], [R("ob")])
     for s in ("", "s"):
         dma("y", R("mg" + s, 0, P), R("vq" + s), "dmg", 2)
-    ts(R("n1", 16, 24), R("sc", 0, 8), 1.0 / 8192, None, O.mult)
-    turn(R("obt"), R("ob"))
+    memset(R("cn", 0, 1), 1.0)
+    ts(R("mk4"), R("c4"), p3, None, O.is_equal)
+    turn(R("obt", 64, 128), R("ob", 64, 128))
     ttg(R("bb"), R("cg"), R("bl"), own, O.is_lt)
     ttg(R("dw"), R("obt"), R("br"), own, O.subtract)
-    memset(R("kd"), 0.0)
+    ts(R("pm"), R("pm0"), lcol, 4096.0, O.is_ge, O.mult)
+    ts(R("hv"), R("hv0"), lcol, None, O.add)
     tt(R("w2"), R("dw"), R("tie"), O.is_gt)
-    memset(R("alg", 0, 1), 1.0)
+    quant("eq", 0, 128, R("et", 3, 515))
     scan(R("rks"), R("rst"), R("w2"), O.max, O.add)
-    ts(R("mk4"), R("c4"), p3, None, O.is_equal)
+    quant("eq", 128, 256, R("et", 2, 514))
     rank = R("rks", 15, 64, st=16)
     copy(R("l1"), rank)
-    ts(R("l2a", 0, 8, st=2), rank, R("ca", 5, 6), None, O.mult)
-    ts(R("l2a", 1, 8, st=2), rank, R("ca", 3, 4), None, O.mult)
+    tt(R("l2a", 0, 4), rank, R("c2", 0, 4), O.subtract)
+    memset(R("kd"), 0.0)
     scatter(R("t1"), R("l1"), R("bb"))
-    tt(R("l2b"), R("l2a"), R("c2"), O.add)
-    copy(R("t1", 15, 128, st=16), R("n1", 8, 16))
-    copy(R("t1", 14, 128, st=16), R("n1", 16, 24))
-    copy(R("l2"), R("l2b"))
-    turn(R("t1t"), R("t1"))
-    ts(R("pm"), R("pm0"), lcol, 4096.0, O.is_ge, O.mult)
+    for k in range(2):
+        ts(R("l2", k, 8, st=2), R("l2a", 0, 4), 32.0, R("ca", 2 + k, 3 + k), O.mult, O.add)
+    turn(R("t1t"), R("t1", 0, 128))
+    ts(R("gl", 0, 5), R("gl0"), R("ca", 13, 14), None, O.add)
     scatter(R("t2"), R("l2"), R("t1t"))
-    ts(R("hv"), R("hv0"), lcol, None, O.add)
+    quant("eq", 256, 384, R("et", 1, 513))
     for k in range(1, 4):
         copy(R("t2", k, 256, st=4), R("t2", 0, 256, st=4))
+    quant("eq", 384, 512, R("et", 0, 512))
     turn(R("t2t"), R("t2", 0, 256))
-    lin(R("ab"), R("idt", 0, 516), 1.0, R("ce"), AF.Abs)
-    for b in range(4):
-        lin(R("et", 512 * b, 512 * b + 512), R("ab", 3 - b, 515 - b), -0.5, 0.5, AF.Relu)
     lin(R("ptv"), R("pt0"), 1.0, R("ca", 1, 2))
     lin(R("jc"), R("jc0"), 1.0, lcol)
+    parts = [(ch, b) for ch in range(2) for b in range(4)]
+    for ch, b in parts:
+        mm(BANKS[4 * ch + b], CUT[ch][1] - CUT[ch][0], "eq", 128 * b, "vq", CUT[ch][0], CUT[ch][1], True, False)
 
-    def both(o, v, k):
-        tt(o, R("t2t", 32 * v + k, 256, st=32), R("t2t", 32 * v + 16 + k, 256, st=32), O.add)
-    both(R("alg", 9, 16), 1, 0)
-    both(R("cu", 8, 14), 2, 1)
-    ts(R("tmp", 10, 16), R("cu", 8, 14), R("alg", 9, 10), None, O.is_ge)
-    both(R("cu", 16, 21), 3, 2)
-    both(R("nn"), 0, 15)
-    for u in range(2, 8):
-        if u < 7:
-            ts(R("tmp", 9 * u + 1, 8 * u + 8), R("cu", 8 * u, 8 * u + 7 - u), R("alg", 9 * u - 8, 9 * u - 7), R("tmp", 9 * u - 8, 9 * u - 7), O.is_ge, O.is_ge)
-        tt(R("alg", 9 * u, 8 * u + 8), R("alg", 9 * u - 8, 8 * u), R("tmp", 9 * u - 8, 8 * u), O.min)
-        if u < 6:
-            both(R("cu", 8 * u + 8, 8 * u + 14 - u), u + 2, u + 1)
-        if u == 2:
-            ts(R("mk8"), R("nn"), R("ca", 8, 9), None, O.add)
+    gather(R("alg", 0, 80), R("t2t"), R("gl", 0, 5))
+    nn, sl8 = R("alg", 48, 56), R("alg", 56, 64)
+
+    def left(u, v, w=None):
+        return R("alg", 64 + 8 * u + v, 64 + 8 * u + (v + 1 if w is None else w))
+
+    def step(u, v, w=None):
+        return R("tmp", 8 * u + v, 8 * u + (v + 1 if w is None else w))
+
+    def cn(u):
+        return R("cn", u, u + 1)
+    ts(step(1, 2, 8), R("alg", 2, 8), left(1, 1), None, O.is_ge)
+    ts(R("mk8"), nn, R("ca", 8, 9), None, O.add)
+    memset(left(0, 0), 1.0)
+    lin(cn(1), left(1, 1), 1.0, 1.0)
+    lin(R("mk7"), R("alg", 55, 56), 1.0, R("ca", 14, 15))
+    for u in range(2, 7):
+        ts(step(u, u + 1, 8), R("alg", 9 * u - 7, 8 * u), left(u - 1, u), step(u - 1, u), O.is_ge, O.is_ge)
         if u == 6:
-            both(R("sl8"), 0, 14)
-    al = R("alg", 0, 64, st=9)
-    scan(R("cn"), al, al, O.add, O.max)
-    tt(R("ck"), R("mk8"), al, O.mult)
-    ts(R("ms8"), R("sl8"), R("ca", 8, 9), None, O.add)
-    tt(R("z8"), R("cn"), R("ck"), O.add)
+            ts(R("q7"), R("mk7"), left(5, 7), step(5, 7), O.mult, O.mult)
+        tt(left(u, u, 8), left(u - 1, u, 8), step(u - 1, u, 8), O.min)
+        lin(cn(u), left(u - 1, u), step(u - 1, u), cn(u - 1))
+    al = R("alg", 64, 128, st=9)
+    tt(R("ck", 0, 6), R("mk8", 0, 6), R("alg", 64, 110, st=9), O.mult)
+    ts(R("z8", 7, 8), R("q7"), step(6, 7), cn(6), O.mult, O.add)
+    ts(R("z8", 6, 7), R("mk8", 6, 7), left(6, 6), cn(6), O.mult, O.add)
+    tt(R("z8", 0, 6), R("cn", 0, 6), R("ck", 0, 6), O.add)
+    tt(left(7, 7), left(6, 7), step(6, 7), O.min)
+    lin(cn(7), left(6, 7), step(6, 7), cn(6))
+    ts(R("ms8"), sl8, R("ca", 8, 9), None, O.add)
     red(R("nlv"), R("z8"), O.min, True)
+    tt(R("ms9"), R("ms8"), al, O.mult)
     ts(R("kl", 0, 1), R("nlv"), 8192.0, R("ca", 4, 5), O.mult, O.min)
     ts(R("own"), R("pm"), R("nlv"), 8192.0, O.add, O.mult)
     ts(R("nls"), R("nlv"), 8192.0, R("ca", 4, 5), O.mult, O.min)
     ttg(R("same"), R("idt"), R("kl", 0, 1), R("own"), O.is_equal)
-    tt(R("ms9"), R("ms8"), al, O.mult)
-    red(R("dup"), R("same"), O.max)
     tt(R("y8"), R("cn"), R("ms9"), O.add)
+    ts(R("kt"), R("nlv"), 0.5, None, O.is_lt)
+    red(R("dup"), R("same"), O.max)
+    red(R("slv"), R("y8"), O.min, True)
+    ts(R("kw"), R("nlv"), 8192.0, 1.0, O.mult, O.add)
     ts(R("kd", 0, 1), R("dup"), R("ca", 4, 5), R("nls"), O.mult, O.max)
     spread(R("kd"), lambda q: R("kla", 2 * here[q], 2 * here[q] + 2), "ark")
 
-    parts = [(ch, b) for ch in range(2) for b in range(4)]
-
-    def twice(t, w):
-        turn(R(t, 0, P), R(w, P * r + 32, P * r + 416))
-        turn(R(t, P), R(w, P * r + 16, P * r + 432))
-    red(R("slv"), R("y8"), O.min, True)
-    scatter(R("wo", 32), R("kd", 0, 1), R("ptv", 16 * r, 16 * r + 16))
     ts(R("yv"), R("slv"), 0.5, 8192.0, O.is_lt, O.mult)
-    turn(R("tko", 0, P), R("wo", P * r + 32, P * r + 416))
+    tt(R("kv"), R("kw"), R("kt"), O.mult)
     tt(R("zz", 96, 97), R("slv"), R("yv"), O.mult)
-    turn(R("tko", P), R("wo", P * r + 16, P * r + 432))
+    ts(R("zz", 64, 68), R("mk4"), R("kv"), None, O.mult)
     turn(R("yr"), R("zz", 96, 128))
-    tt(R("wown"), R("tko", 0, 800, st=32), R("tko", 16, 800, st=32), O.min)
+    turn(R("kpt"), R("zz", 64, 96))
     gather(R("yd"), R("yr"), R("hv"))
-    quant("eq", 0, 512, R("et"))
+    tt(R("kp2"), R("kpt", 0, 32, st=2), R("kpt", 1, 32, st=2), O.add)
     turn(R("ydt"), R("yd"))
-    for ch, b in parts:
-        mm(BANKS[4 * ch + b], CUT[ch][1] - CUT[ch][0], "eq", 128 * b, "vq", CUT[ch][0], CUT[ch][1], True, False)
+    tt(R("kp3"), R("kp2", 0, 16, st=2), R("kp2", 1, 16, st=2), O.add)
     for a in range(4):
         copy(R("ksl", 2 * a, 2 * a + 2, 0, 32), R("ydt", 0, 64, 32 * a, 32 * a + 32, 32), "s")
     for b in range(1, 4):
         copy(R("ksl", 0, 8, 32 * b, 32 * b + 32), R("ksl", 0, 8, 0, 32), "s")
+    ts(R("kpo"), R("kp3"), -1.0, None, O.add)
+    for a in range(4):
+        dma("y", T.kp[:, 8 * a:8 * a + 8], R("kpo", 0, 8, 32 * a, 32 * a + 4), "dk", 4)
 
     note(None, [R("kla")], [], "ark", count["ark"])
-    for k, q in reversed(list(enumerate(others))):
-        scatter(R("wk", 32), R("kla", 2 * k, 2 * k + 1), R("ptv", 16 * q, 16 * q + 16))
-        if k == 2:
-            ts(R("kt"), R("nlv"), 0.5, None, O.is_lt)
-            ts(R("kw"), R("nlv"), 8192.0, 1.0, O.mult, O.add)
-        if k == 1:
-            quant("xa", NOP, NOP + 128, R("xt", 128, 640))
-    tt(R("kv"), R("kw"), R("kt"), O.mult)
-    twice("tk", "wk")
-    ts(R("zz", 64, 68), R("mk4"), R("kv"), None, O.mult)
+    for q in reversed(range(N)):
+        k = q - (q > r)
+        scatter(R("wk", 32), R("kd", 0, 1) if q == r else R("kla", 2 * k, 2 * k + 1), R("ptv", 16 * q, 16 * q + 16))
+        if q in (1, 2):
+            pick("kq", 64 * (2 - q), 64 * (3 - q), "uc", UW, R("ksl", 4 * (2 - q), 4 * (3 - q)))
+    turn(R("tk", 0, P), R("wk", P * r + 32, P * r + 416))
+    turn(R("tk", P), R("wk", P * r + 16, P * r + 432))
     tt(R("wa"), R("tk", 0, 800, st=32), R("tk", 16, 800, st=32), O.min)
-    pick("kq", 0, 64, "uc", UW, R("ksl", 0, 4))
-    tt(R("wb"), R("wa"), R("wown"), O.min)
-    turn(R("kpt"), R("zz", 64, 96))
-    tt(R("wc", 0, 25, 0, 64), R("wb", 0, 25, 0, 64), R("wb", 0, 25, 64, 128), O.min)
+    tt(R("wc", 0, 25, 0, 64), R("wa", 0, 25, 0, 64), R("wa", 0, 25, 64, 128), O.min)
     for a in range(4):
         tt(R("zz", 32, 57, 32 * a, 32 * a + 32), R("wc", 0, 25, 0, 32), R("wc", 0, 25, 32, 64), O.min)
     gather(R("ln"), R("zz", 32, 64), R("wr", 2, 4))
-    tt(R("kp2"), R("kpt", 0, 32, st=2), R("kpt", 1, 32, st=2), O.add)
-    ts(R("sl0"), R("ln", 0, 24), NOP - 0.5, float(P), O.is_lt, O.mult)
 
     note(None, [R("xa" + s, 32 * q + 96 * (q > r), 32 * q + 96 * (q > r) + 32) for q in others for s in ("", "s")], [], "arx", count["arx"])
     for a, b in CUT:
         pick("qp", a, b, "xa", NOP + 128, R("ln", a // 16, b // 16))
     for ch, b in parts:
         mm(BANKS[4 * ch + b], CUT[ch][1] - CUT[ch][0], "eq", 128 * b, "qp", CUT[ch][0], CUT[ch][1], False, True)
-    tt(R("sl1"), R("sl0"), R("jc"), O.add)
-    tt(R("kp3"), R("kp2", 0, 16, st=2), R("kp2", 1, 16, st=2), O.add)
 
-    def half(ch, bs):
-        for b in bs:
-            copy(R("nt", 4 * CUT[ch][0] + b, 4 * CUT[ch][1], st=4), R(BANKS[4 * ch + b], 0, CUT[ch][1] - CUT[ch][0]), "sv"[b % 2])
+    def half(ch, b, q):
+        copy(R("nt", 4 * CUT[ch][0] + b, 4 * CUT[ch][1], st=4), R(BANKS[4 * ch + b], 0, CUT[ch][1] - CUT[ch][0]), q)
 
     def new(ch):
         quant("mg", P + CUT[ch][0], P + CUT[ch][1], R("nt", 4 * CUT[ch][0], 4 * CUT[ch][1]))
 
-    def store(ch, late):
+    def store(ch, who):
         a, b = CUT[ch]
-        pick("oq", a, b, "mg", 2 * P, R("sl", a // 16, b // 16))
-        dma("y", T.oc[:, 4 * a:4 * b], R("oq", a, b), "do%d" % ch, 1)
-        for k in range(4):
-            dma("sy"[k % 2] if late else "y", T.osc[4 * k:4 * k + 4, a:b], R("oqs", a, b, 32 * k, 32 * k + 4), "dp%d" % ch, 4)
-    half(0, (0, 1, 2, 3))
-    copy(R("sl"), R("sl1"))
-    ts(R("kpo"), R("kp3"), -1.0, None, O.add)
-    for a in range(4):
-        dma("y", T.kp[:, 8 * a:8 * a + 8], R("kpo", 0, 8, 32 * a, 32 * a + 4), "dk", 4)
-    new(0)
-    half(1, (0, 2))
-    pick("kq", 64, 128, "uc", UW, R("ksl", 4, 8))
-    mm(BANKS[0], 128, "wq", 0, "kq", 0, 128)
-    store(0, False)
-    half(1, (1, 3))
-    copy(R("yt"), R(BANKS[0], 0, 128), "s")
-    dma("y", T.y[:, :], R("yt"), "dy", 1)
-    new(1)
-    store(1, True)
+        pick("oq", a, b, "mg", 2 * P, R("sl", a // 16, b // 16), who)
+        if who == "v":
+            dma("y", T.oc[:, 4 * a:4 * b], R("oq", a, b), "do%d" % ch, 1)
+        else:
+            for k in range(4):
+                dma("sy"[k % 2] if ch else "y", T.osc[4 * k:4 * k + 4, a:b], R("oqs", a, b, 32 * k, 32 * k + 4), "dp%d" % ch, 4)
+    for w in ORDER.split():
+        if w[0] == "h":
+            half(int(w[1]), int(w[2]), w[3])
+        elif w[0] == "n":
+            new(int(w[1]))
+        elif w[0] == "o":
+            store(int(w[1]), w[2])
+        elif w == "s0":
+            ts(R("sl0"), R("ln", 0, 24), NOP - 0.5, float(P), O.is_lt, O.mult)
+        elif w == "s1":
+            tt(R("sl1"), R("sl0"), R("jc"), O.add)
+        elif w == "s2":
+            copy(R("sl"), R("sl1"))
+        elif w == "ym":
+            mm(BANKS[0], 128, "wq", 0, "kq", 0, 128)
+        elif w[0] == "y":
+            copy(R("yt"), R(BANKS[0], 0, 128), w[1])
+            dma("y", T.y[:, :], R("yt"), "dy", 1)
 
     for s in sorted(count):
         g.wait_ge(T.sem[s], count[s])

@@ -7,11 +7,14 @@ UR = UB + P
 UW = UR + 3 * LC
 DB = P
 MID = P // 2
-DUMP = N * P + 4
+NB = 16
+DUMP = N * P + 4 + NB
 IW = DUMP + 20
 NOP = 224
-CUT = ((0, 160), (160, 384))
-ORDER = "h00v s0 h02v s1 h01s s2 h03s n0 h10s h11s o0v h12s ym o0s ys h13v n1 o1v o1s"
+ZB = 3 * UR + 3 * LC + UB + MID
+LS = (0, 16, 26)
+CUT = ((0, 192), (192, 384))
+ORDER = "s1 h00s h01v s2 h02s h03v h10v n0 h11s h12v o0v h13s o0s n1 o1v o1s"
 
 F32, BF, I32, U16, U8, F8 = "float32", "bfloat16", "int32", "uint16", "uint8", "float8_e4m3fn_x4"
 SCRATCH = {}
@@ -19,23 +22,23 @@ for _d, _names in (
     (BF, "tbt:1664 xt:640 wt:512 et:528 nt:1536"),
     (F8, "vq:384 xq:128 wq:128 eq:512 xa:352 uc:896 pk:480 ex:512 kq:128 qp:384 mg:768 oq:384"),
     (U8, "vqs:384 xqs:128 wqs:128 eqs:512 xas:352 ucs:896 pks:480 exs:512 kqs:128 qps:384 mgs:768 oqs:384"),
-    (I32, "kci:64"), (U16, "bl:4 bo:8 br:4 pl:4 rl:24 hv:4 wr:6 gl:6"), (BF, "ones:16 ptv:64"),
-    (F32, "kcf:512 idt:1560 ab:516 cv:192 zz:128"),
-    (I32, "cdh:4 cdi:32"), (U16, "off:8 wl:12 lst:16 lnd:30"), (BF, "mk:1536 tm:1152 m1:36 m2:36 wn:1184 wnt:352"),
+    (I32, "kci:64"), (U16, "bl:4 bo:8 br:4 pl:4 rl:24 hv:4 wr:6 gl:8"), (BF, "ones:16 ptv:64"),
+    (F32, "kcf:576 idt:1576 cv:192 zz:128"),
+    (I32, "cdh:4 cdi:32"), (U16, "off:8 wl:12 lst:16 lnd:48"), (BF, "mk:1536 tm:1152 m1:36 m2:36 wn:1184 wnt:352 zrep:384 zf:416 zr:512 zt:512"),
     (F32, "req:192 x0:32 xt0:32"),
-    (F32, "cdp:32 zp:12 zrep:384 zf:416 gx:32 zr:512 zt:512 z2:32 sf:32 sc:16 nc:16 n1:24 nr:64 tie:64"), (U16, "og:32 sw:32 nl:4 kl:2"),
-    (F32, "cs:128 cg:512 ob:128 obt:128 gg:64 dw:64 w2:64 bb:64 rks:64 l2a:8 t1:144 t1t:128 t2:1024 t2t:256 tmp:64 alg:128"), (U16, "l1:4 l2:8"),
-    (F32, "pr:160 kpt:32 yr:32 yd:64 ydt:64 yt:128"), (U16, "kd:2 ksl:8 kla:6"),
-    (BF, "wk:1600 tk:800"), (F32, "wm:128 sl0:24 sl1:24"), (U16, "ln:32 sl:24"),
+    (F32, "cdp:32 zp:12 gx:32 z2:32 sf:32 sc:16 nc:16 n1:24 tie:64"), (U16, "og:32 sw:32 nl:8 kl:2"),
+    (F32, "cs:128 cg:512 ob:128 obt:128 dw:64 w2:64 bb:64 rks:64 l2a:8 alg:144"), (BF, "t1:144 t1t:128 t2:1024 t2t:256"), (U16, "l1:4 l2:8"),
+    (F32, "pr:208 kpt:32 yr:32 yd:64 ydt:64 yt:128 al:64"), (U16, "kd:2 ksl:8 kla:6"),
+    (BF, "wk:1616 tk:800"), (F32, "wm:128 sl0:32 sl1:24"), (U16, "ln:32 sl:24"),
 ):
     for _n in _names.split():
         SCRATCH[_n.split(":")[0]] = ("sbuf", [128, int(_n.split(":")[1])], _d)
 PART = {}
 for _d, _names in (
-    ("kcf", "pf:10 xr:14 cq:8 ca:16 t32:32 tri:32 dc0:12 dc:12 dc1:12 plc:12 c4:4 bo0:8 br0:4 br1:4 hv0:4 c2:8 jc0:24 jc:24 mk4:4 rst0:64 rst:64 pm0:16 pm:16 pt0:64 ce:1 gl0:5"),
+    ("kcf", "pf:10 xr:14 cq:8 ca:16 t32:44 tri:32 one:44 dc0:12 dc1:12 c4:4 bo0:8 br0:4 hv0:4 c2:8 jc0:24 jc:24 mk4:4 rst0:64 pm0:16 pm:16 pt0:64 gl0:7"),
     ("kci", "ip:2 ib:4 it:10 ir:24"),
-    ("req", "mm:12 base:1 sn:12 g1:12 g2:12 g3:12"),
-    ("pr", "mk8:8 ms8:8 ms9:8 cn:8 ck:8 z8:8 y8:8 nlv:1 nls:1 slv:1 kt:1 kw:1 kv:1 yv:1 kp2:16 kp3:8 kpo:8 own:16 same:16 dup:1 mk7:1 q7:1"),
+    ("req", "mm:44 sn:44 g1:12 g3:12"),
+    ("pr", "mk8:56 ms8:8 ms9:8 cn:9 dd:8 d7:1 z8:8 y8:8 nlv:1 nls:1 slv:1 kt:1 kw:1 kv:1 yv:1 kp2:16 kp3:8 kpo:8 own:16 same:16 dup:1 q7:1"),
     ("wm", "wa:25 wc:25"),
 ):
     _c = 0
@@ -47,7 +50,7 @@ BANKS = ["pb%d" % _b for _b in range(8)]
 for _n in BANKS:
     SCRATCH[_n] = ("psum", [128, 512], F32)
 SEMAPHORES = ["ev", "ec", "et_", "ep", "dch", "dcd", "dx", "dtb", "dw", "dmg", "dk", "dy", "do0", "do1", "dp0", "dp1",
-              "arx", "arl", "arc", "ark", "loc"]
+              "arx", "al0", "al1", "al2", "al3", "arc", "ark", "loc"]
 
 
 def rank_program(g, core, T, topo):
@@ -208,7 +211,11 @@ def rank_program(g, core, T, topo):
         e = [n for n in topo.engines(core, T.cores[others[0]]) if all(n in topo.engines(core, T.cores[q]) for q in others)]
         ids = [DstId(rid=topo.addr(T.cores[q])[0], pnc=topo.addr(T.cores[q])[1]) for q in ring]
         count["loc"] = count.get("loc", 0) + len(e)
-        count[sem] = count.get(sem, 0) + len(e) * len(others)
+        if sem[:2] == "al":
+            for q in others:
+                count["al%d" % q] = len(e)
+        else:
+            count[sem] = count.get(sem, 0) + len(e) * len(others)
         g.remote_dma_fused([RemoteDMATransfer(dst_ids=ids, dma_engine_mask=sum(1 << n for n in e), remote_sem=T.sem[sem],
                                               srcs=[u8(s)], dsts=[u8(dst(q)) for q in ring])], local_sem=T.sem.loc)
 
@@ -225,170 +232,163 @@ def rank_program(g, core, T, topo):
 
     IQ = IW // 4
     iota("ip", [[1, 1]], 0, 1, 0, 1)
-    iota("t32", [[1, 32]], 0, 0)
-    iota("dc0", [[1, 12]], DB, 0)
+    iota("xt", [[0, 384]], 0, 0, 128, 512)
+    iota("t32", [[1, 44]], 0, 0)
+    iota("dc0", [[-1, 12]], -DB - 12 * 31, 0)
     iota("cv", [[32, 12], [1, 16]], -MID, 0)
-    iota("plc", [[32, 12]], UB - 32 * r, 1)
-    iota("ir", [[1, 12], [0, 2]], 0, 0)
-    iota("c4", [[1, 4]], 0, 0)
     runs = [(a, b, c) for a, b, c in ((0, P * r, 0), (P * r + P, N * P, P * r)) if b > a]
     for a, b, c in runs:
-        memset(R("mk", a, b), 0.0)
-    memset(R("ones"), 1.0)
+        memset(R("mk", a, b), -1.0)
+    memset(R("ones"), 0.0)
     p = R("ip", 0, 1)
     for k, (sh, msk) in enumerate(((0, 15), (4, 1), (0, 1), (4, 7), (0, 3), (0, 7), (0, 31))):
         ts(R("it", k, k + 1), p, sh, msk, O.logical_shift_right, O.bitwise_and)
     lcol, hcol, ecol, gcol, p3, p7, pcol = [R("pf", k, k + 1) for k in range(7)]
-    memset(R("xt", 128, 512), 0.0)
     copy(R("off", 0, 8, st=2), R("cdh"))
     copy(R("pf", 0, 7), R("it", 0, 7))
-    memset(R("mm", 0, 12, 32 * r, 32 * r + 32), 0.0)
-    lin(R("ca", 0, 1), hcol, 16.0)
+    memset(R("mm"), 0.0)
     lin(R("ca", 6, 7), pcol, 12.0)
-    lin(R("wn", 16, 208), R("cv"), 0.0)
-    lin(R("dc"), R("dc0"), 1.0, R("ca", 6, 7))
-    lin(R("cv"), R("cv"), 1.0, R("ca", 0, 1))
-    lin(R("dc1"), R("dc"), -1.0, -1.0)
-    lin(R("zz"), R("cv", 0, 128), 0.0)
+    lin(R("ca", 0, 1), hcol, 16.0)
 
     for i in range(4):
         scatter(R("mk"), R("off", 2 * i, 2 * i + 1), R("ones"))
+        if i == 0:
+            ts(R("one"), R("t32"), 11.5, None, O.is_lt)
         if i == 1:
             quant("xq", 0, 128, R("xt", 0, 512))
             points("")
+            iota("ir", [[1, 12], [0, 2]], 0, 0)
+            iota("zp", [[32, 12]], -MID - 32 * r, 1)
             iota("idt", [[1, IQ]], 0, 0, 0, IQ)
+            iota("idt", [[1, 2 * IQ]], IQ, 0, IQ, 3 * IQ)
         if i == 2:
-            ts(R("tri"), R("t32"), pcol, None, O.is_gt)
-            memset(R("zf", 400, 416), 0.0)
-    memset(R("zf", 0, 16), 0.0)
+            ts(R("tri"), R("t32", 0, 32), pcol, None, O.is_gt)
+    memset(R("wn", 16, 208), 0.0)
     for a, b, c in runs:
         turn(R("tm", c, c + b - a), R("mk", a, b))
 
-    wcol = R("xr", 10, 11)
-    lin(R("cq", 3, 4), hcol, -1.0, gcol)
+    wcol = R("xr", 4, 5)
     lin(R("xr", 9, 10), ecol, -1.0, lcol)
     lin(R("xr", 0, 1), hcol, -1.0, ecol, AF.Abs)
     lin(R("xr", 1, 2), hcol, -1.0, 6.0)
-    lin(R("xr", 2, 3), hcol, -1.0, 13.0)
-    lin(R("cq", 4, 5), R("cq", 3, 4), 1.0, -2.0 * r - 1.0, AF.Sign)
+    lin(R("dc1"), R("dc0"), 1.0, R("ca", 6, 7))
     lin(wcol, R("xr", 9, 10), 0.5)
     lin(R("xr", 7, 8), R("xr", 0, 1), 1.0, R("xr", 9, 10))
     lin(R("xr", 11, 12), ecol, -1.0, p7)
-    lin(R("cq", 5, 6), R("cq", 4, 5), -LC / 2, UR - 1.0 - LC / 2)
-    lin(R("xr", 3, 4), R("xr", 0, 1), R("xr", 1, 2), wcol)
+    lin(R("xr", 2, 3), hcol, -1.0, 13.0)
+    lin(R("cv"), R("cv"), 1.0, R("ca", 0, 1))
+    lin(R("cq", 3, 4), hcol, -1.0, gcol)
     lin(R("xr", 5, 6), R("xr", 0, 1), R("xr", 2, 3), wcol)
+    lin(R("xr", 3, 4), R("xr", 0, 1), R("xr", 1, 2), wcol)
+    lin(R("cq", 4, 5), R("cq", 3, 4), 1.0, -2.0 * r - 1.0, AF.Sign)
     lin(R("xr", 8, 9), R("xr", 7, 8), 1.0, 16.0)
-    lin(R("ca", 1, 2), gcol, 4.0)
-    lin(R("cq", 2, 3), R("cq", 3, 4), LC / 2, R("cq", 5, 6))
-    lin(R("cq", 1, 2), R("cq", 3, 4), -P / 2, 16.0)
-    lin(R("xr", 4, 5), R("xr", 3, 4))
     lin(R("xr", 6, 7), R("xr", 5, 6), 1.0, 8.0)
+    lin(R("cq", 5, 6), R("cq", 4, 5), LC / 2, LC / 2 - UR)
+    lin(R("cq", 1, 2), R("cq", 3, 4), -P / 2, 16.0)
+    lin(R("cq", 2, 3), R("cq", 3, 4), -LC / 2, R("cq", 5, 6))
     for j in range(4):
         copy(R("cdp", 8 * j, 8 * j + 8), R("cdi", j, 32, st=4), "s")
-    for k in range(1, 4):
-        lin(R("idt", IQ * k, IQ * k + IQ), R("idt", 0, IQ), 1.0, float(IQ * k))
+    lin(R("cq", 2, 3, 32 * r, 32 * r + 32), R("cq", 3, 4, 32 * r, 32 * r + 32), 0.0, -float(UB + MID))
+    lin(R("ca", 1, 2), gcol, 4.0)
+    for c in (0, 400):
+        lin(R("zf", c, c + 16), R("t32", 0, 16), 0.0, R("cq", 2, 3))
     tt(R("m1"), R("tm", 0, 3 * P, st=32), R("tm", 16, 3 * P, st=32), O.max)
     memset(R("tbt", 0, 128), 0.0)
     tt(R("m2", 0, 36, 0, 64), R("m1", 0, 36, 0, 64), R("m1", 0, 36, 64, 128), O.max)
     for k, q in enumerate(others):
         tt(R("mm", 0, 12, 32 * q, 32 * q + 32), R("m2", 12 * k, 12 * k + 12, 0, 32), R("m2", 12 * k, 12 * k + 12, 32, 64), O.max)
-    scan(R("sn"), R("mm"), R("mm"), O.add, O.max)
-    tt(R("g1"), R("mm"), R("dc1"), O.mult)
-    ts(R("x0"), R("tri"), R("sn", 11, 12), None, O.mult)
-    tt(R("g2"), R("g1"), R("dc"), O.add)
-    turn(R("xt0"), R("x0"))
-    tt(R("g3"), R("g2"), R("sn"), O.add)
-    red(R("base"), R("xt0"), O.add)
-    copy(R("wr"), R("xr", 3, 9))
+    scan(R("sn"), R("mm"), R("one"), O.add, O.add)
+    tt(R("g1"), R("mm", 0, 12), R("dc1"), O.mult)
     copy(R("rl"), R("ir"))
-    ts(R("wl"), R("g3"), R("base"), None, O.add)
-    ts(R("zp"), R("sn"), R("base"), R("cq", 2, 3), O.add, O.add)
+    turn(R("xt0"), R("sn", 12, 44))
+    tt(R("g3"), R("g1"), R("sn", 0, 12), O.add)
+    copy(R("wr"), R("xr", 3, 9))
+    scan(R("x0"), R("xt0"), R("tri"), O.add, O.mult)
+    base = R("x0", 31, 32)
+    memset(R("zz"), 0.0)
+    ts(R("wl"), R("g3"), base, -1.0, O.add, O.add)
+    for a, b in (((32, 64), (64, 128)), ((0, 32), (64, 128)), ((0, 64), (96, 128)), ((0, 64), (64, 96)))[r]:
+        ts(R("zp", 0, 12, a, b), R("sn", 0, 12, a, b), R("x0", 31, 32, a, b), -1.0, O.add, O.add)
     scatter(R("wn", 32), R("wl"), R("cv"))
-    copy(R("zp", 0, 12, 32 * r, 32 * r + 32), R("plc", 0, 12, 32 * r, 32 * r + 32))
+    gather(R("zrep"), R("zp"), R("rl"), "s")
+    lin(R("idt", 3 * IQ), R("idt", 0, IQ), 1.0, float(3 * IQ))
+    ts(R("gx"), R("cdp"), R("cq", 1, 2), 15.0, O.add, O.max, R("wr", 4, 6))
     turn(R("wnt", 0, LC), R("wn", 32, 192))
     turn(R("wnt", LC), R("wn", 16, 208))
-    ts(R("gx"), R("cdp"), R("cq", 1, 2), 15.0, O.add, O.max, R("wr", 4, 6))
-    tt(R("zz", 0, 11), R("wnt", 0, 352, st=32), R("wnt", 16, 352, st=32), O.add)
-    ts(R("pl", 0, 1), R("xr", 11, 12), 4.0, gcol, O.mult, O.add)
     ts(R("og"), R("gx"), 400.0, None, O.min)
+    ts(R("pl", 0, 1), R("xr", 11, 12), 4.0, gcol, O.mult, O.add)
+    tt(R("zz", 0, 11), R("wnt", 0, 352, st=32), R("wnt", 16, 352, st=32), O.add)
     ts(R("lst"), R("zz", 0, 16), float(MID), None, O.add, None, R("wr", 0, 1))
-    spread(R("lst", 0, 10), lambda q: R("lnd", 10 * here[q], 10 * here[q] + 10), "arl")
-
-    gather(R("zrep"), R("zp"), R("rl"), "s")
-    iota("br0", [[32, 4]], 0, 0)
-    iota("rst0", [[32, 4], [0, 16]], 2, 0)
-    iota("pm0", [[4, 4], [0, 4]], 3, 0)
-    iota("ib", [[128, 4]], 0, 1)
-    iota("bo0", [[33, 4], [0, 2]], 0, 0)
-    iota("ce", [[1, 1]], -3, -4)
-    quant("vq", 0, P, R("tbt", 128))
-    turn(R("zf", 16, 400), R("zrep"))
-    gather(R("nc"), R("cdp"), R("pl", 0, 1))
-    quant("uc", 0, UR, R("tbt"))
-    gather(R("zr", 0, 256), R("zf"), R("og", 0, 16), "s")
-
-    note(None, [R("lnd", 0, 30)], [], "arl", count["arl"])
-    for a in others:
-        copy(R("lnd", 0, 30, 32 * a, 32 * a + 32), R("lnd", 0, 30, 32 * r, 32 * r + 32))
-
-    def piece(s, k):
-        q = others[k]
-        return (q, R("pk" + s, LC * k, LC * k + LC), R("uc" + s, UR + LC * here[q], UR + LC * here[q] + LC))
-    ks = [others.index(q) for q in ring]
-    for i, k in enumerate(ks):
-        pick("pk", LC * k, LC * k + LC, "vq", P, R("lnd", 10 * k, 10 * k + 10))
-        send([piece("", k)], "arc")
-        if i:
-            send([piece("s", ks[0]), piece("s", ks[1])] if i == 1 else [piece("s", k)], "arc")
+    spread(R("lst", 0, 10), lambda q: R("lnd", LS[ring.index(q)], LS[ring.index(q)] + 10), "al%d" % r)
 
     iota("t1", [[0, 144]], 0, 0)
-    iota("gl0", [[2, 3]], 3, 0, 0, 3)
-    iota("gl0", [[1, 2]], 0, 0, 3, 5)
+    iota("ib", [[128, 4]], 0, 1)
+    iota("bo0", [[33, 4], [0, 2]], 0, 0)
+    iota("br0", [[32, 4]], 0, 0)
+    turn(R("zf", 16, 400), R("zrep"))
+    for k in range(2):
+        gather(R("zr", 256 * k, 256 * k + 256), R("zf"), R("og", 16 * k, 16 * k + 16), "s")
+    quant("vq", 0, P, R("tbt", 128))
+    gather(R("nc"), R("cdp"), R("pl", 0, 1))
+    ts(R("pl", 2, 3), R("pl", 0, 1), hcol, None, O.subtract)
+    memset(R("xt", 512, 640), 0.0)
+    copy(R("nl"), R("nc", 0, 8))
+    lin(R("n1", 8, 16), R("nc", 0, 8), 1.0 / 8192, NB / 8192 - 0.75)
+    turn(R("zt", 0, 256), R("zr", 0, 256))
+    quant("uc", 0, UR, R("tbt"))
+
+    back = ring[::-1]
+    for k, q in enumerate(back):
+        note(None, [R("lnd", LS[k], LS[k] + 10)], [], "al%d" % q, count["al%d" % q])
+    for c0, c1, who in ((0, 10, "vvs"), (16, 36, "sss")):
+        for i, a in enumerate(others):
+            copy(R("lnd", c0, c1, 32 * a, 32 * a + 32), R("lnd", c0, c1, 32 * r, 32 * r + 32), who[i])
+
+    def piece(s, k):
+        q = back[k]
+        return (q, R("pk" + s, LC * k, LC * k + LC), R("uc" + s, UR + LC * here[q], UR + LC * here[q] + LC))
+    for k in range(3):
+        pick("pk", LC * k, LC * k + LC, "vq", P, R("lnd", LS[k], LS[k] + 10))
+        send([piece("", k)], "arc")
+    send([piece("s", 0), piece("s", 1)], "arc")
+    send([piece("s", 2)], "arc")
+
     points("s")
-    iota("t2", [[0, 256]], 0, 0, 0, 256)
+    iota("c4", [[1, 4]], 0, 0)
+    iota("rst0", [[32, 4], [0, 16]], 4, 0)
+    iota("pm0", [[4, 4], [0, 4]], 3, 0)
     iota("hv0", [[16, 2], [0, 2]], 0, 0)
+    copy(R("t1", 0, 128, st=16), R("n1", 8, 16), "s")
+    lin(R("et", 0, 516), R("idt", 0, 516), 0.0)
+    et = R("et", 0, 512)
+    op("p", lambda: g.affine_select(et["ap"], et["ap"], [[1, 512]], O.not_equal, 0.5, -3, -4), [et], [et])
+    iota("gl0", [[2, 3]], 5, 0, 0, 3)
+    iota("gl0", [[2, 2]], 0, 0, 3, 5)
+    iota("gl0", [[-62, 2]], 3, 0, 5, 7)
+    iota("t2", [[0, 256]], 0, 0, 0, 256)
     iota("jc0", [[16, 24]], 0, 0)
     iota("pt0", [[A, r + 1], [1, 4], [0, 4]], 0, 0, 0, 16 * r + 16)
     if r < N - 1:
         iota("pt0", [[A, N - 1 - r], [1, 4], [0, 4]], A * r + 128, 0, 16 * r + 16, 64)
     iota("wk", [[0, 416]], NOP, 0, P * r + 16, P * r + 432)
-    gather(R("zr", 256, 512), R("zf"), R("og", 16, 32), "s")
-    for j in range(4):
-        lin(R("gg", 16 * j, 16 * j + 16), R("t32", 0, 16), 0.0, R("nc", 2 * j, 2 * j + 1))
-    lin(R("br1"), R("br0"), 1.0, R("ca", 0, 1))
-    lin(R("rst"), R("rst0"), 1.0, R("ca", 0, 1))
-    lin(R("n1", 8, 16), R("nc", 0, 8), 1.0 / 8192)
-    lin(R("ca", 2, 3), hcol, 16.0, -64.0)
-    lin(R("ca", 3, 4), hcol, -1008.0, 448.0)
-    lin(R("c2", 0, 4), R("c4"), 31.875)
-    lin(R("ca", 12, 13), p7, 31.875, R("ca", 0, 1))
-    lin(R("ca", 4, 5), lcol, 1.0, float(DUMP))
-    lin(R("ca", 8, 9), p3, -1.0, -1.0)
-    lin(R("ca", 14, 15), p3, -1.0)
-    lin(R("ca", 13, 14), lcol, 0.125, R("ca", 12, 13))
-    lin(R("ab"), R("idt", 0, 516), 1.0, R("ce"), AF.Abs)
-    lin(R("et", 0, 516), R("ab"), -0.5, 0.5, AF.Relu)
+    lin(R("bo"), R("bo0"), 1.0, R("ca", 1, 2))
+    lin(R("br"), R("br0"), 1.0, pcol)
+    copy(R("bl"), R("ib"), "s")
 
-    turn(R("zt", 0, 256), R("zr", 0, 256))
-    copy(R("nl"), R("nc", 0, 8, st=2))
-    memset(R("xt", 512, 640), 0.0)
-    quant("wq", 0, 128, R("wt"))
-    ts(R("pl", 2, 3), R("pl", 0, 1), hcol, None, O.subtract)
+    def tie(j):
+        ts(R("tie", 16 * j, 16 * j + 16), R("idt"), R("nc", 2 * j, 2 * j + 1), -2.0 ** -100, O.is_lt, O.mult, R("nl", 2 * j, 2 * j + 1))
     turn(R("zt", 256, 512), R("zr", 256, 512))
-    quant("xa", 32 * r, 32 * r + 128, R("xt", 0, 512))
+    tie(0)
+    tie(1)
     tt(R("z2", 0, 32, 0, 64), R("zt", 0, 512, 0, 64, 16), R("zt", 0, 512, 64, 128, 16), O.add)
     for a in range(4):
         tt(R("sf", 0, 32, 32 * a, 32 * a + 32), R("z2", 0, 32, 0, 32), R("z2", 0, 32, 32, 64), O.add)
-    gather(R("sw"), R("sf"), R("wr", 4, 6))
-    quant("xa", NOP, NOP + 128, R("xt", 128, 640))
-    gather(R("sc"), R("sf"), R("pl", 2, 3))
-    ttg(R("nr"), R("idt"), R("nl"), R("gg"), O.is_lt)
-    copy(R("bl"), R("ib"))
-    ts(R("t1", 1, 128, st=16), R("sc", 0, 8), 1.0 / 8192, None, O.mult)
-    copy(R("t1", 0, 128, st=16), R("n1", 8, 16))
-    ts(R("bo"), R("bo0"), R("ca", 1, 2), None, O.add)
-    ts(R("br"), R("br1"), lcol, None, O.add)
-    ts(R("tie"), R("nr"), -2.0 ** -100, None, O.mult)
+    ts(R("sw"), R("sf"), float(ZB), None, O.add, None, R("wr", 4, 6))
+    ts(R("sc"), R("sf"), 1.0 / 8192, ZB / 8192 - 0.75, O.mult, O.add, R("pl", 2, 3))
+    tie(2)
+    tie(3)
+    copy(R("t1", 2, 128, st=16), R("sc", 0, 8))
+    tt(R("t1", 1, 128, st=16), R("n1", 8, 16), R("t1", 0, 128, st=16), O.subtract)
 
     note(None, [R(n, UR, UW) for n in ("uc", "ucs")], [], "arc", count["arc"])
     for j in range(4):
@@ -407,113 +407,139 @@ def rank_program(g, core, T, topo):
     need("y", [], [R("ob")])
     for s in ("", "s"):
         dma("y", R("mg" + s, 0, P), R("vq" + s), "dmg", 2)
-    memset(R("cn", 0, 1), 1.0)
+    lin(R("c2", 0, 4), R("c4"), 31.875)
+    lin(R("ca", 2, 3), hcol, 528.0, -128.0)
+    lin(R("ca", 3, 4), hcol, -496.0, 384.0)
+    lin(R("ca", 12, 13), p7, 31.875, R("ca", 0, 1))
+    lin(R("ca", 14, 15), p3, -1.0, 0.75)
+    lin(R("ca", 4, 5), lcol, 1.0, float(DUMP))
+    lin(R("ca", 13, 14), lcol, 0.125, R("ca", 12, 13))
+    lin(R("cn", 0, 2), R("t32", 0, 2), 1.0, R("ca", 14, 15))
     ts(R("mk4"), R("c4"), p3, None, O.is_equal)
+    tt(R("t1", 3, 128, st=16), R("sc", 0, 8), R("t1", 2, 128, st=16), O.subtract)
     turn(R("obt", 64, 128), R("ob", 64, 128))
-    ttg(R("bb"), R("cg"), R("bl"), own, O.is_lt)
-    ttg(R("dw"), R("obt"), R("br"), own, O.subtract)
-    ts(R("pm"), R("pm0"), lcol, 4096.0, O.is_ge, O.mult)
+    ts(R("pm0"), R("pm0"), lcol, 8193.0, O.is_lt, O.mult)
     ts(R("hv"), R("hv0"), lcol, None, O.add)
+    ttg(R("dw"), R("obt"), R("br"), own, O.subtract)
+    ttg(R("bb"), R("cg"), R("bl"), own, O.is_lt)
+    lin(R("pm"), R("pm0"), 1.0, -1.0)
+    lin(R("ptv"), R("pt0"), 1.0, R("ca", 1, 2))
+    lin(R("jc"), R("jc0"), 1.0, lcol)
     tt(R("w2"), R("dw"), R("tie"), O.is_gt)
     quant("eq", 0, 128, R("et", 3, 515))
-    scan(R("rks"), R("rst"), R("w2"), O.max, O.add)
+    scan(R("rks"), R("rst0"), R("w2"), O.max, O.add)
     quant("eq", 128, 256, R("et", 2, 514))
     rank = R("rks", 15, 64, st=16)
-    copy(R("l1"), rank)
+    ts(R("l1"), rank, R("ca", 0, 1), None, O.add)
     tt(R("l2a", 0, 4), rank, R("c2", 0, 4), O.subtract)
     memset(R("kd"), 0.0)
     scatter(R("t1"), R("l1"), R("bb"))
     for k in range(2):
         ts(R("l2", k, 8, st=2), R("l2a", 0, 4), 32.0, R("ca", 2 + k, 3 + k), O.mult, O.add)
     turn(R("t1t"), R("t1", 0, 128))
-    ts(R("gl", 0, 5), R("gl0"), R("ca", 13, 14), None, O.add)
+    ts(R("gl", 0, 7), R("gl0"), R("ca", 13, 14), 0.0, O.add, O.max)
     scatter(R("t2"), R("l2"), R("t1t"))
     quant("eq", 256, 384, R("et", 1, 513))
     for k in range(1, 4):
-        copy(R("t2", k, 256, st=4), R("t2", 0, 256, st=4))
+        copy(R("t2", k, 256, st=4), R("t2", 0, 256, st=4), "vvvs"[k])
     quant("eq", 384, 512, R("et", 0, 512))
     turn(R("t2t"), R("t2", 0, 256))
-    lin(R("ptv"), R("pt0"), 1.0, R("ca", 1, 2))
-    lin(R("jc"), R("jc0"), 1.0, lcol)
     parts = [(ch, b) for ch in range(2) for b in range(4)]
-    for ch, b in parts:
+
+    def old(ch, b):
         mm(BANKS[4 * ch + b], CUT[ch][1] - CUT[ch][0], "eq", 128 * b, "vq", CUT[ch][0], CUT[ch][1], True, False)
+    for ch, b in parts[:7]:
+        old(ch, b)
 
-    gather(R("alg", 0, 80), R("t2t"), R("gl", 0, 5))
-    nn, sl8 = R("alg", 48, 56), R("alg", 56, 64)
-
-    def left(u, v, w=None):
-        return R("alg", 64 + 8 * u + v, 64 + 8 * u + (v + 1 if w is None else w))
+    ts(R("alg", 96, 112), R("t2t", 64), R("t2t", 36, 37), R("t2t", 52, 53), O.subtract, O.is_ge, R("gl", 6, 7))
+    ts(R("dd", 2, 3), R("t2t", 68, 69), R("t2t", 84, 85), 0.5, O.add, O.is_lt)
+    ts(R("cn", 2, 3), R("cn", 1, 2), R("t2t", 36, 37), R("t2t", 52, 53), O.add, O.add)
+    gather(R("alg", 0, 96), R("t2t"), R("gl", 0, 6), "s")
 
     def step(u, v, w=None):
-        return R("tmp", 8 * u + v, 8 * u + (v + 1 if w is None else w))
+        return R("alg", 88 + 8 * u + v, 88 + 8 * u + (v + 1 if w is None else w))
 
-    def cn(u):
-        return R("cn", u, u + 1)
-    ts(step(1, 2, 8), R("alg", 2, 8), left(1, 1), None, O.is_ge)
-    ts(R("mk8"), nn, R("ca", 8, 9), None, O.add)
-    memset(left(0, 0), 1.0)
-    lin(cn(1), left(1, 1), 1.0, 1.0)
-    lin(R("mk7"), R("alg", 55, 56), 1.0, R("ca", 14, 15))
+    def one(n, u):
+        return R(n, u, u + 1)
+
+    def fell(o, v, u, w):
+        a = R("alg", 88 + v, 88 + v + 8 * (u - 1) + 1, st=8)
+        op("s", lambda: g.scalar.activation(R("al", 8 * w, 8 * w + u)["ap"], a["ap"], AF.Identity, scale=-1.0, bias=1.0, accum_out=o["ap"]), [o], [a])
     for u in range(2, 7):
-        ts(step(u, u + 1, 8), R("alg", 9 * u - 7, 8 * u), left(u - 1, u), step(u - 1, u), O.is_ge, O.is_ge)
+        ts(step(u, u + 1, 8), R("alg", 9 * u - 7, 8 * u), one("dd", u), step(u - 1, u), O.add, O.is_ge)
+        fell(one("dd", u + 1), u + 1, u, u)
+        if u == 5:
+            fell(R("d7"), 7, 5, 7)
+        ts(one("cn", u + 1), one("dd", u), step(u - 1, u), one("cn", u), O.is_lt, O.add)
+        if u == 2:
+            tt(R("mk8", 0, 8), R("alg", 48, 56), R("alg", 56, 64), O.add)
+        else:
+            ts(one("mk8", 9 * u), one("dd", u), step(u - 1, u), one("mk8", u), O.is_lt, O.mult)
+        if u == 3:
+            lin(one("mk8", 9), one("mk8", 1), step(0, 1))
+            ts(one("mk8", 18), one("dd", 2), step(1, 2), one("mk8", 2), O.is_lt, O.mult)
         if u == 6:
-            ts(R("q7"), R("mk7"), left(5, 7), step(5, 7), O.mult, O.mult)
-        tt(left(u, u, 8), left(u - 1, u, 8), step(u - 1, u, 8), O.min)
-        lin(cn(u), left(u - 1, u), step(u - 1, u), cn(u - 1))
-    al = R("alg", 64, 128, st=9)
-    tt(R("ck", 0, 6), R("mk8", 0, 6), R("alg", 64, 110, st=9), O.mult)
-    ts(R("z8", 7, 8), R("q7"), step(6, 7), cn(6), O.mult, O.add)
-    ts(R("z8", 6, 7), R("mk8", 6, 7), left(6, 6), cn(6), O.mult, O.add)
-    tt(R("z8", 0, 6), R("cn", 0, 6), R("ck", 0, 6), O.add)
-    tt(left(7, 7), left(6, 7), step(6, 7), O.min)
-    lin(cn(7), left(6, 7), step(6, 7), cn(6))
-    ts(R("ms8"), sl8, R("ca", 8, 9), None, O.add)
+            ts(R("q7"), R("d7"), step(5, 7), one("mk8", 7), O.is_lt, O.mult)
+    tt(R("z8", 0, 7), R("cn", 0, 7), R("mk8", 0, 55, st=9), O.add)
+    ts(one("z8", 7), R("q7"), step(6, 7), one("cn", 7), O.mult, O.add)
+    ts(one("cn", 8), one("dd", 7), step(6, 7), one("cn", 7), O.is_lt, O.add)
+    tt(R("ms8"), R("alg", 64, 72), R("alg", 72, 80), O.add)
     red(R("nlv"), R("z8"), O.min, True)
-    tt(R("ms9"), R("ms8"), al, O.mult)
+    tt(R("y8"), R("cn", 1, 9), R("cn", 0, 8), O.subtract)
     ts(R("kl", 0, 1), R("nlv"), 8192.0, R("ca", 4, 5), O.mult, O.min)
-    ts(R("own"), R("pm"), R("nlv"), 8192.0, O.add, O.mult)
+    lin(R("own"), R("pm"), R("nlv"))
     ts(R("nls"), R("nlv"), 8192.0, R("ca", 4, 5), O.mult, O.min)
+    tt(R("ms9"), R("ms8"), R("y8"), O.mult)
     ttg(R("same"), R("idt"), R("kl", 0, 1), R("own"), O.is_equal)
-    tt(R("y8"), R("cn"), R("ms9"), O.add)
-    ts(R("kt"), R("nlv"), 0.5, None, O.is_lt)
+    ts(R("kt"), R("nlv"), 0.22, None, O.is_lt)
+    tt(R("ms8"), R("cn", 0, 8), R("ms9"), O.add)
     red(R("dup"), R("same"), O.max)
-    red(R("slv"), R("y8"), O.min, True)
-    ts(R("kw"), R("nlv"), 8192.0, 1.0, O.mult, O.add)
+    ts(R("kw"), R("nlv"), 8192.0, 1.0 - NB, O.mult, O.add)
+    red(R("slv"), R("ms8"), O.min, True)
     ts(R("kd", 0, 1), R("dup"), R("ca", 4, 5), R("nls"), O.mult, O.max)
     spread(R("kd"), lambda q: R("kla", 2 * here[q], 2 * here[q] + 2), "ark")
 
-    ts(R("yv"), R("slv"), 0.5, 8192.0, O.is_lt, O.mult)
+    ts(R("yv"), R("slv"), 0.22, 8192.0, O.is_lt, O.mult)
     tt(R("kv"), R("kw"), R("kt"), O.mult)
+    quant("wq", 0, 128, R("wt"))
     tt(R("zz", 96, 97), R("slv"), R("yv"), O.mult)
     ts(R("zz", 64, 68), R("mk4"), R("kv"), None, O.mult)
     turn(R("yr"), R("zz", 96, 128))
     turn(R("kpt"), R("zz", 64, 96))
+    quant("xa", 32 * r, 32 * r + 128, R("xt", 0, 512))
     gather(R("yd"), R("yr"), R("hv"))
     tt(R("kp2"), R("kpt", 0, 32, st=2), R("kpt", 1, 32, st=2), O.add)
     turn(R("ydt"), R("yd"))
-    tt(R("kp3"), R("kp2", 0, 16, st=2), R("kp2", 1, 16, st=2), O.add)
+    quant("xa", NOP, NOP + 128, R("xt", 128, 640))
     for a in range(4):
         copy(R("ksl", 2 * a, 2 * a + 2, 0, 32), R("ydt", 0, 64, 32 * a, 32 * a + 32, 32), "s")
     for b in range(1, 4):
         copy(R("ksl", 0, 8, 32 * b, 32 * b + 32), R("ksl", 0, 8, 0, 32), "s")
-    ts(R("kpo"), R("kp3"), -1.0, None, O.add)
-    for a in range(4):
-        dma("y", T.kp[:, 8 * a:8 * a + 8], R("kpo", 0, 8, 32 * a, 32 * a + 4), "dk", 4)
 
     note(None, [R("kla")], [], "ark", count["ark"])
     for q in reversed(range(N)):
         k = q - (q > r)
-        scatter(R("wk", 32), R("kd", 0, 1) if q == r else R("kla", 2 * k, 2 * k + 1), R("ptv", 16 * q, 16 * q + 16))
-        if q in (1, 2):
-            pick("kq", 64 * (2 - q), 64 * (3 - q), "uc", UW, R("ksl", 4 * (2 - q), 4 * (3 - q)))
+        scatter(R("wk", 32 - NB), R("kd", 0, 1) if q == r else R("kla", 2 * k, 2 * k + 1), R("ptv", 16 * q, 16 * q + 16))
+        if q == 3:
+            tt(R("kp3"), R("kp2", 0, 16, st=2), R("kp2", 1, 16, st=2), O.add)
+        if q == 2:
+            ts(R("kpo"), R("kp3"), -1.0, None, O.add)
+            for a in range(4):
+                dma("y", T.kp[:, 8 * a:8 * a + 8], R("kpo", 0, 8, 32 * a, 32 * a + 4), "dk", 4)
+    pick("kq", 0, 64, "uc", UW, R("ksl", 0, 4))
     turn(R("tk", 0, P), R("wk", P * r + 32, P * r + 416))
     turn(R("tk", P), R("wk", P * r + 16, P * r + 432))
+    pick("kq", 64, 128, "uc", UW, R("ksl", 4, 8))
+    mm(BANKS[7], 128, "wq", 0, "kq", 0, 128)
+    copy(R("yt"), R(BANKS[7], 0, 128), "s")
+    dma("y", T.y[:, :], R("yt"), "dy", 1)
+    old(1, 3)
     tt(R("wa"), R("tk", 0, 800, st=32), R("tk", 16, 800, st=32), O.min)
     tt(R("wc", 0, 25, 0, 64), R("wa", 0, 25, 0, 64), R("wa", 0, 25, 64, 128), O.min)
     for a in range(4):
         tt(R("zz", 32, 57, 32 * a, 32 * a + 32), R("wc", 0, 25, 0, 32), R("wc", 0, 25, 32, 64), O.min)
     gather(R("ln"), R("zz", 32, 64), R("wr", 2, 4))
+    ts(R("sl0"), R("zz", 32, 64), NOP - 0.5, float(P), O.is_lt, O.mult, R("wr", 2, 4))
 
     note(None, [R("xa" + s, 32 * q + 96 * (q > r), 32 * q + 96 * (q > r) + 32) for q in others for s in ("", "s")], [], "arx", count["arx"])
     for a, b in CUT:
@@ -529,7 +555,7 @@ def rank_program(g, core, T, topo):
 
     def store(ch, who):
         a, b = CUT[ch]
-        pick("oq", a, b, "mg", 2 * P, R("sl", a // 16, b // 16), who)
+        pick("oq", a, b, "mg", P + b, R("sl", a // 16, b // 16), who)
         if who == "v":
             dma("y", T.oc[:, 4 * a:4 * b], R("oq", a, b), "do%d" % ch, 1)
         else:
@@ -542,17 +568,10 @@ def rank_program(g, core, T, topo):
             new(int(w[1]))
         elif w[0] == "o":
             store(int(w[1]), w[2])
-        elif w == "s0":
-            ts(R("sl0"), R("ln", 0, 24), NOP - 0.5, float(P), O.is_lt, O.mult)
         elif w == "s1":
-            tt(R("sl1"), R("sl0"), R("jc"), O.add)
+            tt(R("sl1"), R("sl0", 0, 24), R("jc"), O.add)
         elif w == "s2":
             copy(R("sl"), R("sl1"))
-        elif w == "ym":
-            mm(BANKS[0], 128, "wq", 0, "kq", 0, 128)
-        elif w[0] == "y":
-            copy(R("yt"), R(BANKS[0], 0, 128), w[1])
-            dma("y", T.y[:, :], R("yt"), "dy", 1)
 
     for s in sorted(count):
         g.wait_ge(T.sem[s], count[s])

@@ -2,15 +2,15 @@ from concourse.bass import DstId, RemoteDMATransfer
 from concourse.mybir import dt, AluOpType, AxisListType, ActivationFunctionType
 
 N, P, A, C, LC = 4, 384, 32, 16, 160
-UB = 32
-UR = UB + P
-UW = UR + 3 * LC
+UR = 0
+UB = 3 * LC
+UW = UB + P + 32
 DB = P
 MID = P // 2
 NB = 16
 DUMP = N * P + 4 + NB
 IW = DUMP + 20
-NOP = 224
+NOP = 128
 ZB = 3 * UR + 3 * LC + UB + MID
 LS = (0, 16, 26)
 CUT = ((0, 192), (192, 384))
@@ -19,15 +19,15 @@ ORDER = "s1 h00s h01v s2 h02s h03v h10v n0 h11s h12v o0v h13s o0s n1 o1v o1s"
 F32, BF, I32, U16, U8, F8 = "float32", "bfloat16", "int32", "uint16", "uint8", "float8_e4m3fn_x4"
 SCRATCH = {}
 for _d, _names in (
-    (BF, "tbt:1664 xt:640 wt:512 et:528 nt:1536"),
-    (F8, "vq:384 xq:128 wq:128 eq:512 xa:352 uc:896 pk:480 ex:512 kq:128 qp:384 mg:768 oq:384"),
-    (U8, "vqs:384 xqs:128 wqs:128 eqs:512 xas:352 ucs:896 pks:480 exs:512 kqs:128 qps:384 mgs:768 oqs:384"),
-    (I32, "kci:64"), (U16, "bl:4 bo:8 br:4 pl:4 rl:24 hv:4 wr:6 gl:8"), (BF, "ones:16 ptv:64"),
-    (F32, "kcf:576 idt:1576 cv:192 zz:128"),
-    (I32, "cdh:4 cdi:32"), (U16, "off:8 wl:12 lst:16 lnd:48"), (BF, "mk:1536 tm:1152 m1:36 m2:36 wn:1184 wnt:352 zrep:384 zf:416 zr:512 zt:512"),
+    (BF, "tbt:1664 xt:512 wt:512 et:528 nt:1536"),
+    (F8, "vq:384 xq:128 wq:128 eq:512 xa:144 uc:896 pk:480 ex:512 kq:128 qp:384 mg:768 oq:384"),
+    (U8, "vqs:384 xqs:128 wqs:128 eqs:512 xas:144 ucs:896 pks:480 exs:512 kqs:128 qps:384 mgs:768 oqs:384"),
+    (I32, "kci:64"), (U16, "bl:4 bo:8 br:4 pl:4 rl:24 hv:4 wr:6 gl:8 il:4"), (BF, "ones:16 ptv:64"),
+    (F32, "kcf:576 idt:1576 ids:1576 cv:192 zz:128"),
+    (I32, "cdh:36 cdi:32"), (U16, "off:8 wl:12 lst:16 lnd:48"), (BF, "mk:1536 tm:1152 m1:36 m2:36 wn:1184 wnt:352 zrep:384 zf:416 zr:512 zt:512"),
     (F32, "req:192 x0:32 xt0:32"),
     (F32, "cdp:32 zp:12 gx:32 z2:32 sf:32 sc:16 nc:16 n1:24 tie:64"), (U16, "og:32 sw:32 nl:8 kl:2"),
-    (F32, "cs:128 cg:512 ob:128 obt:128 dw:64 w2:64 bb:64 rks:64 l2a:8 alg:144"), (BF, "t1:144 t1t:128 t2:1024 t2t:256"), (U16, "l1:4 l2:8"),
+    (F32, "cs:128 cg:512 ob:128 obt:128 dw:64 bb:64 l2a:8 alg:144"), (BF, "w2:128 rks:128 rst0:128 t1:144 t1t:128 t2:1024 t2t:256"), (U16, "l1:4 l2:8"),
     (F32, "pr:208 kpt:32 yr:32 yd:64 ydt:64 yt:128 al:64"), (U16, "kd:2 ksl:8 kla:6"),
     (BF, "wk:1616 tk:800"), (F32, "wm:128 sl0:32 sl1:24"), (U16, "ln:32 sl:24"),
 ):
@@ -35,10 +35,10 @@ for _d, _names in (
         SCRATCH[_n.split(":")[0]] = ("sbuf", [128, int(_n.split(":")[1])], _d)
 PART = {}
 for _d, _names in (
-    ("kcf", "pf:10 xr:14 cq:8 ca:16 t32:44 tri:32 one:44 dc0:12 dc1:12 c4:4 bo0:8 br0:4 hv0:4 c2:8 jc0:24 jc:24 mk4:4 rst0:64 pm0:16 pm:16 pt0:64 gl0:7"),
+    ("kcf", "pf:10 xr:14 cq:8 ca:16 t32:44 tri:32 one:44 dc0:12 dc1:12 c4:4 bo0:8 br0:4 hv0:4 c2:8 jc0:24 jc:24 mk4:4 pm0:16 pm:16 pt0:64 gl0:7"),
     ("kci", "ip:2 ib:4 it:10 ir:24"),
     ("req", "mm:44 sn:44 g1:12 g3:12"),
-    ("pr", "mk8:56 ms8:8 ms9:8 cn:9 dd:8 d7:1 z8:8 y8:8 nlv:1 nls:1 slv:1 kt:1 kw:1 kv:1 yv:1 kp2:16 kp3:8 kpo:8 own:16 same:16 dup:1 q7:1"),
+    ("pr", "mk8:56 ms8:8 ms9:8 cn:9 dd:8 d7:1 d6:1 q6:1 z7:1 z8:8 y8:8 nlv:1 nls:1 slv:1 kt:1 kw:1 kv:1 kp2:16 kp3:8 kpo:8 own:16 same:16 dup:1 q7:1"),
     ("wm", "wa:25 wc:25"),
 ):
     _c = 0
@@ -49,8 +49,8 @@ for _d, _names in (
 BANKS = ["pb%d" % _b for _b in range(8)]
 for _n in BANKS:
     SCRATCH[_n] = ("psum", [128, 512], F32)
-SEMAPHORES = ["ev", "ec", "et_", "ep", "dch", "dcd", "dx", "dtb", "dw", "dmg", "dk", "dy", "do0", "do1", "dp0", "dp1",
-              "arx", "al0", "al1", "al2", "al3", "arc", "ark", "loc"]
+SEMAPHORES = ["ev", "ec", "et_", "ep", "dch", "dcd", "dx", "dtb", "dw", "dmg", "dk", "dy", "do0", "do1", "dp1",
+              "arx", "al0", "al1", "al2", "al3", "arc", "ars", "ark", "loc"]
 
 
 def rank_program(g, core, T, topo):
@@ -220,14 +220,14 @@ def rank_program(g, core, T, topo):
                                               srcs=[u8(s)], dsts=[u8(dst(q)) for q in ring])], local_sem=T.sem.loc)
 
     def points(s):
-        spread(R("xq" + s, 0, 32), lambda q: R("xa" + s, 32 * r + 96 * (r > q), 32 * r + 96 * (r > q) + 32), "arx")
+        spread(R("xq" + s, 0, 32), lambda q: R("xa" + s, 32 * r, 32 * r + 32), "arx")
 
-    for k in range(8):
-        dma("ys"[k % 2], R("cdh", 0, 4, 16 * k, 16 * k + 16), T.cd[:, 4 * k:4 * k + 4], "dch", 8)
-    dma("y", R("xt", 0, 128), T.x[:, :], "dx", 1)
-    dma("y", R("tbt", 128), T.tb[:, :], "dtb", 1)
+    for k in range(2):
+        dma("ys"[k], R("cdh", 4 - 4 * k, 36 - 4 * k, 16 * k, 16 * k + 16), T.cd[:, :], "dch", 2)
+    dma("s", R("xt", 0, 128), T.x[:, :], "dx", 1)
     for k in range(8):
         dma("y", R("cdi", 0, 32, 16 * k, 16 * k + 16), T.cd[:, :], "dcd", 8)
+    dma("y", R("tbt", 0, 4 * P), T.tb[:, :], "dtb", 1)
     dma("y", R("wt"), T.w[:, :], "dw", 1)
 
     IQ = IW // 4
@@ -244,30 +244,35 @@ def rank_program(g, core, T, topo):
     for k, (sh, msk) in enumerate(((0, 15), (4, 1), (0, 1), (4, 7), (0, 3), (0, 7), (0, 31))):
         ts(R("it", k, k + 1), p, sh, msk, O.logical_shift_right, O.bitwise_and)
     lcol, hcol, ecol, gcol, p3, p7, pcol = [R("pf", k, k + 1) for k in range(7)]
-    copy(R("off", 0, 8, st=2), R("cdh"))
-    copy(R("pf", 0, 7), R("it", 0, 7))
-    memset(R("mm"), 0.0)
-    lin(R("ca", 6, 7), pcol, 12.0)
-    lin(R("ca", 0, 1), hcol, 16.0)
+    for a in range(4):
+        copy(R("off", 0, 8, 32 * a, 32 * a + 32, 2), R("cdh", 8 * a + 4, 8 * a + 8, 0, 32), "vvss"[a])
+    need("s", [], [R("off", 0, 8, 64, 128)])
 
     for i in range(4):
         scatter(R("mk"), R("off", 2 * i, 2 * i + 1), R("ones"))
         if i == 0:
+            copy(R("pf", 0, 7), R("it", 0, 7))
             ts(R("one"), R("t32"), 11.5, None, O.is_lt)
+            lin(R("ca", 6, 7), pcol, 12.0)
+            lin(R("ca", 0, 1), hcol, 16.0)
         if i == 1:
             quant("xq", 0, 128, R("xt", 0, 512))
             points("")
             iota("ir", [[1, 12], [0, 2]], 0, 0)
             iota("zp", [[32, 12]], -MID - 32 * r, 1)
+            iota("zz", [[0, 128]], 0, 0)
             iota("idt", [[1, IQ]], 0, 0, 0, IQ)
             iota("idt", [[1, 2 * IQ]], IQ, 0, IQ, 3 * IQ)
         if i == 2:
             ts(R("tri"), R("t32", 0, 32), pcol, None, O.is_gt)
+            memset(R("mm"), 0.0)
     memset(R("wn", 16, 208), 0.0)
+    memset(R("kd"), 0.0)
     for a, b, c in runs:
         turn(R("tm", c, c + b - a), R("mk", a, b))
 
     wcol = R("xr", 4, 5)
+    lin(R("il"), R("t32", 0, 4), 16.0, lcol)
     lin(R("xr", 9, 10), ecol, -1.0, lcol)
     lin(R("xr", 0, 1), hcol, -1.0, ecol, AF.Abs)
     lin(R("xr", 1, 2), hcol, -1.0, 6.0)
@@ -292,8 +297,10 @@ def rank_program(g, core, T, topo):
     lin(R("ca", 1, 2), gcol, 4.0)
     for c in (0, 400):
         lin(R("zf", c, c + 16), R("t32", 0, 16), 0.0, R("cq", 2, 3))
+    lin(R("et", 0, 516), R("tm", 0, 516), 0.0)
     tt(R("m1"), R("tm", 0, 3 * P, st=32), R("tm", 16, 3 * P, st=32), O.max)
-    memset(R("tbt", 0, 128), 0.0)
+    memset(R("tbt", 4 * P), 0.0)
+    pick("xa", NOP, NOP + 16, "xq", 128, R("il", 2, 3), "v")
     tt(R("m2", 0, 36, 0, 64), R("m1", 0, 36, 0, 64), R("m1", 0, 36, 64, 128), O.max)
     for k, q in enumerate(others):
         tt(R("mm", 0, 12, 32 * q, 32 * q + 32), R("m2", 12 * k, 12 * k + 12, 0, 32), R("m2", 12 * k, 12 * k + 12, 32, 64), O.max)
@@ -305,7 +312,8 @@ def rank_program(g, core, T, topo):
     copy(R("wr"), R("xr", 3, 9))
     scan(R("x0"), R("xt0"), R("tri"), O.add, O.mult)
     base = R("x0", 31, 32)
-    memset(R("zz"), 0.0)
+    ts(R("pl", 0, 1), R("xr", 11, 12), 4.0, gcol, O.mult, O.add)
+    pick("xa", 32 * r, 32 * r + 32, "xq", 128, R("il", 0, 2), "v")
     ts(R("wl"), R("g3"), base, -1.0, O.add, O.add)
     for a, b in (((32, 64), (64, 128)), ((0, 32), (64, 128)), ((0, 64), (96, 128)), ((0, 64), (64, 96)))[r]:
         ts(R("zp", 0, 12, a, b), R("sn", 0, 12, a, b), R("x0", 31, 32, a, b), -1.0, O.add, O.add)
@@ -316,8 +324,11 @@ def rank_program(g, core, T, topo):
     turn(R("wnt", 0, LC), R("wn", 32, 192))
     turn(R("wnt", LC), R("wn", 16, 208))
     ts(R("og"), R("gx"), 400.0, None, O.min)
-    ts(R("pl", 0, 1), R("xr", 11, 12), 4.0, gcol, O.mult, O.add)
+    turn(R("zf", 16, 400), R("zrep"))
+    for k in range(2):
+        gather(R("zr", 256 * k, 256 * k + 256), R("zf"), R("og", 16 * k, 16 * k + 16), "s")
     tt(R("zz", 0, 11), R("wnt", 0, 352, st=32), R("wnt", 16, 352, st=32), O.add)
+    ts(R("pl", 2, 3), R("pl", 0, 1), hcol, None, O.subtract)
     ts(R("lst"), R("zz", 0, 16), float(MID), None, O.add, None, R("wr", 0, 1))
     spread(R("lst", 0, 10), lambda q: R("lnd", LS[ring.index(q)], LS[ring.index(q)] + 10), "al%d" % r)
 
@@ -325,17 +336,14 @@ def rank_program(g, core, T, topo):
     iota("ib", [[128, 4]], 0, 1)
     iota("bo0", [[33, 4], [0, 2]], 0, 0)
     iota("br0", [[32, 4]], 0, 0)
-    turn(R("zf", 16, 400), R("zrep"))
-    for k in range(2):
-        gather(R("zr", 256 * k, 256 * k + 256), R("zf"), R("og", 16 * k, 16 * k + 16), "s")
-    quant("vq", 0, P, R("tbt", 128))
-    gather(R("nc"), R("cdp"), R("pl", 0, 1))
-    ts(R("pl", 2, 3), R("pl", 0, 1), hcol, None, O.subtract)
-    memset(R("xt", 512, 640), 0.0)
-    copy(R("nl"), R("nc", 0, 8))
-    lin(R("n1", 8, 16), R("nc", 0, 8), 1.0 / 8192, NB / 8192 - 0.75)
+    quant("vq", 0, P, R("tbt", 0, 4 * P))
+    quant("uc", UB, UW, R("tbt"))
+    lin(R("ca", 2, 3), hcol, 528.0, -128.0)
+    lin(R("ca", 3, 4), hcol, -496.0, 384.0)
+    lin(R("ca", 12, 13), p7, 31.875, R("ca", 0, 1))
+    lin(R("ca", 14, 15), p3, -1.0, 0.75)
     turn(R("zt", 0, 256), R("zr", 0, 256))
-    quant("uc", 0, UR, R("tbt"))
+    turn(R("zt", 256, 512), R("zr", 256, 512))
 
     back = ring[::-1]
     for k, q in enumerate(back):
@@ -350,16 +358,14 @@ def rank_program(g, core, T, topo):
     for k in range(3):
         pick("pk", LC * k, LC * k + LC, "vq", P, R("lnd", LS[k], LS[k] + 10))
         send([piece("", k)], "arc")
-    send([piece("s", 0), piece("s", 1)], "arc")
-    send([piece("s", 2)], "arc")
+    send([piece("s", 0), piece("s", 1)], "ars")
+    send([piece("s", 2)], "ars")
 
     points("s")
     iota("c4", [[1, 4]], 0, 0)
-    iota("rst0", [[32, 4], [0, 16]], 4, 0)
+    iota("rst0", [[32, 4], [0, 32]], 4, 0)
     iota("pm0", [[4, 4], [0, 4]], 3, 0)
     iota("hv0", [[16, 2], [0, 2]], 0, 0)
-    copy(R("t1", 0, 128, st=16), R("n1", 8, 16), "s")
-    lin(R("et", 0, 516), R("idt", 0, 516), 0.0)
     et = R("et", 0, 512)
     op("p", lambda: g.affine_select(et["ap"], et["ap"], [[1, 512]], O.not_equal, 0.5, -3, -4), [et], [et])
     iota("gl0", [[2, 3]], 5, 0, 0, 3)
@@ -367,89 +373,91 @@ def rank_program(g, core, T, topo):
     iota("gl0", [[-62, 2]], 3, 0, 5, 7)
     iota("t2", [[0, 256]], 0, 0, 0, 256)
     iota("jc0", [[16, 24]], 0, 0)
-    iota("pt0", [[A, r + 1], [1, 4], [0, 4]], 0, 0, 0, 16 * r + 16)
-    if r < N - 1:
-        iota("pt0", [[A, N - 1 - r], [1, 4], [0, 4]], A * r + 128, 0, 16 * r + 16, 64)
+    iota("pt0", [[A, N], [1, 4], [0, 4]], 0, 0)
     iota("wk", [[0, 416]], NOP, 0, P * r + 16, P * r + 432)
     lin(R("bo"), R("bo0"), 1.0, R("ca", 1, 2))
     lin(R("br"), R("br0"), 1.0, pcol)
     copy(R("bl"), R("ib"), "s")
 
     def tie(j):
-        ts(R("tie", 16 * j, 16 * j + 16), R("idt"), R("nc", 2 * j, 2 * j + 1), -2.0 ** -100, O.is_lt, O.mult, R("nl", 2 * j, 2 * j + 1))
-    turn(R("zt", 256, 512), R("zr", 256, 512))
-    tie(0)
-    tie(1)
+        ts(R("tie", 16 * j, 16 * j + 16), R("idt"), R("nc", 2 * j, 2 * j + 1), 1e29, O.is_ge, O.mult, R("nl", 2 * j, 2 * j + 1))
+    gather(R("nc"), R("cdp"), R("pl", 0, 1))
+    lin(R("n1", 8, 16), R("nc", 0, 8), 1.0 / 8192, NB / 8192 - 0.75)
+    lin(R("ca", 13, 14), lcol, 0.125, R("ca", 12, 13))
+    lin(R("cn", 0, 2), R("t32", 0, 2), 1.0, R("ca", 14, 15))
+    copy(R("t1", 0, 128, st=16), R("n1", 8, 16), "s")
+    lin(R("ids", 0, IQ), R("idt", 0, IQ), 1.0 / 8192)
     tt(R("z2", 0, 32, 0, 64), R("zt", 0, 512, 0, 64, 16), R("zt", 0, 512, 64, 128, 16), O.add)
     for a in range(4):
         tt(R("sf", 0, 32, 32 * a, 32 * a + 32), R("z2", 0, 32, 0, 32), R("z2", 0, 32, 32, 64), O.add)
     ts(R("sw"), R("sf"), float(ZB), None, O.add, None, R("wr", 4, 6))
     ts(R("sc"), R("sf"), 1.0 / 8192, ZB / 8192 - 0.75, O.mult, O.add, R("pl", 2, 3))
-    tie(2)
-    tie(3)
-    copy(R("t1", 2, 128, st=16), R("sc", 0, 8))
+    copy(R("nl"), R("nc", 0, 8))
     tt(R("t1", 1, 128, st=16), R("n1", 8, 16), R("t1", 0, 128, st=16), O.subtract)
 
-    note(None, [R(n, UR, UW) for n in ("uc", "ucs")], [], "arc", count["arc"])
+    note(None, [R("uc", UR, UB)], [], "arc", count["arc"])
+    note(None, [R("ucs", UR, UB)], [], "ars", count["ars"])
     for j in range(4):
-        pick("ex", 128 * j, 128 * j + 128, "uc", UW, R("sw", 8 * j, 8 * j + 8))
-    for j, w in ((0, 1), (0, 0), (1, 1), (1, 0), (2, 1), (3, 1), (2, 0), (3, 0)):
+        pick("ex", 128 * j, 128 * j + 128, "uc", UW, R("sw", 8 * j, 8 * j + 8), "vs" if j != 1 else "v")
+        if j == 1:
+            gather(R("exs", 128, 256), R("ucs", 0, UW), R("sw", 8, 16))
+    tie(0)
+    for j, w in ((0, 1), (1, 1), (2, 1), (3, 1), (0, 0), (1, 0), (2, 0), (3, 0)):
         mm(BANKS[4 * w + j], 128, "ex", 128 * j, "xq" if w else "ex", 0 if w else 128 * j, 128 if w else 128 * j + 128)
         if w:
             copy(R("cs", 32 * j, 32 * j + 32), R(BANKS[4 + j], 0, 32))
+            if j == 1:
+                gather(R("ob", 0, 64), R("cs", 0, 64), R("bo", 0, 4), "s")
             if j == 2:
-                gather(R("ob", 0, 64), R("cs", 0, 64), R("bo", 0, 4))
+                gather(R("ob", 64, 96), R("cs", 0, 96), R("bo", 4, 6), "s")
+                for k in (1, 2):
+                    tie(k)
         else:
             copy(R("cg", 128 * j, 128 * j + 128), R(BANKS[j], 0, 128), "s")
     turn(R("obt", 0, 64), R("ob", 0, 64))
-    gather(R("ob", 64, 128), R("cs"), R("bo", 4, 8))
+    gather(R("ob", 96, 128), R("cs"), R("bo", 6, 8))
     own = R("ob", 0, 128, st=2)
     need("y", [], [R("ob")])
     for s in ("", "s"):
         dma("y", R("mg" + s, 0, P), R("vq" + s), "dmg", 2)
     lin(R("c2", 0, 4), R("c4"), 31.875)
-    lin(R("ca", 2, 3), hcol, 528.0, -128.0)
-    lin(R("ca", 3, 4), hcol, -496.0, 384.0)
-    lin(R("ca", 12, 13), p7, 31.875, R("ca", 0, 1))
-    lin(R("ca", 14, 15), p3, -1.0, 0.75)
     lin(R("ca", 4, 5), lcol, 1.0, float(DUMP))
-    lin(R("ca", 13, 14), lcol, 0.125, R("ca", 12, 13))
-    lin(R("cn", 0, 2), R("t32", 0, 2), 1.0, R("ca", 14, 15))
-    ts(R("mk4"), R("c4"), p3, None, O.is_equal)
-    tt(R("t1", 3, 128, st=16), R("sc", 0, 8), R("t1", 2, 128, st=16), O.subtract)
+    lin(R("z8", 7, 8), lcol, 1.0 / 8192, DUMP / 8192)
+    tie(3)
+    copy(R("t1", 2, 128, st=16), R("sc", 0, 8))
     turn(R("obt", 64, 128), R("ob", 64, 128))
-    ts(R("pm0"), R("pm0"), lcol, 8193.0, O.is_lt, O.mult)
-    ts(R("hv"), R("hv0"), lcol, None, O.add)
-    ttg(R("dw"), R("obt"), R("br"), own, O.subtract)
+    tt(R("dw"), own, R("tie"), O.add)
+    ttg(R("w2", 0, 128, st=2), R("obt"), R("br"), own, O.is_gt)
+    ttg(R("w2", 1, 128, st=2), R("obt"), R("br"), R("dw"), O.is_equal)
     ttg(R("bb"), R("cg"), R("bl"), own, O.is_lt)
-    lin(R("pm"), R("pm0"), 1.0, -1.0)
-    lin(R("ptv"), R("pt0"), 1.0, R("ca", 1, 2))
-    lin(R("jc"), R("jc0"), 1.0, lcol)
-    tt(R("w2"), R("dw"), R("tie"), O.is_gt)
-    quant("eq", 0, 128, R("et", 3, 515))
+    lin(R("ids", IQ), R("idt", IQ), 1.0 / 8192)
     scan(R("rks"), R("rst0"), R("w2"), O.max, O.add)
-    quant("eq", 128, 256, R("et", 2, 514))
-    rank = R("rks", 15, 64, st=16)
+    tt(R("t1", 3, 128, st=16), R("sc", 0, 8), R("t1", 2, 128, st=16), O.subtract)
+    ts(R("mk4"), R("c4"), p3, None, O.is_equal)
+    rank = R("rks", 31, 128, st=32)
     ts(R("l1"), rank, R("ca", 0, 1), None, O.add)
     tt(R("l2a", 0, 4), rank, R("c2", 0, 4), O.subtract)
-    memset(R("kd"), 0.0)
+    ts(R("gl", 0, 7), R("gl0"), R("ca", 13, 14), 0.0, O.add, O.max)
     scatter(R("t1"), R("l1"), R("bb"))
     for k in range(2):
         ts(R("l2", k, 8, st=2), R("l2a", 0, 4), 32.0, R("ca", 2 + k, 3 + k), O.mult, O.add)
     turn(R("t1t"), R("t1", 0, 128))
-    ts(R("gl", 0, 7), R("gl0"), R("ca", 13, 14), 0.0, O.add, O.max)
+    quant("eq", 0, 128, R("et", 3, 515))
     scatter(R("t2"), R("l2"), R("t1t"))
     quant("eq", 256, 384, R("et", 1, 513))
     for k in range(1, 4):
         copy(R("t2", k, 256, st=4), R("t2", 0, 256, st=4), "vvvs"[k])
     quant("eq", 384, 512, R("et", 0, 512))
     turn(R("t2t"), R("t2", 0, 256))
+    ts(R("hv"), R("hv0"), lcol, None, O.add)
+    ts(R("pm"), R("pm0"), lcol, 0.5, O.is_lt, O.subtract)
     parts = [(ch, b) for ch in range(2) for b in range(4)]
 
     def old(ch, b):
         mm(BANKS[4 * ch + b], CUT[ch][1] - CUT[ch][0], "eq", 128 * b, "vq", CUT[ch][0], CUT[ch][1], True, False)
-    for ch, b in parts[:7]:
-        old(ch, b)
+    for ch, b in parts:
+        if b != 1 and (ch, b) != (1, 3):
+            old(ch, b)
 
     ts(R("alg", 96, 112), R("t2t", 64), R("t2t", 36, 37), R("t2t", 52, 53), O.subtract, O.is_ge, R("gl", 6, 7))
     ts(R("dd", 2, 3), R("t2t", 68, 69), R("t2t", 84, 85), 0.5, O.add, O.is_lt)
@@ -468,82 +476,88 @@ def rank_program(g, core, T, topo):
     for u in range(2, 7):
         ts(step(u, u + 1, 8), R("alg", 9 * u - 7, 8 * u), one("dd", u), step(u - 1, u), O.add, O.is_ge)
         fell(one("dd", u + 1), u + 1, u, u)
-        if u == 5:
-            fell(R("d7"), 7, 5, 7)
+        if u > 3 and u < 6:
+            fell(R("d%d" % (u + 2)), u + 2, u, 7 * (u - 4))
         ts(one("cn", u + 1), one("dd", u), step(u - 1, u), one("cn", u), O.is_lt, O.add)
         if u == 2:
             tt(R("mk8", 0, 8), R("alg", 48, 56), R("alg", 56, 64), O.add)
-        else:
+        elif u < 6:
             ts(one("mk8", 9 * u), one("dd", u), step(u - 1, u), one("mk8", u), O.is_lt, O.mult)
         if u == 3:
             lin(one("mk8", 9), one("mk8", 1), step(0, 1))
             ts(one("mk8", 18), one("dd", 2), step(1, 2), one("mk8", 2), O.is_lt, O.mult)
-        if u == 6:
-            ts(R("q7"), R("d7"), step(5, 7), one("mk8", 7), O.is_lt, O.mult)
-    tt(R("z8", 0, 7), R("cn", 0, 7), R("mk8", 0, 55, st=9), O.add)
-    ts(one("z8", 7), R("q7"), step(6, 7), one("cn", 7), O.mult, O.add)
+        if u > 4:
+            ts(R("q%d" % (u + 1)), R("d%d" % (u + 1)), step(u - 1, u + 1), one("mk8", u + 1), O.is_lt, O.mult)
+    lin(R("z7"), R("q7"), step(6, 7), one("cn", 7), AF.Abs)
+    ts(one("z8", 6), R("q6"), step(5, 6), one("cn", 6), O.mult, O.add)
+    tt(R("z8", 0, 6), R("cn", 0, 6), R("mk8", 0, 46, st=9), O.add)
     ts(one("cn", 8), one("dd", 7), step(6, 7), one("cn", 7), O.is_lt, O.add)
     tt(R("ms8"), R("alg", 64, 72), R("alg", 72, 80), O.add)
     red(R("nlv"), R("z8"), O.min, True)
     tt(R("y8"), R("cn", 1, 9), R("cn", 0, 8), O.subtract)
-    ts(R("kl", 0, 1), R("nlv"), 8192.0, R("ca", 4, 5), O.mult, O.min)
-    lin(R("own"), R("pm"), R("nlv"))
-    ts(R("nls"), R("nlv"), 8192.0, R("ca", 4, 5), O.mult, O.min)
+    ts(R("kl", 0, 1), R("z7"), R("nlv"), 8192.0, O.min, O.mult)
+    ts(R("own"), R("pm"), R("z7"), R("nlv"), O.min, O.min)
+    ts(R("nls"), R("z7"), R("nlv"), 8192.0, O.min, O.mult)
     tt(R("ms9"), R("ms8"), R("y8"), O.mult)
-    ttg(R("same"), R("idt"), R("kl", 0, 1), R("own"), O.is_equal)
-    ts(R("kt"), R("nlv"), 0.22, None, O.is_lt)
+    ttg(R("same"), R("ids"), R("kl", 0, 1), R("own"), O.is_equal)
+    ts(R("kt"), R("nls"), DUMP - 2.0, None, O.is_lt)
     tt(R("ms8"), R("cn", 0, 8), R("ms9"), O.add)
     red(R("dup"), R("same"), O.max)
-    ts(R("kw"), R("nlv"), 8192.0, 1.0 - NB, O.mult, O.add)
+    ts(R("kw"), R("nls"), 1.0 - NB, None, O.add)
     red(R("slv"), R("ms8"), O.min, True)
     ts(R("kd", 0, 1), R("dup"), R("ca", 4, 5), R("nls"), O.mult, O.max)
     spread(R("kd"), lambda q: R("kla", 2 * here[q], 2 * here[q] + 2), "ark")
 
-    ts(R("yv"), R("slv"), 0.22, 8192.0, O.is_lt, O.mult)
+    lin(R("ptv"), R("pt0"), 1.0, R("ca", 1, 2))
+    lin(R("jc"), R("jc0"), 1.0, lcol)
+    pick("xa", NOP, NOP + 16, "xq", 128, R("il", 2, 3), "s")
+    pick("xa", 32 * r, 32 * r + 32, "xq", 128, R("il", 0, 2), "s")
+    ts(R("zz", 96, 97), R("slv"), 8192.0, UW - 16.0, O.mult, O.min)
     tt(R("kv"), R("kw"), R("kt"), O.mult)
-    quant("wq", 0, 128, R("wt"))
-    tt(R("zz", 96, 97), R("slv"), R("yv"), O.mult)
-    ts(R("zz", 64, 68), R("mk4"), R("kv"), None, O.mult)
+    quant("eq", 128, 256, R("et", 2, 514))
+    old(0, 1)
+    old(1, 1)
     turn(R("yr"), R("zz", 96, 128))
-    turn(R("kpt"), R("zz", 64, 96))
-    quant("xa", 32 * r, 32 * r + 128, R("xt", 0, 512))
+    ts(R("zz", 64, 68), R("mk4"), R("kv"), None, O.mult)
     gather(R("yd"), R("yr"), R("hv"))
-    tt(R("kp2"), R("kpt", 0, 32, st=2), R("kpt", 1, 32, st=2), O.add)
-    turn(R("ydt"), R("yd"))
-    quant("xa", NOP, NOP + 128, R("xt", 128, 640))
-    for a in range(4):
-        copy(R("ksl", 2 * a, 2 * a + 2, 0, 32), R("ydt", 0, 64, 32 * a, 32 * a + 32, 32), "s")
-    for b in range(1, 4):
-        copy(R("ksl", 0, 8, 32 * b, 32 * b + 32), R("ksl", 0, 8, 0, 32), "s")
+    turn(R("kpt"), R("zz", 64, 96))
 
     note(None, [R("kla")], [], "ark", count["ark"])
     for q in reversed(range(N)):
         k = q - (q > r)
         scatter(R("wk", 32 - NB), R("kd", 0, 1) if q == r else R("kla", 2 * k, 2 * k + 1), R("ptv", 16 * q, 16 * q + 16))
         if q == 3:
-            tt(R("kp3"), R("kp2", 0, 16, st=2), R("kp2", 1, 16, st=2), O.add)
-        if q == 2:
-            ts(R("kpo"), R("kp3"), -1.0, None, O.add)
+            turn(R("ydt"), R("yd"))
             for a in range(4):
-                dma("y", T.kp[:, 8 * a:8 * a + 8], R("kpo", 0, 8, 32 * a, 32 * a + 4), "dk", 4)
-    pick("kq", 0, 64, "uc", UW, R("ksl", 0, 4))
+                copy(R("ksl", 2 * a, 2 * a + 2, 0, 32), R("ydt", 0, 64, 32 * a, 32 * a + 32, 32), "s")
+            for b in range(1, 4):
+                copy(R("ksl", 0, 8, 32 * b, 32 * b + 32), R("ksl", 0, 8, 0, 32), "s")
+            tt(R("kp2"), R("kpt", 0, 32, st=2), R("kpt", 1, 32, st=2), O.add)
+        if q == 2:
+            tt(R("kp3"), R("kp2", 0, 16, st=2), R("kp2", 1, 16, st=2), O.add)
+        if q == 1:
+            quant("wq", 0, 128, R("wt"))
+    ts(R("kpo"), R("kp3"), -1.0, None, O.add)
+    for a in range(4):
+        dma("y", T.kp[:, 8 * a:8 * a + 8], R("kpo", 0, 8, 32 * a, 32 * a + 4), "dk", 4)
     turn(R("tk", 0, P), R("wk", P * r + 32, P * r + 416))
     turn(R("tk", P), R("wk", P * r + 16, P * r + 432))
+    pick("kq", 0, 64, "uc", UW, R("ksl", 0, 4))
+    tt(R("wa"), R("tk", 0, 800, st=32), R("tk", 16, 800, st=32), O.min)
     pick("kq", 64, 128, "uc", UW, R("ksl", 4, 8))
     mm(BANKS[7], 128, "wq", 0, "kq", 0, 128)
     copy(R("yt"), R(BANKS[7], 0, 128), "s")
     dma("y", T.y[:, :], R("yt"), "dy", 1)
     old(1, 3)
-    tt(R("wa"), R("tk", 0, 800, st=32), R("tk", 16, 800, st=32), O.min)
     tt(R("wc", 0, 25, 0, 64), R("wa", 0, 25, 0, 64), R("wa", 0, 25, 64, 128), O.min)
     for a in range(4):
         tt(R("zz", 32, 57, 32 * a, 32 * a + 32), R("wc", 0, 25, 0, 32), R("wc", 0, 25, 32, 64), O.min)
     gather(R("ln"), R("zz", 32, 64), R("wr", 2, 4))
     ts(R("sl0"), R("zz", 32, 64), NOP - 0.5, float(P), O.is_lt, O.mult, R("wr", 2, 4))
 
-    note(None, [R("xa" + s, 32 * q + 96 * (q > r), 32 * q + 96 * (q > r) + 32) for q in others for s in ("", "s")], [], "arx", count["arx"])
+    note(None, [R("xa" + s, 32 * q, 32 * q + 32) for q in others for s in ("", "s")], [], "arx", count["arx"])
     for a, b in CUT:
-        pick("qp", a, b, "xa", NOP + 128, R("ln", a // 16, b // 16))
+        pick("qp", a, b, "xa", NOP + 16, R("ln", a // 16, b // 16))
     for ch, b in parts:
         mm(BANKS[4 * ch + b], CUT[ch][1] - CUT[ch][0], "eq", 128 * b, "qp", CUT[ch][0], CUT[ch][1], False, True)
 
@@ -558,9 +572,9 @@ def rank_program(g, core, T, topo):
         pick("oq", a, b, "mg", P + b, R("sl", a // 16, b // 16), who)
         if who == "v":
             dma("y", T.oc[:, 4 * a:4 * b], R("oq", a, b), "do%d" % ch, 1)
-        else:
+        elif ch:
             for k in range(4):
-                dma("sy"[k % 2] if ch else "y", T.osc[4 * k:4 * k + 4, a:b], R("oqs", a, b, 32 * k, 32 * k + 4), "dp%d" % ch, 4)
+                dma("sy"[k % 2], T.osc[4 * k:4 * k + 4, :], R("oqs", 0, P, 32 * k, 32 * k + 4), "dp1", 4)
     for w in ORDER.split():
         if w[0] == "h":
             half(int(w[1]), int(w[2]), w[3])
@@ -573,5 +587,5 @@ def rank_program(g, core, T, topo):
         elif w == "s2":
             copy(R("sl"), R("sl1"))
 
-    for s in sorted(count):
-        g.wait_ge(T.sem[s], count[s])
+    for s in sorted(count, key=lambda n: n == "do1"):
+        (g.vector if s == "dp1" else g).wait_ge(T.sem[s], count[s])

from concourse.bass import DstId, RemoteDMATransfer
from concourse.mybir import dt, AluOpType, AxisListType, ActivationFunctionType

N, P, A, C, LC = 4, 384, 32, 16, 160
UR = 0
UB = 3 * LC
UW = UB + P + 32
DB = P
MID = P // 2
NB = 16
DUMP = N * P + 4 + NB
IW = DUMP + 20
NOP = 128
ZB = 3 * UR + 3 * LC + UB + MID
LS = (0, 16, 26)
CUT = ((0, 192), (192, 384))
ORDER = "s1 h00s h01v s2 h02s h03v h10v n0 h11s h12v o0v h13s o0s n1 o1v o1s"

F32, BF, I32, U16, U8, F8 = "float32", "bfloat16", "int32", "uint16", "uint8", "float8_e4m3fn_x4"
SCRATCH = {}
for _d, _names in (
    (BF, "tbt:1664 xt:512 wt:512 et:528 nt:1536"),
    (F8, "vq:384 xq:128 wq:128 eq:512 xa:144 uc:896 pk:480 ex:512 kq:128 qp:384 mg:768 oq:384"),
    (U8, "vqs:384 xqs:128 wqs:128 eqs:512 xas:144 ucs:896 pks:480 exs:512 kqs:128 qps:384 mgs:768 oqs:384"),
    (I32, "kci:64"), (U16, "bl:4 bo:8 br:4 pl:4 rl:24 hv:4 wr:6 gl:8 il:4"), (BF, "ones:16 ptv:64"),
    (F32, "kcf:576 idt:1576 ids:1576 cv:192 zz:128"),
    (I32, "cdh:36 cdi:32"), (U16, "off:8 wl:12 lst:16 lnd:48"), (BF, "mk:1536 tm:1152 m1:36 m2:36 wn:1184 wnt:352 zrep:384 zf:416 zr:512 zt:512"),
    (F32, "req:192 x0:32 xt0:32"),
    (F32, "cdp:32 zp:12 gx:32 z2:32 sf:32 sc:16 nc:16 n1:24 tie:64"), (U16, "og:32 sw:32 nl:8 kl:2"),
    (F32, "cs:128 cg:512 ob:128 obt:128 dw:64 bb:64 l2a:8 alg:144"), (BF, "w2:128 rks:128 rst0:128 t1:144 t1t:128 t2:1024 t2t:256"), (U16, "l1:4 l2:8"),
    (F32, "pr:208 kpt:32 yr:32 yd:64 ydt:64 yt:128 al:64"), (U16, "kd:2 ksl:8 kla:6"),
    (BF, "wk:1616 tk:800"), (F32, "wm:128 sl0:32 sl1:24"), (U16, "ln:32 sl:24"),
):
    for _n in _names.split():
        SCRATCH[_n.split(":")[0]] = ("sbuf", [128, int(_n.split(":")[1])], _d)
PART = {}
for _d, _names in (
    ("kcf", "pf:10 xr:14 cq:8 ca:16 t32:44 tri:32 one:44 dc0:12 dc1:12 c4:4 bo0:8 br0:4 hv0:4 c2:8 jc0:24 jc:24 mk4:4 pm0:16 pm:16 pt0:64 gl0:7"),
    ("kci", "ip:2 ib:4 it:10 ir:24"),
    ("req", "mm:44 sn:44 g1:12 g3:12"),
    ("pr", "mk8:56 ms8:8 ms9:8 cn:9 dd:8 d7:1 d6:1 q6:1 z7:1 z8:8 y8:8 nlv:1 nls:1 slv:1 kt:1 kw:1 kv:1 kp2:16 kp3:8 kpo:8 own:16 same:16 dup:1 q7:1"),
    ("wm", "wa:25 wc:25"),
):
    _c = 0
    for _n in _names.split():
        PART[_n.split(":")[0]] = (_d, _c, int(_n.split(":")[1]))
        _c += PART[_n.split(":")[0]][2]
    assert _c <= SCRATCH[_d][1][1]
BANKS = ["pb%d" % _b for _b in range(8)]
for _n in BANKS:
    SCRATCH[_n] = ("psum", [128, 512], F32)
SEMAPHORES = ["ev", "ec", "et_", "ep", "dch", "dcd", "dx", "dtb", "dw", "dmg", "dk", "dy", "do0", "do1", "dp1",
              "arx", "al0", "al1", "al2", "al3", "arc", "ars", "ark", "loc"]


def rank_program(g, core, T, topo):
    r = T.rank_of(core)
    if r is None:
        return
    O, AF, X = AluOpType, ActivationFunctionType, AxisListType.X
    eng = {"v": g.vector, "s": g.scalar, "t": g.tensor, "p": g, "y": g.sync}
    semof = {"v": "ev", "s": "ec", "t": "et_", "p": "ep"}
    count = {}
    known = {k: {} for k in eng}
    log = {}

    def R(name, c0=0, c1=None, p0=0, p1=128, st=1):
        name, base, n = PART.get(name, (name, 0, SCRATCH[name][1][1] if name in SCRATCH else 0))
        c0, c1 = base + c0, base + (n if c1 is None else c1)
        ap = T[name][p0:p1, c0:c1] if st == 1 else T[name][p0:p1, c0:c1:st]
        return {"n": name, "c0": c0, "c1": c1, "p0": p0, "p1": p1, "st": st, "ap": ap}

    def meet(a, b):
        if a["p1"] <= b["p0"] or b["p1"] <= a["p0"] or a["c1"] <= b["c0"] or b["c1"] <= a["c0"]:
            return False
        return not (a["st"] == b["st"] and a["st"] > 1 and (a["c0"] - b["c0"]) % a["st"])

    def need(q, outs, ins, skip=None):
        todo = {}
        for kind, regs in (("w", outs), ("r", ins)):
            for x in regs:
                bank = x["n"] in BANKS
                for y, k, tok in log.get(x["n"], []):
                    if (skip is not None and tok[3] == skip) or known[q].get(tok[0], 0) >= tok[1]:
                        continue
                    if bank:
                        hit = tok[0] != semof.get(q) or (q != "t" and meet(x, y) and "w" in (kind, k))
                    else:
                        hit = "w" in (kind, k) and meet(x, y)
                    if hit and (tok[0] not in todo or todo[tok[0]][1] < tok[1]):
                        todo[tok[0]] = tok
        for s in sorted(todo):
            tok = todo[s]
            if known[q].get(s, 0) >= tok[1]:
                continue
            eng[q].wait_ge(T.sem[s], tok[1])
            for a, b in list(tok[2].items()) + [(s, tok[1])]:
                known[q][a] = max(known[q].get(a, 0), b)

    def note(q, outs, ins, sem, val, tag=None):
        tok = (sem, val, dict(known[q]) if q else {}, tag)
        for k, regs in (("w", outs), ("r", ins)):
            for x in regs:
                log.setdefault(x["n"], []).append((x, k, tok))

    def op(q, call, outs, ins):
        need(q, outs, ins)
        s = semof[q]
        count[s] = count.get(s, 0) + 1
        call().then_inc(T.sem[s], 1)
        note(q, outs, ins, s, count[s])

    def u8(x):
        return x["ap"].bitcast(dt.uint8) if SCRATCH[x["n"]][2] == F8 else x["ap"]

    def dma(q, o, i, sem, total):
        outs, ins = [x for x in (o,) if isinstance(x, dict)], [x for x in (i,) if isinstance(x, dict)]
        need(q, outs, ins, skip=sem)
        eng[q].dma_start(u8(o) if outs else o, u8(i) if ins else i).then_inc(T.sem[sem], 16)
        count[sem] = count.get(sem, 0) + 16
        note(q, outs, ins, sem, 16 * total, tag=sem)

    def memset(a, c):
        op("v", lambda: g.vector.memset(a["ap"], c), [a], [])

    def copy(o, i, q="v"):
        if q == "v":
            op("v", lambda: g.vector.tensor_copy(o["ap"], i["ap"]), [o], [i])
        else:
            op("s", lambda: g.scalar.activation(o["ap"], i["ap"], AF.Copy), [o], [i])

    def tt(o, a, b, f):
        op("v", lambda: g.vector.tensor_tensor(o["ap"], a["ap"], b["ap"], f), [o], [a, b])

    def ttg(o, win, off, b, f):
        op("v", lambda: g.vector.tensor_tensor(o["ap"], win["ap"].indirect(off["ap"]), b["ap"], f), [o], [win, off, b])

    def ts(o, a, s1, s2, f1, f2=None, off=None):
        ins = [a] + [s for s in (s1, s2, off) if isinstance(s, dict)]
        v0 = a["ap"] if off is None else a["ap"].indirect(off["ap"])
        v1 = s1["ap"] if isinstance(s1, dict) else s1
        v2 = s2["ap"] if isinstance(s2, dict) else s2
        if f2 is None:
            op("v", lambda: g.vector.tensor_scalar(o["ap"], v0, v1, None, f1), [o], ins)
        else:
            op("v", lambda: g.vector.tensor_scalar(o["ap"], v0, v1, v2, f1, f2), [o], ins)

    def red(o, a, f, size=False):
        kw = {"apply_absolute_value": True} if size else {}
        op("v", lambda: g.vector.tensor_reduce(o["ap"], a["ap"], X, f, **kw), [o], [a])

    def scan(o, a, b, f1, f2):
        op("v", lambda: g.vector.tensor_tensor_scan(o["ap"], a["ap"], b["ap"], 0.0, f1, f2), [o], [a, b])

    def lin(o, a, scale=1.0, bias=0.0, f=AF.Identity):
        ins = [a] + [s for s in (scale, bias) if isinstance(s, dict)]
        kw = {"scale": scale["ap"] if isinstance(scale, dict) else scale, "bias": bias["ap"] if isinstance(bias, dict) else bias}
        op("s", lambda: g.scalar.activation(o["ap"], a["ap"], f, **kw), [o], ins)

    def turn(o, a):
        op("v", lambda: g.vector.transpose(o["ap"], a["ap"]), [o], [a])

    def gather(o, win, off, q="v"):
        if q == "v":
            op("v", lambda: g.vector.tensor_copy(o["ap"], win["ap"].indirect(off["ap"])), [o], [win, off])
        else:
            op("s", lambda: g.scalar.activation(o["ap"], win["ap"].indirect(off["ap"]), AF.Copy), [o], [win, off])

    def scatter(win, off, i):
        op("v", lambda: g.vector.tensor_copy(win["ap"].indirect(off["ap"]), i["ap"]), [win], [off, i])

    def pick(cn, o0, o1, wn, w1, off, who="vs"):
        o, w = R(cn, o0, o1), R(wn, 0, w1)
        if "v" in who:
            op("v", lambda: g.vector.tensor_copy(o["ap"].bitcast(dt.uint32), w["ap"].bitcast(dt.uint32).indirect(off["ap"])), [o], [w, off])
        if "s" in who:
            gather(R(cn + "s", o0, o1), R(wn + "s", 0, w1), off, "s")

    def quant(cn, c0, c1, tile):
        o, s = R(cn, c0, c1), R(cn + "s", c0, c1)
        op("v", lambda: g.vector.quantize_mx(o["ap"], s["ap"], tile["ap"]), [o, s], [tile])

    def mm(bank, n, a, a0, b, b0, b1, start=True, stop=True):
        o, l, ls, m, ms = R(bank, 0, n), R(a, a0, a0 + 128), R(a + "s", a0, a0 + 128), R(b, b0, b1), R(b + "s", b0, b1)
        op("t", lambda: g.tensor.matmul_mx(o["ap"], l["ap"], ls["ap"], m["ap"], ms["ap"], start, stop), [o], [l, ls, m, ms])

    def iota(name, pattern, base, cm, c0=0, c1=None):
        o = R(name, c0, c1)
        kw = {"allow_small_or_imprecise_dtypes": True} if SCRATCH[o["n"]][2] in (F32, BF) else {}
        op("p", lambda: g.iota(o["ap"], pattern, base, cm, **kw), [o], [])

    others = [q for q in range(N) if q != r]
    ring = [(r + 1 + i) % N for i in range(N - 1)]
    here = {q: (r if r < q else r - 1) for q in others}

    def send(pieces, sem):
        need("p", [], [s for _q, s, _d in pieces])
        tr = []
        for k, (q, s, d) in enumerate(pieces):
            e = topo.engines(core, T.cores[q])
            m = len(e) // len(pieces)
            rid, pid, _s = topo.addr(T.cores[q])
            tr.append(RemoteDMATransfer(dst_ids=[DstId(rid=rid, pnc=pid)], dma_engine_mask=sum(1 << n for n in e[k * m:k * m + m]),
                                        remote_sem=T.sem[sem], src=u8(s), dst=u8(d)))
            count["loc"] = count.get("loc", 0) + m
            count[sem] = count.get(sem, 0) + m
        g.remote_dma_fused(tr, local_sem=T.sem.loc)

    def spread(s, dst, sem):
        need("p", [], [s])
        e = [n for n in topo.engines(core, T.cores[others[0]]) if all(n in topo.engines(core, T.cores[q]) for q in others)]
        ids = [DstId(rid=topo.addr(T.cores[q])[0], pnc=topo.addr(T.cores[q])[1]) for q in ring]
        count["loc"] = count.get("loc", 0) + len(e)
        if sem[:2] == "al":
            for q in others:
                count["al%d" % q] = len(e)
        else:
            count[sem] = count.get(sem, 0) + len(e) * len(others)
        g.remote_dma_fused([RemoteDMATransfer(dst_ids=ids, dma_engine_mask=sum(1 << n for n in e), remote_sem=T.sem[sem],
                                              srcs=[u8(s)], dsts=[u8(dst(q)) for q in ring])], local_sem=T.sem.loc)

    def points(s):
        spread(R("xq" + s, 0, 32), lambda q: R("xa" + s, 32 * r, 32 * r + 32), "arx")

    for k in range(2):
        dma("ys"[k], R("cdh", 4 - 4 * k, 36 - 4 * k, 16 * k, 16 * k + 16), T.cd[:, :], "dch", 2)
    dma("s", R("xt", 0, 128), T.x[:, :], "dx", 1)
    for k in range(8):
        dma("y", R("cdi", 0, 32, 16 * k, 16 * k + 16), T.cd[:, :], "dcd", 8)
    dma("y", R("tbt", 0, 4 * P), T.tb[:, :], "dtb", 1)
    dma("y", R("wt"), T.w[:, :], "dw", 1)

    IQ = IW // 4
    iota("ip", [[1, 1]], 0, 1, 0, 1)
    iota("xt", [[0, 384]], 0, 0, 128, 512)
    iota("t32", [[1, 44]], 0, 0)
    iota("dc0", [[-1, 12]], -DB - 12 * 31, 0)
    iota("cv", [[32, 12], [1, 16]], -MID, 0)
    runs = [(a, b, c) for a, b, c in ((0, P * r, 0), (P * r + P, N * P, P * r)) if b > a]
    for a, b, c in runs:
        memset(R("mk", a, b), -1.0)
    memset(R("ones"), 0.0)
    p = R("ip", 0, 1)
    for k, (sh, msk) in enumerate(((0, 15), (4, 1), (0, 1), (4, 7), (0, 3), (0, 7), (0, 31))):
        ts(R("it", k, k + 1), p, sh, msk, O.logical_shift_right, O.bitwise_and)
    lcol, hcol, ecol, gcol, p3, p7, pcol = [R("pf", k, k + 1) for k in range(7)]
    for a in range(4):
        copy(R("off", 0, 8, 32 * a, 32 * a + 32, 2), R("cdh", 8 * a + 4, 8 * a + 8, 0, 32), "vvss"[a])
    need("s", [], [R("off", 0, 8, 64, 128)])

    for i in range(4):
        scatter(R("mk"), R("off", 2 * i, 2 * i + 1), R("ones"))
        if i == 0:
            copy(R("pf", 0, 7), R("it", 0, 7))
            ts(R("one"), R("t32"), 11.5, None, O.is_lt)
            lin(R("ca", 6, 7), pcol, 12.0)
            lin(R("ca", 0, 1), hcol, 16.0)
        if i == 1:
            quant("xq", 0, 128, R("xt", 0, 512))
            points("")
            iota("ir", [[1, 12], [0, 2]], 0, 0)
            iota("zp", [[32, 12]], -MID - 32 * r, 1)
            iota("zz", [[0, 128]], 0, 0)
            iota("idt", [[1, IQ]], 0, 0, 0, IQ)
            iota("idt", [[1, 2 * IQ]], IQ, 0, IQ, 3 * IQ)
        if i == 2:
            ts(R("tri"), R("t32", 0, 32), pcol, None, O.is_gt)
            memset(R("mm"), 0.0)
    memset(R("wn", 16, 208), 0.0)
    memset(R("kd"), 0.0)
    for a, b, c in runs:
        turn(R("tm", c, c + b - a), R("mk", a, b))

    wcol = R("xr", 4, 5)
    lin(R("il"), R("t32", 0, 4), 16.0, lcol)
    lin(R("xr", 9, 10), ecol, -1.0, lcol)
    lin(R("xr", 0, 1), hcol, -1.0, ecol, AF.Abs)
    lin(R("xr", 1, 2), hcol, -1.0, 6.0)
    lin(R("dc1"), R("dc0"), 1.0, R("ca", 6, 7))
    lin(wcol, R("xr", 9, 10), 0.5)
    lin(R("xr", 7, 8), R("xr", 0, 1), 1.0, R("xr", 9, 10))
    lin(R("xr", 11, 12), ecol, -1.0, p7)
    lin(R("xr", 2, 3), hcol, -1.0, 13.0)
    lin(R("cv"), R("cv"), 1.0, R("ca", 0, 1))
    lin(R("cq", 3, 4), hcol, -1.0, gcol)
    lin(R("xr", 5, 6), R("xr", 0, 1), R("xr", 2, 3), wcol)
    lin(R("xr", 3, 4), R("xr", 0, 1), R("xr", 1, 2), wcol)
    lin(R("cq", 4, 5), R("cq", 3, 4), 1.0, -2.0 * r - 1.0, AF.Sign)
    lin(R("xr", 8, 9), R("xr", 7, 8), 1.0, 16.0)
    lin(R("xr", 6, 7), R("xr", 5, 6), 1.0, 8.0)
    lin(R("cq", 5, 6), R("cq", 4, 5), LC / 2, LC / 2 - UR)
    lin(R("cq", 1, 2), R("cq", 3, 4), -P / 2, 16.0)
    lin(R("cq", 2, 3), R("cq", 3, 4), -LC / 2, R("cq", 5, 6))
    for j in range(4):
        copy(R("cdp", 8 * j, 8 * j + 8), R("cdi", j, 32, st=4), "s")
    lin(R("cq", 2, 3, 32 * r, 32 * r + 32), R("cq", 3, 4, 32 * r, 32 * r + 32), 0.0, -float(UB + MID))
    lin(R("ca", 1, 2), gcol, 4.0)
    for c in (0, 400):
        lin(R("zf", c, c + 16), R("t32", 0, 16), 0.0, R("cq", 2, 3))
    lin(R("et", 0, 516), R("tm", 0, 516), 0.0)
    tt(R("m1"), R("tm", 0, 3 * P, st=32), R("tm", 16, 3 * P, st=32), O.max)
    memset(R("tbt", 4 * P), 0.0)
    pick("xa", NOP, NOP + 16, "xq", 128, R("il", 2, 3), "v")
    tt(R("m2", 0, 36, 0, 64), R("m1", 0, 36, 0, 64), R("m1", 0, 36, 64, 128), O.max)
    for k, q in enumerate(others):
        tt(R("mm", 0, 12, 32 * q, 32 * q + 32), R("m2", 12 * k, 12 * k + 12, 0, 32), R("m2", 12 * k, 12 * k + 12, 32, 64), O.max)
    scan(R("sn"), R("mm"), R("one"), O.add, O.add)
    tt(R("g1"), R("mm", 0, 12), R("dc1"), O.mult)
    copy(R("rl"), R("ir"))
    turn(R("xt0"), R("sn", 12, 44))
    tt(R("g3"), R("g1"), R("sn", 0, 12), O.add)
    copy(R("wr"), R("xr", 3, 9))
    scan(R("x0"), R("xt0"), R("tri"), O.add, O.mult)
    base = R("x0", 31, 32)
    ts(R("pl", 0, 1), R("xr", 11, 12), 4.0, gcol, O.mult, O.add)
    pick("xa", 32 * r, 32 * r + 32, "xq", 128, R("il", 0, 2), "v")
    ts(R("wl"), R("g3"), base, -1.0, O.add, O.add)
    for a, b in (((32, 64), (64, 128)), ((0, 32), (64, 128)), ((0, 64), (96, 128)), ((0, 64), (64, 96)))[r]:
        ts(R("zp", 0, 12, a, b), R("sn", 0, 12, a, b), R("x0", 31, 32, a, b), -1.0, O.add, O.add)
    scatter(R("wn", 32), R("wl"), R("cv"))
    gather(R("zrep"), R("zp"), R("rl"), "s")
    lin(R("idt", 3 * IQ), R("idt", 0, IQ), 1.0, float(3 * IQ))
    ts(R("gx"), R("cdp"), R("cq", 1, 2), 15.0, O.add, O.max, R("wr", 4, 6))
    turn(R("wnt", 0, LC), R("wn", 32, 192))
    turn(R("wnt", LC), R("wn", 16, 208))
    ts(R("og"), R("gx"), 400.0, None, O.min)
    turn(R("zf", 16, 400), R("zrep"))
    for k in range(2):
        gather(R("zr", 256 * k, 256 * k + 256), R("zf"), R("og", 16 * k, 16 * k + 16), "s")
    tt(R("zz", 0, 11), R("wnt", 0, 352, st=32), R("wnt", 16, 352, st=32), O.add)
    ts(R("pl", 2, 3), R("pl", 0, 1), hcol, None, O.subtract)
    ts(R("lst"), R("zz", 0, 16), float(MID), None, O.add, None, R("wr", 0, 1))
    spread(R("lst", 0, 10), lambda q: R("lnd", LS[ring.index(q)], LS[ring.index(q)] + 10), "al%d" % r)

    iota("t1", [[0, 144]], 0, 0)
    iota("ib", [[128, 4]], 0, 1)
    iota("bo0", [[33, 4], [0, 2]], 0, 0)
    iota("br0", [[32, 4]], 0, 0)
    quant("vq", 0, P, R("tbt", 0, 4 * P))
    quant("uc", UB, UW, R("tbt"))
    lin(R("ca", 2, 3), hcol, 528.0, -128.0)
    lin(R("ca", 3, 4), hcol, -496.0, 384.0)
    lin(R("ca", 12, 13), p7, 31.875, R("ca", 0, 1))
    lin(R("ca", 14, 15), p3, -1.0, 0.75)
    turn(R("zt", 0, 256), R("zr", 0, 256))
    turn(R("zt", 256, 512), R("zr", 256, 512))

    back = ring[::-1]
    for k, q in enumerate(back):
        note(None, [R("lnd", LS[k], LS[k] + 10)], [], "al%d" % q, count["al%d" % q])
    for c0, c1, who in ((0, 10, "vvs"), (16, 36, "sss")):
        for i, a in enumerate(others):
            copy(R("lnd", c0, c1, 32 * a, 32 * a + 32), R("lnd", c0, c1, 32 * r, 32 * r + 32), who[i])

    def piece(s, k):
        q = back[k]
        return (q, R("pk" + s, LC * k, LC * k + LC), R("uc" + s, UR + LC * here[q], UR + LC * here[q] + LC))
    for k in range(3):
        pick("pk", LC * k, LC * k + LC, "vq", P, R("lnd", LS[k], LS[k] + 10))
        send([piece("", k)], "arc")
    send([piece("s", 0), piece("s", 1)], "ars")
    send([piece("s", 2)], "ars")

    points("s")
    iota("c4", [[1, 4]], 0, 0)
    iota("rst0", [[32, 4], [0, 32]], 4, 0)
    iota("pm0", [[4, 4], [0, 4]], 3, 0)
    iota("hv0", [[16, 2], [0, 2]], 0, 0)
    et = R("et", 0, 512)
    op("p", lambda: g.affine_select(et["ap"], et["ap"], [[1, 512]], O.not_equal, 0.5, -3, -4), [et], [et])
    iota("gl0", [[2, 3]], 5, 0, 0, 3)
    iota("gl0", [[2, 2]], 0, 0, 3, 5)
    iota("gl0", [[-62, 2]], 3, 0, 5, 7)
    iota("t2", [[0, 256]], 0, 0, 0, 256)
    iota("jc0", [[16, 24]], 0, 0)
    iota("pt0", [[A, N], [1, 4], [0, 4]], 0, 0)
    iota("wk", [[0, 416]], NOP, 0, P * r + 16, P * r + 432)
    lin(R("bo"), R("bo0"), 1.0, R("ca", 1, 2))
    lin(R("br"), R("br0"), 1.0, pcol)
    copy(R("bl"), R("ib"), "s")

    def tie(j):
        ts(R("tie", 16 * j, 16 * j + 16), R("idt"), R("nc", 2 * j, 2 * j + 1), 1e29, O.is_ge, O.mult, R("nl", 2 * j, 2 * j + 1))
    gather(R("nc"), R("cdp"), R("pl", 0, 1))
    lin(R("n1", 8, 16), R("nc", 0, 8), 1.0 / 8192, NB / 8192 - 0.75)
    lin(R("ca", 13, 14), lcol, 0.125, R("ca", 12, 13))
    lin(R("cn", 0, 2), R("t32", 0, 2), 1.0, R("ca", 14, 15))
    copy(R("t1", 0, 128, st=16), R("n1", 8, 16), "s")
    lin(R("ids", 0, IQ), R("idt", 0, IQ), 1.0 / 8192)
    tt(R("z2", 0, 32, 0, 64), R("zt", 0, 512, 0, 64, 16), R("zt", 0, 512, 64, 128, 16), O.add)
    for a in range(4):
        tt(R("sf", 0, 32, 32 * a, 32 * a + 32), R("z2", 0, 32, 0, 32), R("z2", 0, 32, 32, 64), O.add)
    ts(R("sw"), R("sf"), float(ZB), None, O.add, None, R("wr", 4, 6))
    ts(R("sc"), R("sf"), 1.0 / 8192, ZB / 8192 - 0.75, O.mult, O.add, R("pl", 2, 3))
    copy(R("nl"), R("nc", 0, 8))
    tt(R("t1", 1, 128, st=16), R("n1", 8, 16), R("t1", 0, 128, st=16), O.subtract)

    note(None, [R("uc", UR, UB)], [], "arc", count["arc"])
    note(None, [R("ucs", UR, UB)], [], "ars", count["ars"])
    for j in range(4):
        pick("ex", 128 * j, 128 * j + 128, "uc", UW, R("sw", 8 * j, 8 * j + 8), "vs" if j != 1 else "v")
        if j == 1:
            gather(R("exs", 128, 256), R("ucs", 0, UW), R("sw", 8, 16))
    tie(0)
    for j, w in ((0, 1), (1, 1), (2, 1), (3, 1), (0, 0), (1, 0), (2, 0), (3, 0)):
        mm(BANKS[4 * w + j], 128, "ex", 128 * j, "xq" if w else "ex", 0 if w else 128 * j, 128 if w else 128 * j + 128)
        if w:
            copy(R("cs", 32 * j, 32 * j + 32), R(BANKS[4 + j], 0, 32))
            if j == 1:
                gather(R("ob", 0, 64), R("cs", 0, 64), R("bo", 0, 4), "s")
            if j == 2:
                gather(R("ob", 64, 96), R("cs", 0, 96), R("bo", 4, 6), "s")
                for k in (1, 2):
                    tie(k)
        else:
            copy(R("cg", 128 * j, 128 * j + 128), R(BANKS[j], 0, 128), "s")
    turn(R("obt", 0, 64), R("ob", 0, 64))
    gather(R("ob", 96, 128), R("cs"), R("bo", 6, 8))
    own = R("ob", 0, 128, st=2)
    need("y", [], [R("ob")])
    for s in ("", "s"):
        dma("y", R("mg" + s, 0, P), R("vq" + s), "dmg", 2)
    lin(R("c2", 0, 4), R("c4"), 31.875)
    lin(R("ca", 4, 5), lcol, 1.0, float(DUMP))
    lin(R("z8", 7, 8), lcol, 1.0 / 8192, DUMP / 8192)
    tie(3)
    copy(R("t1", 2, 128, st=16), R("sc", 0, 8))
    turn(R("obt", 64, 128), R("ob", 64, 128))
    tt(R("dw"), own, R("tie"), O.add)
    ttg(R("w2", 0, 128, st=2), R("obt"), R("br"), own, O.is_gt)
    ttg(R("w2", 1, 128, st=2), R("obt"), R("br"), R("dw"), O.is_equal)
    ttg(R("bb"), R("cg"), R("bl"), own, O.is_lt)
    lin(R("ids", IQ), R("idt", IQ), 1.0 / 8192)
    scan(R("rks"), R("rst0"), R("w2"), O.max, O.add)
    tt(R("t1", 3, 128, st=16), R("sc", 0, 8), R("t1", 2, 128, st=16), O.subtract)
    ts(R("mk4"), R("c4"), p3, None, O.is_equal)
    rank = R("rks", 31, 128, st=32)
    ts(R("l1"), rank, R("ca", 0, 1), None, O.add)
    tt(R("l2a", 0, 4), rank, R("c2", 0, 4), O.subtract)
    ts(R("gl", 0, 7), R("gl0"), R("ca", 13, 14), 0.0, O.add, O.max)
    scatter(R("t1"), R("l1"), R("bb"))
    for k in range(2):
        ts(R("l2", k, 8, st=2), R("l2a", 0, 4), 32.0, R("ca", 2 + k, 3 + k), O.mult, O.add)
    turn(R("t1t"), R("t1", 0, 128))
    quant("eq", 0, 128, R("et", 3, 515))
    scatter(R("t2"), R("l2"), R("t1t"))
    quant("eq", 256, 384, R("et", 1, 513))
    for k in range(1, 4):
        copy(R("t2", k, 256, st=4), R("t2", 0, 256, st=4), "vvvs"[k])
    quant("eq", 384, 512, R("et", 0, 512))
    turn(R("t2t"), R("t2", 0, 256))
    ts(R("hv"), R("hv0"), lcol, None, O.add)
    ts(R("pm"), R("pm0"), lcol, 0.5, O.is_lt, O.subtract)
    parts = [(ch, b) for ch in range(2) for b in range(4)]

    def old(ch, b):
        mm(BANKS[4 * ch + b], CUT[ch][1] - CUT[ch][0], "eq", 128 * b, "vq", CUT[ch][0], CUT[ch][1], True, False)
    for ch, b in parts:
        if b != 1 and (ch, b) != (1, 3):
            old(ch, b)

    ts(R("alg", 96, 112), R("t2t", 64), R("t2t", 36, 37), R("t2t", 52, 53), O.subtract, O.is_ge, R("gl", 6, 7))
    ts(R("dd", 2, 3), R("t2t", 68, 69), R("t2t", 84, 85), 0.5, O.add, O.is_lt)
    ts(R("cn", 2, 3), R("cn", 1, 2), R("t2t", 36, 37), R("t2t", 52, 53), O.add, O.add)
    gather(R("alg", 0, 96), R("t2t"), R("gl", 0, 6), "s")

    def step(u, v, w=None):
        return R("alg", 88 + 8 * u + v, 88 + 8 * u + (v + 1 if w is None else w))

    def one(n, u):
        return R(n, u, u + 1)

    def fell(o, v, u, w):
        a = R("alg", 88 + v, 88 + v + 8 * (u - 1) + 1, st=8)
        op("s", lambda: g.scalar.activation(R("al", 8 * w, 8 * w + u)["ap"], a["ap"], AF.Identity, scale=-1.0, bias=1.0, accum_out=o["ap"]), [o], [a])
    for u in range(2, 7):
        ts(step(u, u + 1, 8), R("alg", 9 * u - 7, 8 * u), one("dd", u), step(u - 1, u), O.add, O.is_ge)
        fell(one("dd", u + 1), u + 1, u, u)
        if u > 3 and u < 6:
            fell(R("d%d" % (u + 2)), u + 2, u, 7 * (u - 4))
        ts(one("cn", u + 1), one("dd", u), step(u - 1, u), one("cn", u), O.is_lt, O.add)
        if u == 2:
            tt(R("mk8", 0, 8), R("alg", 48, 56), R("alg", 56, 64), O.add)
        elif u < 6:
            ts(one("mk8", 9 * u), one("dd", u), step(u - 1, u), one("mk8", u), O.is_lt, O.mult)
        if u == 3:
            lin(one("mk8", 9), one("mk8", 1), step(0, 1))
            ts(one("mk8", 18), one("dd", 2), step(1, 2), one("mk8", 2), O.is_lt, O.mult)
        if u > 4:
            ts(R("q%d" % (u + 1)), R("d%d" % (u + 1)), step(u - 1, u + 1), one("mk8", u + 1), O.is_lt, O.mult)
    lin(R("z7"), R("q7"), step(6, 7), one("cn", 7), AF.Abs)
    ts(one("z8", 6), R("q6"), step(5, 6), one("cn", 6), O.mult, O.add)
    tt(R("z8", 0, 6), R("cn", 0, 6), R("mk8", 0, 46, st=9), O.add)
    ts(one("cn", 8), one("dd", 7), step(6, 7), one("cn", 7), O.is_lt, O.add)
    tt(R("ms8"), R("alg", 64, 72), R("alg", 72, 80), O.add)
    red(R("nlv"), R("z8"), O.min, True)
    tt(R("y8"), R("cn", 1, 9), R("cn", 0, 8), O.subtract)
    ts(R("kl", 0, 1), R("z7"), R("nlv"), 8192.0, O.min, O.mult)
    ts(R("own"), R("pm"), R("z7"), R("nlv"), O.min, O.min)
    ts(R("nls"), R("z7"), R("nlv"), 8192.0, O.min, O.mult)
    tt(R("ms9"), R("ms8"), R("y8"), O.mult)
    ttg(R("same"), R("ids"), R("kl", 0, 1), R("own"), O.is_equal)
    ts(R("kt"), R("nls"), DUMP - 2.0, None, O.is_lt)
    tt(R("ms8"), R("cn", 0, 8), R("ms9"), O.add)
    red(R("dup"), R("same"), O.max)
    ts(R("kw"), R("nls"), 1.0 - NB, None, O.add)
    red(R("slv"), R("ms8"), O.min, True)
    ts(R("kd", 0, 1), R("dup"), R("ca", 4, 5), R("nls"), O.mult, O.max)
    spread(R("kd"), lambda q: R("kla", 2 * here[q], 2 * here[q] + 2), "ark")

    lin(R("ptv"), R("pt0"), 1.0, R("ca", 1, 2))
    lin(R("jc"), R("jc0"), 1.0, lcol)
    pick("xa", NOP, NOP + 16, "xq", 128, R("il", 2, 3), "s")
    pick("xa", 32 * r, 32 * r + 32, "xq", 128, R("il", 0, 2), "s")
    ts(R("zz", 96, 97), R("slv"), 8192.0, UW - 16.0, O.mult, O.min)
    tt(R("kv"), R("kw"), R("kt"), O.mult)
    quant("eq", 128, 256, R("et", 2, 514))
    old(0, 1)
    old(1, 1)
    turn(R("yr"), R("zz", 96, 128))
    ts(R("zz", 64, 68), R("mk4"), R("kv"), None, O.mult)
    gather(R("yd"), R("yr"), R("hv"))
    turn(R("kpt"), R("zz", 64, 96))

    note(None, [R("kla")], [], "ark", count["ark"])
    for q in reversed(range(N)):
        k = q - (q > r)
        scatter(R("wk", 32 - NB), R("kd", 0, 1) if q == r else R("kla", 2 * k, 2 * k + 1), R("ptv", 16 * q, 16 * q + 16))
        if q == 3:
            turn(R("ydt"), R("yd"))
            for a in range(4):
                copy(R("ksl", 2 * a, 2 * a + 2, 0, 32), R("ydt", 0, 64, 32 * a, 32 * a + 32, 32), "s")
            for b in range(1, 4):
                copy(R("ksl", 0, 8, 32 * b, 32 * b + 32), R("ksl", 0, 8, 0, 32), "s")
            tt(R("kp2"), R("kpt", 0, 32, st=2), R("kpt", 1, 32, st=2), O.add)
        if q == 2:
            tt(R("kp3"), R("kp2", 0, 16, st=2), R("kp2", 1, 16, st=2), O.add)
        if q == 1:
            quant("wq", 0, 128, R("wt"))
    ts(R("kpo"), R("kp3"), -1.0, None, O.add)
    for a in range(4):
        dma("y", T.kp[:, 8 * a:8 * a + 8], R("kpo", 0, 8, 32 * a, 32 * a + 4), "dk", 4)
    turn(R("tk", 0, P), R("wk", P * r + 32, P * r + 416))
    turn(R("tk", P), R("wk", P * r + 16, P * r + 432))
    pick("kq", 0, 64, "uc", UW, R("ksl", 0, 4))
    tt(R("wa"), R("tk", 0, 800, st=32), R("tk", 16, 800, st=32), O.min)
    pick("kq", 64, 128, "uc", UW, R("ksl", 4, 8))
    mm(BANKS[7], 128, "wq", 0, "kq", 0, 128)
    copy(R("yt"), R(BANKS[7], 0, 128), "s")
    dma("y", T.y[:, :], R("yt"), "dy", 1)
    old(1, 3)
    tt(R("wc", 0, 25, 0, 64), R("wa", 0, 25, 0, 64), R("wa", 0, 25, 64, 128), O.min)
    for a in range(4):
        tt(R("zz", 32, 57, 32 * a, 32 * a + 32), R("wc", 0, 25, 0, 32), R("wc", 0, 25, 32, 64), O.min)
    gather(R("ln"), R("zz", 32, 64), R("wr", 2, 4))
    ts(R("sl0"), R("zz", 32, 64), NOP - 0.5, float(P), O.is_lt, O.mult, R("wr", 2, 4))

    note(None, [R("xa" + s, 32 * q, 32 * q + 32) for q in others for s in ("", "s")], [], "arx", count["arx"])
    for a, b in CUT:
        pick("qp", a, b, "xa", NOP + 16, R("ln", a // 16, b // 16))
    for ch, b in parts:
        mm(BANKS[4 * ch + b], CUT[ch][1] - CUT[ch][0], "eq", 128 * b, "qp", CUT[ch][0], CUT[ch][1], False, True)

    def half(ch, b, q):
        copy(R("nt", 4 * CUT[ch][0] + b, 4 * CUT[ch][1], st=4), R(BANKS[4 * ch + b], 0, CUT[ch][1] - CUT[ch][0]), q)

    def new(ch):
        quant("mg", P + CUT[ch][0], P + CUT[ch][1], R("nt", 4 * CUT[ch][0], 4 * CUT[ch][1]))

    def store(ch, who):
        a, b = CUT[ch]
        pick("oq", a, b, "mg", P + b, R("sl", a // 16, b // 16), who)
        if who == "v":
            dma("y", T.oc[:, 4 * a:4 * b], R("oq", a, b), "do%d" % ch, 1)
        elif ch:
            for k in range(4):
                dma("sy"[k % 2], T.osc[4 * k:4 * k + 4, :], R("oqs", 0, P, 32 * k, 32 * k + 4), "dp1", 4)
    for w in ORDER.split():
        if w[0] == "h":
            half(int(w[1]), int(w[2]), w[3])
        elif w[0] == "n":
            new(int(w[1]))
        elif w[0] == "o":
            store(int(w[1]), w[2])
        elif w == "s1":
            tt(R("sl1"), R("sl0", 0, 24), R("jc"), O.add)
        elif w == "s2":
            copy(R("sl"), R("sl1"))

    for s in sorted(count, key=lambda n: n == "do1"):
        (g.vector if s == "dp1" else g).wait_ge(T.sem[s], count[s])
